import numpy as np, ml_dtypes
CORES = [9,25,41,57]
N = 4
import mx_ref
BF = ml_dtypes.bfloat16
def gcols(t, e):
    v = np.concatenate([t.reshape(8, 16, -1, 4), np.zeros((8, 16, 1, 4), BF)], axis=2)
    return np.ascontiguousarray(np.stack([v[g][:, e[g]] for g in range(8)])).reshape(128, -1)
def gpick(z, e):
    return np.concatenate([z[16 * g:16 * g + 16][:, e[g]] for g in range(8)])
def tile(rs):
    return np.stack(rs, axis=2).reshape(128, -1).astype(BF)
def pick(q, e):
    c = np.concatenate([q[0].reshape(128, -1, 4), np.zeros((128, 1, 4), np.uint8)], axis=1); s = np.concatenate([q[1], np.ones((16, 1), np.uint8)], axis=1)
    return (np.ascontiguousarray(c[:, e].reshape(128, -1)), np.ascontiguousarray(s[:, e]))
def join(*qs):
    return (np.concatenate([q[0] for q in qs], axis=1), np.concatenate([q[1] for q in qs], axis=1))
def put(q, e, v):
    c, s = q[0].reshape(128, -1, 4).copy(), q[1].copy(); c[:, e] = v[0].reshape(128, -1, 4); s[:, e] = v[1]
    return (c.reshape(128, -1), s)
def pk(c, s):
    return (np.ascontiguousarray(c), mx_ref.live(s))
def emit(q):
    return q[0], q[1]
def packed(v, rng):
    q = [mx_ref.quantize(np.ascontiguousarray(v[r])) for r in range(N)]
    return np.stack([a for a, b in q]), np.stack([mx_ref.plane(b, rng) for a, b in q])
def values_of_codes():
    e, c = np.zeros((128, 128, 4), np.float32), np.zeros((128, 2, 4), np.uint8)
    e[np.arange(128), np.arange(128), 0] = 1
    c[:127, :, 0] = np.arange(256).reshape(2, 128).T[:127]
    return mx_ref.matmul(mx_ref.quantize(e.reshape(128, 512).astype(BF)), (c.reshape(128, 8), np.full((16, 2), 127, np.uint8))).T.reshape(-1).astype(np.float64)
CODE_VALUE, SCALE_VALUE = values_of_codes(), 2.0 ** (np.arange(256) - 127.0)
def decode(q):
    return (CODE_VALUE[q[0]].reshape(16, 8, -1, 4) * SCALE_VALUE[q[1]][:, None, :, None] + 0.0).reshape(128, -1).astype(np.float32)
def f(rng, *shape):
    return mx_ref.flush((rng.standard_normal(shape, dtype=np.float32) * np.exp2(rng.integers(-2, 3, shape[:-1] + (1,)))).astype(BF))
def wide(rng, *shape, cols=0):
    v = rng.standard_normal(shape, dtype=np.float32) * np.exp2(rng.integers(-12, 13, shape)).astype(np.float32)
    if cols: v *= np.repeat(np.exp2(rng.integers(-cols, cols + 1, shape[:-2] + (1, shape[-1] // 4))) * (rng.random(shape[:-2] + (1, shape[-1] // 4)) > 0.0625), 4, axis=-1).astype(np.float32)
    return mx_ref.flush(v.astype(BF))
C, K, R = 384, 96, 2
STEP = [1, 2]
def partner(r, t):
    return r ^ STEP[t]
def basins(s):
    s = s + np.float32(0.0)
    j = np.arange(C)
    o = np.argsort(-s, axis=1, kind="stable")
    w = C - 1 - np.argsort(o, axis=1)
    up = w[:, None, :] > w[:, :, None]
    before, behind = j < j[:, None], j > j[:, None]
    l = np.max(np.where(up & before, j, -1), axis=2)
    r = np.min(np.where(up & behind, j, C), axis=2)
    a = np.where(l < 0, -1, np.min(np.where(before & (j > l[:, :, None]), w[:, None, :], C), axis=2))
    b = np.where(r == C, -1, np.min(np.where(behind & (j < r[:, :, None]), w[:, None, :], C), axis=2))
    other = (a < C) & (b < C) & (w < C - 1)
    q = np.where(other, np.take_along_axis(o, np.where(other, C - 1 - np.maximum(a, b), 0), axis=1), j)
    p = s - np.take_along_axis(s, q, axis=1)
    first = np.where(w == C - 1, 0, np.where(other, 1, 2))
    e = np.sort(np.lexsort((-p, first))[:, :K], axis=1)
    edge = np.full((8, 1), -1)
    beside = np.where(np.concatenate([edge, w[:, :-1]], axis=1) > np.concatenate([w[:, 1:], edge], axis=1), j - 1, j + 1)
    to = np.where(other, np.where(a > b, l, r), beside)
    np.put_along_axis(to, e, e, axis=1)
    for i in range(C.bit_length()): to = np.take_along_axis(to, to, axis=1)
    k = np.zeros((8, C), np.int64)
    np.put_along_axis(k, e, np.tile(np.arange(K), (8, 1)), axis=1)
    return e, np.take_along_axis(q, e, axis=1), to, np.take_along_axis(k, to, axis=1)
def big(v):
    v = v.astype(np.float32)
    v[np.abs(v) < np.float32(2.0 ** -16)] = 0
    return v.astype(BF)
def numbers_of(rng):
    return {"x": big(f(rng, N, 128, 4 * C)), "u": np.array(f(rng, N, 128, 512)), "v": np.array(f(rng, N, 128, 512))}
def weights(rng, w):
    c, p = packed(w, rng)
    return {"wc": c, "ws": p}
def some(rng, keep):
    w = np.array(f(rng, N, 128, 2048)).reshape(N, 128, 4, 8, 16, 4)
    w[:, :, :, :, [i for i in range(16) if i not in keep]] = 0
    return weights(rng, w.reshape(N, 128, 2048))
def unit(rng, keep, a):
    w = np.zeros((N, 128, 4, 128, 4), np.float32)
    i = np.array([i for i in range(128) if i % 16 in keep])
    for b in range(4): w[:, i, b, i, b] = a
    return weights(rng, w.reshape(N, 128, 2048).astype(BF))
def whole(rng, *shape):
    return rng.integers(4, 8, shape) * rng.choice([-1.0, 1.0], shape)
def plant(d, s, c, m, top, k):
    x = d["x"].astype(np.float32).reshape(N, 8, 16, C, 4)
    x[:, :, 0] = 0
    x[:, :, 0, :, 0] = c * m
    u = d["u"].reshape(N, 128, 128, 4)
    u[:, :, ::16] = 0
    for i in range(3): x[:, :, 8 + i] = ((s[..., None] >> np.arange(4 * i, 4 * i + 4)) & 1) * 2.0 ** np.arange(4) * m
    for h in range(0, 128, 16):
        u[:, h, h, 0] = (k * top).astype(np.float32).astype(BF)
        for i in range(3): u[:, h + 8 + i, h] = (k * 16.0 ** i).astype(np.float32).astype(BF)[:, None]
    return {"x": x.reshape(N, 128, 4 * C).astype(BF), "u": u.reshape(N, 128, 512), "v": d["v"]}
def setup_inputs(rng):
    return {**numbers_of(rng), **weights(rng, f(rng, N, 128, 2048))}
def setup_inputs_ties(rng):
    d = numbers_of(rng)
    e = rng.permutation(N)
    x = d["x"].reshape(N, 8, 16, C, 4)
    for r in range(N):
        k = np.zeros(C, int) if r == e[0] else rng.permutation(C) % 3
        a = x[r][:, :8, :3].copy()
        a[:, :, 2] = 0
        x[r][:, :8] = a[:, :, k]
    x[e[1]] = 0
    u = d["u"].reshape(N, 8, 16, 128, 4)
    u[:, :, 8:, ::16] = 0
    return {"x": x.reshape(N, 128, 4 * C), "u": u.reshape(N, 128, 512), "v": d["v"], **some(rng, range(8, 16))}
def setup_inputs_near(rng):
    d = numbers_of(rng)
    m = 2.0 ** -29
    x = np.zeros((N, 8, 16, C, 4), np.float32)
    x[:, :, 1:8] = whole(rng, N, 8, 7, C, 4) * 4 * m
    x[:, :, 11:] = whole(rng, N, 8, 5, C, 4) * m
    d["x"] = x
    j = np.arange(C)
    fall = C // 2 - 1 - j // 2
    fall = fall + 2 * (fall == C // 2 - K - 1) - 2 * (fall == C // 2 - K + 1)
    c, s = np.zeros((N, 8, C)), np.zeros((N, 8, C), np.int64)
    for r in range(N):
        g = rng.permutation(8)
        for i in range(8):
            c[r, i] = np.where(j % 2 == 1, 1.0, -1.0 * (g[i] % 2))
            s[r, i] = np.where(j % 2 == 1, fall if g[i] == 3 else j // 2, 0)
            if g[i] >= 4:
                s[r, i] = rng.integers(0, 256, C)
                c[r, i, 2 * rng.permutation(C // 2)[:2] + 1] = 2.0 ** 30
    k = np.where(rng.permutation(N) < N // 2, 2.0 ** -30, 1.0)
    return {**plant(d, s, c, m, 2.0 ** 23, k), **unit(rng, range(1, 8), 32)}
def setup_inputs_slopes(rng):
    d = numbers_of(rng)
    j = np.arange(C)
    e = np.stack([j, C - 1 - j, np.minimum(j, C - 1 - j), np.abs(j - C // 2), 0 * j, j // 2, j // 8, np.where(j < 2 * K, j % 2 * (C + j), C - 1 - j)])
    s = np.stack([e[rng.permutation(8)] for r in range(N)])
    c = np.where(rng.permutation(N) < N // 2, -1.0, 0.0)[:, None, None] * np.ones((N, 8, C))
    return {**plant(d, s, c, 1.0, 4096.0, np.ones(N)), **some(rng, range(1, 8))}
def setup_inputs_huge(rng):
    d = numbers_of(rng)
    x = 2.0 ** 30 * (0.5 + 0.3 * rng.random((N, 128, C, 4)))
    c = np.tile(np.arange(C) % 2 * 2.0 - 1.0, (N, 1))
    c[rng.permutation(N) < N // 2] = 1
    x *= c[:, None, :, None]
    g = np.stack([rng.permutation(8) % 2 * 2.0 - 1.0 for r in range(N)])
    u = d["u"].reshape(N, 128, 128, 4)
    u[:, :, ::16] = (2.0 ** 30 * (1 - 0.25 * rng.random((N, 128, 8, 4))) * g[:, None, :, None]).astype(np.float32).astype(BF)
    return {"x": x.astype(np.float32).reshape(N, 128, 4 * C).astype(BF), "u": u.reshape(N, 128, 512), "v": d["v"], **unit(rng, range(16), 1)}
def setup_inputs_spread(rng):
    d = setup_inputs(rng)
    d["x"] = big(wide(rng, N, 128, 4 * C, cols=6))
    return d
def check_inputs(d):
    b = []
    for k in ("x", "u", "v"):
        a = np.abs(d[k].astype(np.float32))
        if not (np.isfinite(a).all() and ((a == 0) | (a >= 2.0 ** -30) & (a <= 2.0 ** 30)).all()): b.append("a value of " + k)
    return b
def reference(x, u, v, wc, ws):
    qu = [mx_ref.quantize(u[r]) for r in range(N)]
    lay = [pk(wc[r], ws[r]) for r in range(N)]
    now = [x[r] for r in range(N)]
    ends = [None] * N
    for t in range(R):
        held, place, sent = [], [], []
        for r in range(N):
            q = mx_ref.quantize(now[r])
            held.append(decode(q))
            e, low, ends[r], h = basins(mx_ref.matmul(qu[r], q)[::16])
            place.append(h)
            own = held[r].astype(BF)
            blend = (gcols(own, e).astype(np.float32) + gcols(own, low).astype(np.float32)) * np.float32(0.5)
            sent.append(mx_ref.quantize(blend.astype(BF)))
        for r in range(N):
            came = sent[partner(r, t)]
            made = [np.maximum(mx_ref.matmul(pick(lay[r], np.arange(128 * b, 128 * b + 128)), came), np.float32(0.0)) * np.float32(0.03125) for b in range(4)]
            now[r] = tile([held[r][:, b::4] + gpick(made[b], place[r]) for b in range(4)])
    y, ol = np.zeros((N, 128, C), np.float32), np.zeros((N, 8, C), np.float32)
    oc, osc = np.zeros((N, 128, 4 * C), np.uint8), np.zeros((N, 16, C), np.uint8)
    for r in range(N):
        q = mx_ref.quantize(now[r])
        y[r] = mx_ref.matmul(mx_ref.quantize(v[r]), q)
        ol[r] = ends[r]
        oc[r], osc[r] = emit(q)
    return {"y": y, "ol": ol, "oc": oc, "osc": osc}

@@ -1,0 +1,565 @@
+import math
+from concourse.mybir import dt, AluOpType as A, ActivationFunctionType as AF, AxisListType
+
+C, K, R = 384, 96, 2
+NS = C // 2
+M = NS // 16
+BIG = 1.0e29
+KS = 2.0 ** -18
+INIT = (500 * 512 + C + 1) * KS
+SCH = 6
+TW = NS + K
+TS = NS + C
+TURNS, NOISE = 500, 60.0
+CASES = ((50.0, 3500.0), (120.0, 5000.0))
+ORDER = []
+
+X4, U8, F32, BF, I32, U16 = "float8_e4m3fn_x4", "uint8", "float32", "bfloat16", "int32", "uint16"
+SCRATCH = {}
+for _d, _l in [
+    (X4, [("qx0", C), ("qx1", C), ("qx2", C), ("qu", 128), ("qur", 128), ("qv", 128), ("qe", 512), ("qw", 512), ("qf0", 128), ("qf1", 128),
+          ("ql0", K + 128), ("ql1", K + 128)]),
+    (U8, [("sx0", C), ("sx1", C), ("sx2", C), ("su", 128), ("sur", 128), ("sv", 128), ("se", 512), ("sw", 512), ("sf0", 128), ("sf1", 128),
+          ("sl0", K + 128), ("sl1", K + 128)]),
+    (I32, [("ci", 64), ("wi", 48)]),
+    (U16, [("co", 64), ("of", 160)]),
+    (BF, [("x0", 4 * C), ("x1", 4 * C), ("x2", 4 * C), ("ut", 512), ("vt", 512), ("zt", 512), ("ez", 516), ("ft", 512), ("keepb", C), ("kptab", C),
+          ("irow", NS), ("sg", M * NS), ("fl", (M - SCH) * NS), ("fc", (M - SCH) * NS), ("s2", SCH * NS), ("j2", SCH * NS), ("j3", 5 * NS),
+          ("eb", NS), ("ec", NS), ("kp", NS), ("cum", 24 + NS), ("tf", 3 * NS), ("lp", 6 * 208), ("lb", NS), ("lc", NS), ("na", NS), ("nc", C),
+          ("cpv", NS), ("ncs", 16 + NS), ("r0", NS), ("r1", NS), ("r2", NS + 8), ("r3", NS), ("r4", NS), ("r5", TW), ("hb", C), ("hc", C)]),
+    (F32, [("cf", 192), ("j16", C), ("oh", C), ("tri", NS), ("keep", C), ("uraw", 2 * C), ("utab", 2 * C), ("iot", C), ("c2t", NS), ("al", NS),
+           ("ar", NS), ("a0", NS), ("zm", K), ("z0", K), ("idn", 128), ("vv", NS), ("pp", NS), ("mk", 4 * NS), ("wsc", 4 * NS), ("ssb", C + 8),
+           ("w", 768), ("thp", 16), ("acc", 64), ("uu", NS), ("um", NS), ("lr", M * 208), ("lm", NS), ("rm", NS), ("ex", NS), ("sm", NS),
+           ("sc", NS), ("ngp", NS), ("eq", NS), ("dd", 112), ("npc", K), ("cx", 112), ("zk", K), ("zs", K), ("tt", 4 * TS), ("tq", 4 * TW),
+           ("gq", 4 * K), ("ht", 4 * K), ("hg", 2 * C), ("et", TW), ("er", K), ("olr", C), ("ysb", C)]),
+]:
+    for _n, _w in _l:
+        SCRATCH[_n] = ("sbuf", [128, _w], _d)
+for _b in range(8):
+    SCRATCH["ps%d" % _b] = ("psum", [128, 512], F32)
+
+SEMAPHORES = ["cv", "cs", "ct", "cg", "du", "dx0", "dx1", "dw", "dv", "out", "ar0", "ar1", "sent"]
+COUNTER = {"v": "cv", "s": "cs", "t": "ct", "g": "cg"}
+
+
+def rank_program(g, core, T, topo):
+    rank = T.rank_of(core)
+    if rank is None:
+        return
+    Q = {"v": g.vector, "s": g.scalar, "t": g.tensor, "g": g, "y": g.sync}
+    ops = []
+
+    def V(n, lo, hi, step=1):
+        return (T[n][:, lo:hi:step], n, lo, hi, step)
+
+    def RV(n, lo, hi):
+        return (T[n][:, hi - 1:(lo - 1 if lo else None):-1], n, lo, hi, 1)
+
+    def col(n, j):
+        return V(n, j, j + 1)
+
+    def IX(win, off):
+        return (win[0].indirect(off[0]), win[1], win[2], win[3], 1, off)
+
+    def size(a):
+        return 16 * size(a[5]) if len(a) > 5 else len(range(a[2], a[3], a[4]))
+
+    def cost(o, a, rate):
+        if len(a) > 5:
+            return 50 + 1.6 * size(a)
+        if len(o) > 5:
+            return 50 + 4.0 * size(o)
+        return max(64, size(a) * rate)
+
+    def half(*xs):
+        return 0.5 if all(SCRATCH[x[1]][2] in (BF, U16) for x in xs) else 1.0
+
+    def op(q, fn, wr, rd, ns, dma=None, lat=0.0):
+        rs = []
+        for a in rd:
+            if isinstance(a, tuple):
+                rs.append(a[1:5])
+                if len(a) > 5:
+                    rs.append(a[5][1:5])
+        ws = [a[1:5] for a in wr]
+        rs += [a[5][1:5] for a in wr if len(a) > 5]
+        ops.append((q, fn, ws, rs, dma, ns, lat))
+
+    def ap(a):
+        return a[0] if isinstance(a, tuple) else a
+
+    def tt(o, a, b, f):
+        op("v", lambda: g.vector.tensor_tensor(o[0], a[0], b[0], f), [o], [a, b], cost(o, a, 1 if "ps" in (a[1][:2], b[1][:2]) else 2))
+
+    def ts(o, a, s1, f0, s2=None, f1=None):
+        if s2 is None:
+            op("v", lambda: g.vector.tensor_scalar(o[0], a[0], ap(s1), None, f0), [o], [a, s1], cost(o, a, half(o, a)))
+        else:
+            op("v", lambda: g.vector.tensor_scalar(o[0], a[0], ap(s1), ap(s2), f0, f1), [o], [a, s1, s2], cost(o, a, half(o, a)))
+
+    def cp(o, a):
+        op("v", lambda: g.vector.tensor_copy(o[0], a[0]), [o], [a], cost(o, a, half(o, a)))
+
+    def scan(o, a, b, init, f0, f1):
+        op("v", lambda: g.vector.tensor_tensor_scan(o[0], a[0], b[0], ap(init), f0, f1), [o], [a, b, init], cost(o, a, half(o, a, b)))
+
+    def red(o, a):
+        op("v", lambda: g.vector.tensor_reduce(o[0], a[0], AxisListType.X, A.add), [o], [a], cost(o, a, 1))
+
+    def ms(o, c):
+        op("v", lambda: g.vector.memset(o[0], c), [o], [], cost(o, o, half(o)))
+
+    def act(o, a, f, bias=None, scale=None, acc=None):
+        kw = {}
+        if bias is not None:
+            kw["bias"] = ap(bias)
+        if scale is not None:
+            kw["scale"] = scale
+        if acc is not None:
+            kw["accum_out"] = acc[0]
+        op("s", lambda: g.scalar.activation(o[0], a[0], f, **kw), [o] + ([acc] if acc else []), [a, bias], cost(o, a, 1) + (20 if acc else 0))
+
+    def lin(o, a, scale, bias):
+        act(o, a, AF.Identity, bias=bias, scale=scale)
+
+    def quant(q, s, a):
+        op("v", lambda: g.vector.quantize_mx(q[0], s[0], a[0]), [q, s], [a], 12 + 0.25 * size(a))
+
+    def mm(o, lq, ls, rq, rs):
+        op("t", lambda: g.tensor.matmul_mx(o[0], lq[0], ls[0], rq[0], rs[0], True, True), [o], [lq, ls, rq, rs], size(rq) + 16)
+
+    def iota(o, pat, base, cm=0):
+        if SCRATCH[o[1]][2] == I32:
+            op("g", lambda: g.iota(o[0], pat, base, cm), [o], [], 130 + 2 * size(o))
+        else:
+            op("g", lambda: g.iota(o[0], pat, base, cm, allow_small_or_imprecise_dtypes=True), [o], [], 130 + 2 * size(o))
+
+    def fill(o, c):
+        iota(o, [[0, size(o)]], c)
+
+    def dma(q, sem, out, in_, wr, rd, lat=2000.0):
+        op(q, lambda: Q[q].dma_start(out, in_), wr, rd, 60, dma=(sem, 16), lat=lat)
+
+    def W(j, n=M):
+        return V("w", 16 * j, 16 * j + n)
+
+    def ends(n, lo, k=M):
+        return V(n, lo + 15, lo + 16 * k, 16)
+
+    def PS(b, lo, hi, step=1):
+        return V("ps%d" % b, lo, hi, step)
+
+    def IO(lo, hi, step=1):
+        return V("iot", lo, hi, step)
+
+    u8 = dt.uint8
+    dma("y", "du", T.ut[:], T.u[:], [V("ut", 0, 512)], [])
+    dma("s", "dx1", T.x0[:, 2 * C:], T.x[:, 2 * C:], [V("x0", 2 * C, 4 * C)], [], 2500)
+    dma("y", "dx0", T.x0[:, :2 * C], T.x[:, :2 * C], [V("x0", 0, 2 * C)], [], 2500)
+    dma("y", "dw", T.qw[:].bitcast(u8), T.wc[:], [V("qw", 0, 512)], [V("x0", 0, 4 * C)])
+    dma("y", "dw", T.sw[:], T.ws[:], [V("sw", 0, 512)], [V("x0", 0, 4 * C)])
+    dma("y", "dv", T.vt[:], T.v[:], [V("vt", 0, 512)], [V("x0", 0, 4 * C)])
+
+    PM, CW, PK0, JW, J192 = col("cf", 0), V("cf", 4, 16), V("cf", 16, 28), V("cf", 28, 52), V("cf", 52, 76)
+    KH, AT, BASE, KT, KD, JT, CN = V("cf", 76, 82), V("cf", 82, 88), V("cf", 88, 100), V("cf", 100, 106), V("cf", 106, 112), V("cf", 112, 136), V("cf", 136, 148)
+    CK = V("cf", 156, 168)
+    O_U, O_LR, O_M, O_LP = V("co", 0, 8), V("co", 8, 20), V("co", 20, 32), V("co", 32, 44)
+    iota(col("ci", 0), [[1, 1]], 0, 1)
+    iota(V("ci", 8, 16), [[16, 8]], 0)
+    iota(V("j16", 0, C), [[0, 2 * M], [1, 16]], 0)
+    iota(V("idn", 0, 128), [[-1, 128]], 0, 1)
+    iota(IO(0, C), [[1, C]], 0)
+    iota(V("uraw", 0, 2 * C), [[-512, C], [1, 2]], C * 512)
+    ms(V("ez", 0, 516), 0.0)
+    ts(col("ci", 1), col("ci", 0), 15, A.bitwise_and)
+    cp(O_U, V("ci", 8, 16))
+    cp(PM, col("ci", 1))
+    ts(V("oh", 0, NS), V("j16", 0, NS), PM, A.is_equal)
+    ts(V("oh", NS, C), V("j16", NS, C), PM, A.is_equal)
+    act(V("keep", 0, C), V("j16", 0, C), AF.Sign)
+    act(V("keepb", 0, C), V("j16", 0, C), AF.Sign)
+    ts(V("ez", 3, 515, 4), V("idn", 0, 128), 0.0, A.is_equal)
+    act(col("mk", 0), col("oh", 0), AF.Copy, scale=-BIG)
+    act(col("mk", 4 * NS - 1), col("oh", 15), AF.Copy, scale=-BIG)
+    quant(V("qu", 0, 128), V("su", 0, 128), V("ut", 0, 512))
+    op("v", lambda: g.vector.tensor_copy(T.qur[:].bitcast(dt.uint32), T.qu[:].bitcast(dt.uint32).indirect(O_U[0])), [V("qur", 0, 128)], [V("qu", 0, 128), O_U], 250)
+    act(V("sur", 0, 128), IX(V("su", 0, 128), O_U), AF.Copy)
+    for b in range(4):
+        quant(V("qe", 128 * b, 128 * b + 128), V("se", 128 * b, 128 * b + 128), V("ez", 3 - b, 515 - b))
+    act(V("utab", 0, 2 * C), V("uraw", 0, 2 * C), AF.Copy, scale=KS)
+    lin(CW, IO(0, NS, 16), 1.0, PM)
+    lin(PK0, CW, 2.0, 1.0)
+    act(V("cf", 28, 40), CW, AF.Copy, scale=2.0)
+    lin(V("cf", 40, 52), CW, 2.0, 1.0)
+    lin(J192, JW, 1.0, float(NS))
+    lin(JT, JW, 2.0, -float(K))
+    lin(KH, V("cf", 4, 10), 1.0, 0.5)
+    lin(KT, V("cf", 4, 10), 2.0, -float(K))
+    lin(CN, CW, -1.0 / 256, -1.0 / 256)
+    lin(CK, CW, 1.0, -NS - 1.0)
+    act(V("c2t", 0, NS), IO(1, C, 2), AF.Copy, scale=KS)
+    ts(O_LR, IO(0, M), 224.0, A.mult, PM, A.add)
+    cp(O_M, IO(0, M))
+    ts(V("co", 32, 38), IO(0, 6), 224.0, A.mult, PM, A.add)
+    iota(V("cf", 148, 154), [[-208, 6]], 208 * 5 + NS)
+    ts(V("co", 38, 44), V("cf", 148, 154), PM, A.add)
+    iota(V("a0", 0, NS), [[1, M], [0, 16]], 52)
+    tt(V("a0", 0, NS), V("a0", 0, NS), V("oh", 0, NS), A.mult)
+    lin(V("al", 0, NS), V("a0", 0, NS), -1.0, 64.0)
+    lin(V("ar", 0, NS), V("a0", 0, NS), -1.0, 65.0)
+    lin(V("lr", 0, M * 208, 208), IO(0, M), 0.0, INIT)
+    lin(V("lr", 207, M * 208, 208), IO(0, M), 0.0, INIT - 1.0)
+    lin(col("ssb", C), IO(0, 1), 0.0, BIG)
+    lin(col("ssb", C + 1), IO(0, 1), 0.0, -BIG)
+    fill(col("dd", 0), 0)
+    lin(col("cx", 0), IO(0, 1), 0.0, 0.5)
+    ts(V("tri", 0, NS), V("j16", 0, NS), PM, A.is_lt)
+    fill(V("kptab", 0, K), 1)
+    fill(V("kptab", K, C), 0)
+    fill(col("cum", 16 + NS), -1)
+    fill(col("cum", 17 + NS), 0)
+    fill(col("r2", NS), 0)
+    iota(V("z0", 0, K), [[2, K // 2], [2, 2]], 2 * NS)
+    tt(V("zm", 0, K), V("z0", 0, K), V("oh", 0, K), A.mult)
+    cp(V("ci", 16, 22), V("cf", 4, 10))
+    ts(V("ci", 24, 30), V("ci", 16, 22), 126, A.bitwise_and)
+    cp(KD, V("ci", 24, 30))
+    fill(V("cf", 82, 85), 0)
+    iota(V("cf", 85, 88), [[16, 3]], 160)
+    iota(V("cf", 88, 88 + SCH), [[16, SCH]], 0)
+    fill(V("cf", 88 + SCH, 100), 0)
+    fill(V("acc", 16, 32), 0)
+    fill(col("cum", 15), 0)
+    fill(V("ft", 4 * K, 512), 0)
+    fill(V("zt", 0, 512), 0)
+    for b in range(4):
+        fill(V("tq", TW * b + NS, TW * b + TW), 0)
+    lin(V("irow", 0, NS), IO(0, NS), -1.0 / 256, 255.0 / 256)
+    fill(V("lp", 0, 6 * 208, 208), 1)
+    fill(V("lp", 16, 6 * 208, 224), 1)
+    fill(col("ncs", 15), 1)
+    fill(col("ncs", 15 + NS), 1)
+    iota(V("et", NS, TW), [[1, K]], 0)
+    iota(V("r5", NS, TW), [[1, K]], 1)
+    for t in range(R):
+        quant(V("ql%d" % t, K, K + 128), V("sl%d" % t, K, K + 128), V("zt", 0, 512))
+    quant(V("qv", 0, 128), V("sv", 0, 128), V("vt", 0, 512))
+
+    oh = V("oh", 0, NS)
+    O_K, O_PK, O_QV, O_QT, O_RK, O_L = [V("of", 12 * j, 12 * j + M) for j in range(6)]
+    O_F, O_CE, O_CO, O_CS, O_H, O_KC = V("of", 72, 78), V("of", 80, 92), V("of", 92, 104), V("of", 80, 104), V("of", 104, 128), V("of", 128, 140)
+
+    def TB(b, lo=0, hi=C, step=1):
+        return V("tt", TS * b + NS + lo, TS * b + NS + hi, step)
+
+    for t in range(R):
+        QX, SX = V("qx%d" % t, 0, C), V("sx%d" % t, 0, C)
+        quant(QX, SX, V("x%d" % t, 0, 4 * C))
+        for b in (0, 1):
+            mm(PS(b, 0, C), V("qur", 0, 128), V("sur", 0, 128), QX, SX)
+        for b in range(4):
+            mm(PS(4 + b, 0, C), V("qe", 128 * b, 128 * b + 128), V("se", 128 * b, 128 * b + 128), QX, SX)
+
+        OP_, E_, O_, EN_ = ends("wsc", 0), ends("wsc", NS), ends("wsc", 2 * NS), ends("wsc", 3 * NS)
+        THV, THP, BB, AW, PK = W(0), W(1), W(2), W(3), W(4)
+        act(V("ssb", 0, C), PS(1, 0, C), AF.Copy)
+        tt(V("mk", 2 * NS, 3 * NS), PS(0, 1, C, 2), oh, A.mult)
+        tt(V("mk", 3 * NS, 4 * NS - 1), PS(0, 2, C, 2), V("oh", 0, NS - 1), A.mult)
+        scan(V("wsc", 2 * NS, 4 * NS), V("keep", 0, C), V("mk", 2 * NS, 4 * NS), 0.0, A.mult, A.add)
+        tt(V("vv", 0, NS - 1), V("ssb", 1, C - 2, 2), PS(0, 2, C, 2), A.min)
+        tt(THV, O_, EN_, A.min)
+        for b in range(4):
+            act(TB(b), PS(4 + b, 0, C), AF.Copy)
+        for m in range(M):
+            act(V("sg", NS * m, NS * m + NS - 1), V("vv", 0, NS - 1), AF.Sign, bias=col("w", m), scale=-1.0, acc=col("acc", 32 + m))
+        tt(V("pp", 0, NS), V("ssb", 1, C, 2), PS(0, 0, C, 2), A.max)
+        tt(V("mk", NS, 2 * NS), PS(0, 0, C, 2), oh, A.mult)
+        tt(V("mk", 1, NS), PS(0, 1, C - 2, 2), V("oh", 1, NS), A.mult)
+        scan(V("wsc", 0, 2 * NS), V("keep", 0, C), V("mk", 0, 2 * NS), 0.0, A.mult, A.add)
+        tt(W(5), O_, EN_, A.is_ge)
+        tt(THP, E_, O_, A.max)
+        tt(AW, E_, O_, A.is_ge)
+        ts(BB, W(5), float(C), A.add, 0.5, A.mult)
+        tt(PK, PK0, AW, A.subtract)
+        cp(O_PK, PK)
+        tt(W(6), OP_, O_, A.is_ge)
+        tt(W(8), EN_, E_, A.is_gt)
+        tt(W(7), W(6), AW, A.is_gt)
+        tt(W(28), W(8), AW, A.mult)
+        CS0 = W(9, 24)
+        tt(V("w", 16 * 9, 16 * 9 + 12), CW, W(7), A.subtract)
+        tt(V("w", 16 * 9 + 12, 16 * 9 + 24), CW, W(28), A.add)
+        tt(V("dd", 1, K + 1), V("ssb", 0, K), PS(0, 1, K + 1), A.is_ge)
+        tt(V("npc", 0, K), V("dd", 1, K + 1), V("dd", 0, K), A.is_le)
+        scan(V("cx", 1, K + 1), V("npc", 0, K), V("npc", 0, K), 0.5, A.add, A.max)
+        tt(V("zk", 0, K), V("npc", 0, K), V("zm", 0, K), A.mult)
+        scan(V("zs", 0, K), V("keep", 0, K), V("zk", 0, K), 0.0, A.mult, A.add)
+        tt(W(29, 6), ends("zs", 0, 6), KD, A.add)
+        for m in range(M):
+            act(V("sg", NS * m, NS * m + NS), V("pp", 0, NS), AF.Sign, bias=col("w", 16 + m), scale=-1.0)
+        for b in range(4):
+            act(V("tt", TS * b, TS * b + NS), IX(TB(b), O_PK), AF.Copy, scale=0.5)
+        tt(W(11), V("acc", 32, 32 + M), BB, A.add)
+        ts(O_K, W(11), 2.0, A.mult)
+        tt(V("uu", 0, NS), IX(V("utab", 0, 2 * C), O_K), V("c2t", 0, NS), A.add)
+        lin(V("um", 0, NS), V("uu", 0, NS), 1.0, -1.0)
+        for m in range(M):
+            n = 16 * m + 15
+            scan(V("lr", 208 * m + 1, 208 * m + 1 + n), V("sg", NS * m, NS * m + n), V("uu", 0, n), INIT, A.min, A.max)
+            scan(RV("lr", 208 * m + 16 + 16 * m, 208 * m + 207), RV("sg", NS * m + 16 * m + 1, NS * m + NS), RV("um", 16 * m, NS - 1), INIT - 1.0, A.min, A.max)
+        tt(V("lm", 0, NS), IX(V("lr", 0, M * 208), O_LR), V("al", 0, NS), A.add)
+        tt(V("rm", 0, NS), IX(V("lr", 16, M * 208), O_LR), V("ar", 0, NS), A.add)
+        scan(V("ex", 0, NS), V("lm", 0, NS), V("rm", 0, NS), 100.0, A.min, A.min)
+        QI, NPW, QV = V("wi", 16, 16 + M), W(12), W(13)
+        ts(V("wi", 0, M), ends("ex", 0), 1.0 / KS, A.mult)
+        ts(QI, V("wi", 0, M), 511, A.bitwise_and)
+        tt(NPW, QI, PK, A.is_equal)
+        ts(W(14), NPW, float(C), A.mult)
+        tt(QV, W(14), QI, A.max)
+        cp(O_QV, QV)
+        SS = V("ssb", 0, C + 2)
+        tt(V("sm", 0, NS), IX(SS, O_QV), oh, A.mult)
+        tt(V("ngp", 0, NS), IX(SS, O_QV), V("pp", 0, NS), A.subtract)
+        scan(V("sc", 0, NS), V("keep", 0, NS), V("sm", 0, NS), 0.0, A.mult, A.add)
+        TH = V("thp", 0, M)
+        tt(TH, ends("sc", 0), THP, A.subtract)
+        tt(W(16), QI, PK, A.subtract)
+        ts(W(15), QI, float(C), A.is_lt)
+        tt(W(30), W(16), W(15), A.mult)
+        tt(W(17), W(30), PK, A.add)
+        cp(O_QT, W(17))
+        NPA, XA, NN = col("acc", 48), col("acc", 49), col("acc", 50)
+        act(V("j3", 0, NS), V("ngp", 0, NS), AF.Sign, bias=-BIG / 4, acc=NPA)
+        act(V("j3", NS, NS + K), V("cx", 0, K), AF.Sign, bias=NPA, scale=-2.0, acc=XA)
+        act(NN, NPA, AF.Relu, scale=0.5)
+        for m in range(SCH):
+            s2 = NS * m
+            act(V("s2", s2, s2 + NS), V("ngp", 0, NS), AF.Sign, bias=col("thp", m), scale=-1.0)
+            act(V("j2", s2 + 16 * m, s2 + NS), V("s2", s2 + 16 * m, s2 + NS), AF.Relu, acc=col("acc", m))
+            if m:
+                act(V("j2", s2, s2 + 16 * m), V("s2", s2, s2 + 16 * m), AF.Relu, scale=-1.0, acc=col("acc", 16 + m))
+        for m in range(SCH, M):
+            f0 = NS * (m - SCH)
+            ts(V("fl", f0, f0 + 16 * m), V("ngp", 0, 16 * m), col("thp", m), A.is_le)
+            ts(V("fl", f0 + 16 * m, f0 + NS), V("ngp", 16 * m, NS), col("thp", m), A.is_lt)
+            f = V("fl", f0, f0 + NS)
+            scan(V("fc", f0, f0 + NS), f, f, 0.0, A.add, A.max)
+        tt(V("eq", 0, NS), IX(TH, O_M), V("ngp", 0, NS), A.is_equal)
+        tt(V("eb", 0, NS), V("eq", 0, NS), V("tri", 0, NS), A.mult)
+        scan(V("ec", 0, NS), V("keepb", 0, NS), V("eb", 0, NS), 0.0, A.mult, A.add)
+        ts(W(18), NPW, float(NS), A.mult)
+        tt(W(31), W(18), BASE, A.add)
+        tt(W(32), W(31), ends("ec", 0), A.add)
+        tt(V("w", 16 * 33 + SCH, 16 * 33 + M), V("w", 16 * 32 + SCH, 16 * 32 + M), V("fc", NS - 1, (M - SCH) * NS, NS), A.add)
+        for b in range(4):
+            act(V("tq", TW * b, TW * b + NS), IX(TB(b), O_QT), AF.Copy, scale=0.5)
+        tt(W(19, SCH), V("acc", 0, SCH), V("acc", 16, 16 + SCH), A.subtract)
+        tt(W(33, SCH), W(19, SCH), W(32, SCH), A.add)
+        cp(O_RK, W(33))
+        KP, CUM = V("kp", 0, NS), V("cum", 16, 16 + NS)
+        cp(KP, IX(V("kptab", 0, C), O_RK))
+        scan(CUM, KP, KP, NN, A.add, A.max)
+        ts(W(34, 6), KT, XA, A.is_lt)
+        tt(W(35, 6), W(34, 6), W(29, 6), A.mult)
+        for m in range(3, 6):
+            n = 16 * m + 112
+            act(V("j3", NS * (m - 1), NS * (m - 1) + n), V("cum", 16, 16 + n), AF.Sign, bias=col("cf", 76 + m), scale=-1.0, acc=col("acc", 52 + m))
+        for m in range(3):
+            n = 16 * m + 112
+            ts(V("tf", NS * m, NS * m + n), V("cum", 16, 16 + n), col("cf", 4 + m), A.is_le, 2.0, A.mult)
+            red(col("acc", 52 + m), V("tf", NS * m, NS * m + n))
+        tt(W(20, 6), V("acc", 52, 58), AT, A.add)
+        tt(W(36, 6), W(20, 6), W(35, 6), A.max)
+        ts(O_F, W(36, 6), 0.5, A.mult)
+        for b in range(4):
+            act(V("gq", K * b, K * b + K), IX(V("tq", TW * b, TW * b + TW), O_F), AF.Copy)
+            tt(V("ft", b, 4 * K, 4), IX(V("tt", TS * b, TS * b + TW), O_F), V("gq", K * b, K * b + K), A.add)
+        qf, sf, ql, sl = ["%s%d" % (n, t) for n in ("qf", "sf", "ql", "sl")]
+        quant(V(qf, 0, 128), V(sf, 0, 128), V("ft", 0, 512))
+        dst = T.cores[rank ^ (1 << t)]
+        rid, pid = topo.addr(dst)[:2]
+        mask = topo.mask(core, dst)
+        ne = len(topo.engines(core, dst))
+        arr = T.sem["ar%d" % t]
+        op("g", lambda qf=qf, ql=ql, arr=arr, pid=pid, rid=rid, mask=mask: g.remote_dma(
+            T[ql][:, 0:K].bitcast(u8), T[qf][:, 0:K].bitcast(u8), arr, T.sem.sent, pid, rid, mask), [], [V(qf, 0, K)], 500, dma=("", 0), lat=4000)
+        op("g", lambda sf=sf, sl=sl, arr=arr, pid=pid, rid=rid, mask=mask: g.remote_dma(
+            T[sl][:, 0:K], T[sf][:, 0:K], arr, T.sem.sent, pid, rid, mask), [], [V(sf, 0, K)], 500, dma=("", 0), lat=4000)
+        op("arrive", None, [V(ql, 0, K), V(sl, 0, K)], [V(qf, 0, K)], 0, dma=("ar%d" % t, 2 * ne), lat=5000)
+
+        for m in range(M):
+            n = 16 * m + 15
+            b0 = 208 * m if m < 6 else 208 * (11 - m) + 16 * (12 - m)
+            scan(V("lp", b0 + 1, b0 + 1 + n), V("sg", NS * m, NS * m + n), V("irow", 0, n), 1.0, A.min, A.max)
+        tt(V("lb", 0, NS), IX(V("lp", 0, 6 * 208), O_LP), oh, A.mult)
+        scan(V("lc", 0, NS), V("keepb", 0, NS), V("lb", 0, NS), 0.0, A.mult, A.add)
+        tt(W(21), QV, PK, A.is_ge)
+        tt(W(22), W(21), CN, A.mult)
+        lin(W(23), W(22), 1.0, 1.0)
+        ts(W(40), W(33), float(K), A.is_lt)
+        tt(W(41), W(40), W(15), A.mult)
+        lin(W(42), W(41), 63.0 / 256 - 1.0, 1.0)
+        tt(W(43), W(42), W(23), A.min)
+        tt(W(37), W(43), ends("lc", 0), A.min)
+        ts(O_L, W(37), -256.0, A.mult, 255.0, A.add)
+        tt(W(44), W(40), CK, A.mult)
+        ts(O_KC, W(44), NS + 1.0, A.add)
+        lin(V("nc", 0, C), IO(0, C), 0.0, 1.0)
+        act(V("cpv", 0, NS), V("cum", 15, 15 + NS), AF.Copy)
+        tt(V("na", 0, NS), IX(V("cum", 16, 18 + NS), O_L), V("cpv", 0, NS), A.is_ge)
+        cp(IX(V("nc", 0, C), O_QT), V("na", 0, NS))
+        tt(V("ncs", 16, 15 + NS), V("nc", 1, C - 2, 2), V("nc", 2, C, 2), A.min)
+        act(V("r0", 0, NS), IX(V("cum", 16, 18 + NS), O_KC), AF.Copy)
+        scan(V("r1", 0, NS), V("ncs", 15, 15 + NS), V("r0", 0, NS), 0.0, A.mult, A.max)
+        scan(RV("r2", 0, NS), RV("ncs", 16, 16 + NS), RV("r1", 0, NS), 0.0, A.mult, A.max)
+        tt(V("r3", 0, NS), IX(V("r2", 0, NS + 1), O_L), V("r1", 0, NS), A.max)
+        scan(V("r4", 0, NS), V("ncs", 15, 15 + NS), V("r3", 0, NS), 0.0, A.mult, A.max)
+        scan(RV("r5", 0, NS), RV("ncs", 16, 16 + NS), RV("r4", 0, NS), 0.0, A.mult, A.max)
+        ts(W(24, 24), JT, XA, A.is_lt)
+        tt(W(26, 24), W(24, 24), J192, A.mult)
+        tt(W(38, 24), W(26, 24), CS0, A.max)
+        cp(O_CS, W(38, 24))
+        tt(V("hb", 0, C, 2), IX(V("r5", 0, TW), O_CE), V("oh", 0, C, 2), A.mult)
+        tt(V("hb", 1, C, 2), IX(V("r5", 0, TW), O_CO), V("oh", 1, C, 2), A.mult)
+        scan(V("hc", 0, C), V("keepb", 0, C), V("hb", 0, C), 0.0, A.mult, A.add)
+        ts(O_H, ends("hc", 0, 2 * M), -1.0, A.add)
+        if t == R - 1:
+            act(V("et", 0, NS), IX(IO(0, C), O_PK), AF.Copy)
+            act(V("er", 0, K), IX(V("et", 0, TW), O_F), AF.Copy)
+
+        XN = "x%d" % (t + 1)
+        for b in range(4):
+            mm(PS(b, 0, 128), V("qw", 128 * b, 128 * b + 128), V("sw", 128 * b, 128 * b + 128), V(ql, 0, 128), V(sl, 0, 128))
+            act(V("ht", K * b, K * b + K), PS(b, 0, K), AF.Relu, scale=0.03125)
+        for b in (2, 3):
+            act(V("hg", C * (b - 2), C * (b - 1)), IX(V("ht", K * b, K * b + K), O_H), AF.Copy)
+        for b in (0, 1):
+            tt(V(XN, b, 4 * C, 4), IX(V("ht", K * b, K * b + K), O_H), TB(b), A.add)
+        for b in (2, 3):
+            tt(V(XN, b, 4 * C, 4), V("hg", C * (b - 2), C * (b - 1)), PS(4 + b, 0, C), A.add)
+
+    act(V("olr", 0, C), IX(V("er", 0, K), O_H), AF.Copy)
+    for k in range(8):
+        dma("y", "out", T.ol[k:k + 1, :], T.olr[16 * k:16 * k + 1, :], [], [V("olr", 0, C)])
+    QX, SX = V("qx%d" % R, 0, C), V("sx%d" % R, 0, C)
+    quant(QX, SX, V("x%d" % R, 0, 4 * C))
+    for h in range(2):
+        mm(PS(h, 0, NS), V("qv", 0, 128), V("sv", 0, 128), V(QX[1], NS * h, NS * h + NS), V(SX[1], NS * h, NS * h + NS))
+    dma("y", "out", T.oc[:], QX[0].bitcast(u8), [], [QX])
+    cp(V("ysb", 0, NS), PS(0, 0, NS))
+    act(V("ysb", NS, C), PS(1, 0, NS), AF.Copy)
+    dma("s", "out", T.y[:], T.ysb[:], [], [V("ysb", 0, C)])
+    for k in range(4):
+        dma("y", "out", T.osc[4 * k:4 * k + 4, :], T[SX[1]][32 * k:32 * k + 4, :], [], [SX])
+
+    def meet(a, b):
+        return a[1] < b[2] and b[1] < a[2] and (a[1] - b[1]) % math.gcd(a[3], b[3]) == 0
+
+    deps, touch = [], {}
+    for i, (q, fn, ws, rs, d, ns, lat) in enumerate(ops):
+        ds = set()
+        for a, wr in [(a, True) for a in ws] + [(a, False) for a in rs]:
+            for j, b, wr2 in touch.get(a[0], []):
+                if (a[0][:2] == "ps" and (ops[j][0] != q or wr or wr2)) or ((wr or wr2) and meet(a, b)):
+                    ds.add(j)
+        deps.append(ds)
+        for a, wr in [(a, True) for a in ws] + [(a, False) for a in rs]:
+            touch.setdefault(a[0], []).append((i, a, wr))
+    n = len(ops)
+    users = [[] for i in range(n)]
+    for i in range(n):
+        for j in deps[i]:
+            users[j].append(i)
+
+    def schedule(before, after, prio, back, wake, slack):
+        left = [len(ds) for ds in before]
+        ready = [i for i in range(n) if not left[i]]
+        can, free, order, end = [(ops[i][6] if back else 0.0) for i in range(n)], {}, [], [0.0] * n
+        while ready:
+            first, q = min((max(can[i], free.get(ops[i][0], 0.0)), ops[i][0]) for i in ready)
+            i = -max((prio[i], -i) for i in ready if ops[i][0] == q and can[i] <= first + slack)[1]
+            end[i] = free[q] = max(can[i], free.get(q, 0.0)) + ops[i][5]
+            ready.remove(i)
+            order.append(i)
+            for u in after[i]:
+                can[u] = max(can[u], end[i] + ops[u if back else i][6] + wake)
+                left[u] -= 1
+                if not left[u]:
+                    ready.append(u)
+        return order, end
+
+    def span_of(order):
+        s = 0.0
+        for wake, far in CASES:
+            free, end = {}, [0.0] * n
+            for i in order:
+                q, lat = ops[i][0], (far if ops[i][0] == "arrive" else ops[i][6])
+                t0 = max([free.get(q, 0.0)] + [end[j] + wake for j in deps[i]])
+                free[q] = t0 + ops[i][5]
+                end[i] = free[q] + lat
+            s += max(end)
+        return s
+
+    if not ORDER:
+        seed = [12345]
+
+        def uni():
+            seed[0] = (seed[0] * 1103515245 + 12345) % 2147483648
+            return seed[0] / 2147483648.0
+
+        prio = [float(i) for i in range(n)]
+        for k in range(TURNS):
+            wake, slack = 40 + 90 * uni(), 40 * uni()
+            if ORDER and k % 4:
+                back = [x + 2 * NOISE * (1 + k % 3) * (uni() + uni() + uni() - 1.5) for x in ORDER[2]]
+            else:
+                back = schedule(users, deps, prio, True, wake, slack)[1]
+            order, prio = schedule(deps, users, back, False, wake, slack)
+            span = span_of(order)
+            if not ORDER or span < ORDER[0]:
+                ORDER[:] = [span, order, back]
+    order = ORDER[1]
+    place = {i: k for k, i in enumerate(order)}
+    waits = {}
+    for i in order:
+        last = {}
+        for j in sorted(deps[i], key=lambda j: place[j]):
+            last[ops[j][4][0] if ops[j][4] else ops[j][0]] = j
+        waits[i] = [] if ops[i][0] == "arrive" else list(last.values())
+    total = {}
+    for o in ops:
+        if o[4] and o[4][0]:
+            total[o[4][0]] = total.get(o[4][0], 0) + o[4][1]
+    needed, seen = set(), {}
+    for i in order:
+        for j in waits[i]:
+            if not ops[j][4] and seen.get((ops[i][0], ops[j][0]), -1) < place[j]:
+                needed.add(j)
+                seen[(ops[i][0], ops[j][0])] = place[j]
+    token, count, seen, mark = {}, {}, {}, {}
+    for i in order:
+        q, fn, ws, rs, d, ns, lat = ops[i]
+        if q == "arrive":
+            continue
+        for j in waits[i]:
+            if ops[j][4]:
+                s, c = ops[j][4][0], total[ops[j][4][0]]
+            elif mark.get((q, ops[j][0]), -1) < place[j]:
+                s, c = token[j]
+                mark[(q, ops[j][0])] = place[j]
+            else:
+                continue
+            if seen.get((q, s), 0) < c:
+                Q[q].wait_ge(T.sem[s], c)
+                seen[(q, s)] = c
+        ins = fn()
+        if d:
+            if d[0]:
+                ins.then_inc(T.sem[d[0]], d[1])
+        elif i in needed:
+            s = COUNTER[q]
+            count[s] = count.get(s, 0) + 1
+            ins.then_inc(T.sem[s], 1)
+            token[i] = (s, count[s])
+    g.sync.wait_ge(T.sem.out, total["out"])
+    g.wait_ge(T.sem.sent, 2 * R * ne)

@@ -8,10 +8,11 @@ BIG = 1.0e29
 KS = 2.0 ** -18
 INIT = (500 * 512 + C + 1) * KS
 SCH = 6
+VW = 32
 TW = NS + K
 TS = NS + C
-TURNS, NOISE = 500, 60.0
-CASES = ((50.0, 3500.0), (120.0, 5000.0))
+TURNS, NOISE = 900, 60.0
+CASES = ((100.0, 8000.0), (200.0, 5000.0), (130.0, 5500.0))
 ORDER = []
 
 X4, U8, F32, BF, I32, U16 = "float8_e4m3fn_x4", "uint8", "float32", "bfloat16", "int32", "uint16"
@@ -24,11 +25,11 @@ for _d, _l in [
     (I32, [("ci", 64), ("wi", 48)]),
     (U16, [("co", 64), ("of", 160)]),
     (BF, [("x0", 4 * C), ("x1", 4 * C), ("x2", 4 * C), ("ut", 512), ("vt", 512), ("zt", 512), ("ez", 516), ("ft", 512), ("keepb", C), ("kptab", C),
-          ("irow", NS), ("sg", M * NS), ("fl", (M - SCH) * NS), ("fc", (M - SCH) * NS), ("s2", SCH * NS), ("j2", SCH * NS), ("j3", 5 * NS),
+          ("irow", NS), ("kw", VW * M), ("sg", M * NS), ("fl", (M - SCH) * NS), ("fc", (M - SCH) * NS), ("s2", SCH * NS), ("j2", SCH * NS), ("j3", 5 * NS),
           ("eb", NS), ("ec", NS), ("kp", NS), ("cum", 24 + NS), ("tf", 3 * NS), ("lp", 6 * 208), ("lb", NS), ("lc", NS), ("na", NS), ("nc", C),
           ("cpv", NS), ("ncs", 16 + NS), ("r0", NS), ("r1", NS), ("r2", NS + 8), ("r3", NS), ("r4", NS), ("r5", TW), ("hb", C), ("hc", C)]),
     (F32, [("cf", 192), ("j16", C), ("oh", C), ("tri", NS), ("keep", C), ("uraw", 2 * C), ("utab", 2 * C), ("iot", C), ("c2t", NS), ("al", NS),
-           ("ar", NS), ("a0", NS), ("zm", K), ("z0", K), ("idn", 128), ("vv", NS), ("pp", NS), ("mk", 4 * NS), ("wsc", 4 * NS), ("ssb", C + 8),
+           ("ar", NS), ("a0", NS), ("zm", K), ("z0", K), ("idn", 128), ("vv", NS), ("pp", C), ("pq", NS), ("mk", 4 * NS), ("wsc", 4 * NS), ("ssb", C + 8),
            ("w", 768), ("thp", 16), ("acc", 64), ("uu", NS), ("um", NS), ("lr", M * 208), ("lm", NS), ("rm", NS), ("ex", NS), ("sm", NS),
            ("sc", NS), ("ngp", NS), ("eq", NS), ("dd", 112), ("npc", K), ("cx", 112), ("zk", K), ("zs", K), ("tt", 4 * TS), ("tq", 4 * TW),
            ("gq", 4 * K), ("ht", 4 * K), ("hg", 2 * C), ("et", TW), ("er", K), ("olr", C), ("ysb", C)]),
@@ -212,6 +213,7 @@ def rank_program(g, core, T, topo):
     lin(col("ssb", C), IO(0, 1), 0.0, BIG)
     lin(col("ssb", C + 1), IO(0, 1), 0.0, -BIG)
     fill(col("dd", 0), 0)
+    lin(V("pp", NS, C), IO(0, NS), 0.0, -BIG)
     lin(col("cx", 0), IO(0, 1), 0.0, 0.5)
     ts(V("tri", 0, NS), V("j16", 0, NS), PM, A.is_lt)
     fill(V("kptab", 0, K), 1)
@@ -225,11 +227,13 @@ def rank_program(g, core, T, topo):
     ts(V("ci", 24, 30), V("ci", 16, 22), 126, A.bitwise_and)
     cp(KD, V("ci", 24, 30))
     fill(V("cf", 82, 85), 0)
-    iota(V("cf", 85, 88), [[16, 3]], 160)
+    fill(V("cf", 85, 88), NS)
     iota(V("cf", 88, 88 + SCH), [[16, SCH]], 0)
     fill(V("cf", 88 + SCH, 100), 0)
     fill(V("acc", 16, 32), 0)
     fill(col("cum", 15), 0)
+    fill(V("kw", 0, VW * M), 1)
+    fill(V("kw", 0, VW * M, VW), 0)
     fill(V("ft", 4 * K, 512), 0)
     fill(V("zt", 0, 512), 0)
     for b in range(4):
@@ -248,6 +252,7 @@ def rank_program(g, core, T, topo):
     oh = V("oh", 0, NS)
     O_K, O_PK, O_QV, O_QT, O_RK, O_L = [V("of", 12 * j, 12 * j + M) for j in range(6)]
     O_F, O_CE, O_CO, O_CS, O_H, O_KC = V("of", 72, 78), V("of", 80, 92), V("of", 92, 104), V("of", 80, 104), V("of", 104, 128), V("of", 128, 140)
+    O_NP = V("of", 140, 152)
 
     def TB(b, lo=0, hi=C, step=1):
         return V("tt", TS * b + NS + lo, TS * b + NS + hi, step)
@@ -271,7 +276,9 @@ def rank_program(g, core, T, topo):
         for b in range(4):
             act(TB(b), PS(4 + b, 0, C), AF.Copy)
         for m in range(M):
-            act(V("sg", NS * m, NS * m + NS - 1), V("vv", 0, NS - 1), AF.Sign, bias=col("w", m), scale=-1.0, acc=col("acc", 32 + m))
+            act(V("sg", NS * m, NS * m + NS - 1 - VW), V("vv", VW, NS - 1), AF.Sign, bias=col("w", m), scale=-1.0, acc=col("acc", 32 + m))
+            ts(V("fl", VW * m, VW * m + VW), V("vv", 0, VW), col("w", m), A.is_lt)
+        scan(V("fc", 0, VW * M), V("kw", 0, VW * M), V("fl", 0, VW * M), 0.0, A.mult, A.add)
         tt(V("pp", 0, NS), V("ssb", 1, C, 2), PS(0, 0, C, 2), A.max)
         tt(V("mk", NS, 2 * NS), PS(0, 0, C, 2), oh, A.mult)
         tt(V("mk", 1, NS), PS(0, 1, C - 2, 2), V("oh", 1, NS), A.mult)
@@ -286,6 +293,18 @@ def rank_program(g, core, T, topo):
         tt(W(8), EN_, E_, A.is_gt)
         tt(W(7), W(6), AW, A.is_gt)
         tt(W(28), W(8), AW, A.mult)
+        NPW = W(12)
+        tt(W(13), OP_, E_, A.is_ge)
+        tt(W(14), W(13), AW, A.mult)
+        tt(W(45), AW, W(5), A.max)
+        tt(W(46), W(45), W(14), A.subtract)
+        ts(NPW, W(46), -1.0, A.mult, 1.0, A.add)
+        ts(W(18), NPW, float(NS), A.mult)
+        tt(W(47), W(18), CW, A.add)
+        cp(O_NP, W(47))
+        act(V("pq", 0, NS), IX(V("pp", 0, C), O_NP), AF.Copy)
+        ts(W(13), NPW, -BIG, A.mult)
+        tt(W(14), W(13), THP, A.add)
         CS0 = W(9, 24)
         tt(V("w", 16 * 9, 16 * 9 + 12), CW, W(7), A.subtract)
         tt(V("w", 16 * 9 + 12, 16 * 9 + 24), CW, W(28), A.add)
@@ -299,7 +318,8 @@ def rank_program(g, core, T, topo):
             act(V("sg", NS * m, NS * m + NS), V("pp", 0, NS), AF.Sign, bias=col("w", 16 + m), scale=-1.0)
         for b in range(4):
             act(V("tt", TS * b, TS * b + NS), IX(TB(b), O_PK), AF.Copy, scale=0.5)
-        tt(W(11), V("acc", 32, 32 + M), BB, A.add)
+        tt(W(39), BB, V("fc", VW - 1, VW * M, VW), A.add)
+        tt(W(11), V("acc", 32, 32 + M), W(39), A.add)
         ts(O_K, W(11), 2.0, A.mult)
         tt(V("uu", 0, NS), IX(V("utab", 0, 2 * C), O_K), V("c2t", 0, NS), A.add)
         lin(V("um", 0, NS), V("uu", 0, NS), 1.0, -1.0)
@@ -310,19 +330,16 @@ def rank_program(g, core, T, topo):
         tt(V("lm", 0, NS), IX(V("lr", 0, M * 208), O_LR), V("al", 0, NS), A.add)
         tt(V("rm", 0, NS), IX(V("lr", 16, M * 208), O_LR), V("ar", 0, NS), A.add)
         scan(V("ex", 0, NS), V("lm", 0, NS), V("rm", 0, NS), 100.0, A.min, A.min)
-        QI, NPW, QV = V("wi", 16, 16 + M), W(12), W(13)
+        QI = V("wi", 16, 16 + M)
         ts(V("wi", 0, M), ends("ex", 0), 1.0 / KS, A.mult)
         ts(QI, V("wi", 0, M), 511, A.bitwise_and)
-        tt(NPW, QI, PK, A.is_equal)
-        ts(W(14), NPW, float(C), A.mult)
-        tt(QV, W(14), QI, A.max)
-        cp(O_QV, QV)
+        cp(O_QV, QI)
         SS = V("ssb", 0, C + 2)
         tt(V("sm", 0, NS), IX(SS, O_QV), oh, A.mult)
-        tt(V("ngp", 0, NS), IX(SS, O_QV), V("pp", 0, NS), A.subtract)
+        tt(V("ngp", 0, NS), IX(SS, O_QV), V("pq", 0, NS), A.subtract)
         scan(V("sc", 0, NS), V("keep", 0, NS), V("sm", 0, NS), 0.0, A.mult, A.add)
         TH = V("thp", 0, M)
-        tt(TH, ends("sc", 0), THP, A.subtract)
+        tt(TH, ends("sc", 0), W(14), A.subtract)
         tt(W(16), QI, PK, A.subtract)
         ts(W(15), QI, float(C), A.is_lt)
         tt(W(30), W(16), W(15), A.mult)
@@ -347,14 +364,13 @@ def rank_program(g, core, T, topo):
         tt(V("eq", 0, NS), IX(TH, O_M), V("ngp", 0, NS), A.is_equal)
         tt(V("eb", 0, NS), V("eq", 0, NS), V("tri", 0, NS), A.mult)
         scan(V("ec", 0, NS), V("keepb", 0, NS), V("eb", 0, NS), 0.0, A.mult, A.add)
-        ts(W(18), NPW, float(NS), A.mult)
         tt(W(31), W(18), BASE, A.add)
         tt(W(32), W(31), ends("ec", 0), A.add)
         tt(V("w", 16 * 33 + SCH, 16 * 33 + M), V("w", 16 * 32 + SCH, 16 * 32 + M), V("fc", NS - 1, (M - SCH) * NS, NS), A.add)
         for b in range(4):
             act(V("tq", TW * b, TW * b + NS), IX(TB(b), O_QT), AF.Copy, scale=0.5)
-        tt(W(19, SCH), V("acc", 0, SCH), V("acc", 16, 16 + SCH), A.subtract)
-        tt(W(33, SCH), W(19, SCH), W(32, SCH), A.add)
+        tt(W(19, SCH), W(32, SCH), V("acc", 16, 16 + SCH), A.subtract)
+        tt(W(33, SCH), W(19, SCH), V("acc", 0, SCH), A.add)
         cp(O_RK, W(33))
         KP, CUM = V("kp", 0, NS), V("cum", 16, 16 + NS)
         cp(KP, IX(V("kptab", 0, C), O_RK))
@@ -362,15 +378,15 @@ def rank_program(g, core, T, topo):
         ts(W(34, 6), KT, XA, A.is_lt)
         tt(W(35, 6), W(34, 6), W(29, 6), A.mult)
         for m in range(3, 6):
-            n = 16 * m + 112
-            act(V("j3", NS * (m - 1), NS * (m - 1) + n), V("cum", 16, 16 + n), AF.Sign, bias=col("cf", 76 + m), scale=-1.0, acc=col("acc", 52 + m))
+            act(V("j3", NS * (m - 1), NS * m), CUM, AF.Sign, bias=col("cf", 76 + m), scale=-1.0, acc=col("acc", 52 + m))
         for m in range(3):
             n = 16 * m + 112
             ts(V("tf", NS * m, NS * m + n), V("cum", 16, 16 + n), col("cf", 4 + m), A.is_le, 2.0, A.mult)
             red(col("acc", 52 + m), V("tf", NS * m, NS * m + n))
-        tt(W(20, 6), V("acc", 52, 58), AT, A.add)
-        tt(W(36, 6), W(20, 6), W(35, 6), A.max)
-        ts(O_F, W(36, 6), 0.5, A.mult)
+        tt(W(20, 6), W(35, 6), AT, A.subtract)
+        tt(W(36, 6), W(20, 6), V("acc", 52, 58), A.max)
+        ts(V("of", 72, 75), W(36, 3), 0.5, A.mult)
+        ts(V("of", 75, 78), V("w", 16 * 36 + 3, 16 * 36 + 6), float(NS), A.add, 0.5, A.mult)
         for b in range(4):
             act(V("gq", K * b, K * b + K), IX(V("tq", TW * b, TW * b + TW), O_F), AF.Copy)
             tt(V("ft", b, 4 * K, 4), IX(V("tt", TS * b, TS * b + TW), O_F), V("gq", K * b, K * b + K), A.add)
@@ -385,7 +401,7 @@ def rank_program(g, core, T, topo):
             T[ql][:, 0:K].bitcast(u8), T[qf][:, 0:K].bitcast(u8), arr, T.sem.sent, pid, rid, mask), [], [V(qf, 0, K)], 500, dma=("", 0), lat=4000)
         op("g", lambda sf=sf, sl=sl, arr=arr, pid=pid, rid=rid, mask=mask: g.remote_dma(
             T[sl][:, 0:K], T[sf][:, 0:K], arr, T.sem.sent, pid, rid, mask), [], [V(sf, 0, K)], 500, dma=("", 0), lat=4000)
-        op("arrive", None, [V(ql, 0, K), V(sl, 0, K)], [V(qf, 0, K)], 0, dma=("ar%d" % t, 2 * ne), lat=5000)
+        op("arrive", None, [V(ql, 0, K), V(sl, 0, K)], [V(qf, 0, K)], 0, dma=("ar%d" % t, 2 * ne), lat=6500)
 
         for m in range(M):
             n = 16 * m + 15
@@ -393,7 +409,7 @@ def rank_program(g, core, T, topo):
             scan(V("lp", b0 + 1, b0 + 1 + n), V("sg", NS * m, NS * m + n), V("irow", 0, n), 1.0, A.min, A.max)
         tt(V("lb", 0, NS), IX(V("lp", 0, 6 * 208), O_LP), oh, A.mult)
         scan(V("lc", 0, NS), V("keepb", 0, NS), V("lb", 0, NS), 0.0, A.mult, A.add)
-        tt(W(21), QV, PK, A.is_ge)
+        tt(W(21), QI, PK, A.is_ge)
         tt(W(22), W(21), CN, A.mult)
         lin(W(23), W(22), 1.0, 1.0)
         ts(W(40), W(33), float(K), A.is_lt)
@@ -430,25 +446,31 @@ def rank_program(g, core, T, topo):
         XN = "x%d" % (t + 1)
         for b in range(4):
             mm(PS(b, 0, 128), V("qw", 128 * b, 128 * b + 128), V("sw", 128 * b, 128 * b + 128), V(ql, 0, 128), V(sl, 0, 128))
-            act(V("ht", K * b, K * b + K), PS(b, 0, K), AF.Relu, scale=0.03125)
-        for b in (2, 3):
-            act(V("hg", C * (b - 2), C * (b - 1)), IX(V("ht", K * b, K * b + K), O_H), AF.Copy)
-        for b in (0, 1):
-            tt(V(XN, b, 4 * C, 4), IX(V("ht", K * b, K * b + K), O_H), TB(b), A.add)
-        for b in (2, 3):
-            tt(V(XN, b, 4 * C, 4), V("hg", C * (b - 2), C * (b - 1)), PS(4 + b, 0, C), A.add)
+            if b < 2:
+                ts(V("ht", K * b, K * b + K), PS(b, 0, K), 0.0, A.max, 0.03125, A.mult)
+            else:
+                act(V("ht", K * b, K * b + K), PS(b, 0, K), AF.Relu, scale=0.03125)
+        n = NS if t == R - 1 else C
+        for lo in range(0, C, n):
+            o_h = V("of", 104 + lo // 16, 104 + (lo + n) // 16)
+            for b in (2, 3):
+                act(V("hg", C * (b - 2) + lo, C * (b - 2) + lo + n), IX(V("ht", K * b, K * b + K), o_h), AF.Copy)
+            for b in (0, 1):
+                tt(V(XN, 4 * lo + b, 4 * (lo + n), 4), IX(V("ht", K * b, K * b + K), o_h), TB(b, lo, lo + n), A.add)
+            for b in (2, 3):
+                tt(V(XN, 4 * lo + b, 4 * (lo + n), 4), V("hg", C * (b - 2) + lo, C * (b - 2) + lo + n), PS(4 + b, lo, lo + n), A.add)
 
     act(V("olr", 0, C), IX(V("er", 0, K), O_H), AF.Copy)
     for k in range(8):
         dma("y", "out", T.ol[k:k + 1, :], T.olr[16 * k:16 * k + 1, :], [], [V("olr", 0, C)])
     QX, SX = V("qx%d" % R, 0, C), V("sx%d" % R, 0, C)
-    quant(QX, SX, V("x%d" % R, 0, 4 * C))
     for h in range(2):
-        mm(PS(h, 0, NS), V("qv", 0, 128), V("sv", 0, 128), V(QX[1], NS * h, NS * h + NS), V(SX[1], NS * h, NS * h + NS))
-    dma("y", "out", T.oc[:], QX[0].bitcast(u8), [], [QX])
-    cp(V("ysb", 0, NS), PS(0, 0, NS))
-    act(V("ysb", NS, C), PS(1, 0, NS), AF.Copy)
-    dma("s", "out", T.y[:], T.ysb[:], [], [V("ysb", 0, C)])
+        lo, hi = NS * h, NS * h + NS
+        quant(V(QX[1], lo, hi), V(SX[1], lo, hi), V("x%d" % R, 4 * lo, 4 * hi))
+        mm(PS(h, 0, NS), V("qv", 0, 128), V("sv", 0, 128), V(QX[1], lo, hi), V(SX[1], lo, hi))
+        dma("y", "out", T.oc[:, 4 * lo:4 * hi], V(QX[1], lo, hi)[0].bitcast(u8), [], [V(QX[1], lo, hi)])
+        act(V("ysb", lo, hi), PS(h, 0, NS), AF.Copy)
+        dma("s", "out", T.y[:, lo:hi], T.ysb[:, lo:hi], [], [V("ysb", lo, hi)])
     for k in range(4):
         dma("y", "out", T.osc[4 * k:4 * k + 4, :], T[SX[1]][32 * k:32 * k + 4, :], [], [SX])
 
@@ -509,7 +531,7 @@ def rank_program(g, core, T, topo):
 
         prio = [float(i) for i in range(n)]
         for k in range(TURNS):
-            wake, slack = 40 + 90 * uni(), 40 * uni()
+            wake, slack = 80 + 150 * uni(), 200 * uni() ** 2
             if ORDER and k % 4:
                 back = [x + 2 * NOISE * (1 + k % 3) * (uni() + uni() + uni() - 1.5) for x in ORDER[2]]
             else:

@@ -1,18 +1,25 @@
 import math
-from concourse.mybir import dt, AluOpType as A, ActivationFunctionType as AF, AxisListType
+from concourse.mybir import dt, AluOpType as A, ActivationFunctionType as AF
 
 C, K, R = 384, 96, 2
 NS = C // 2
 M = NS // 16
 BIG = 1.0e29
-KS = 2.0 ** -18
-INIT = (500 * 512 + C + 1) * KS
+KS = 2.0 ** -20
+INIT = (500 * 2048 + 1024) * KS
 SCH = 6
-VW = 32
-TW = NS + K
-TS = NS + C
-TURNS, NOISE = 900, 60.0
-CASES = ((100.0, 8000.0), (200.0, 5000.0), (130.0, 5500.0))
+VW = 0
+IVV = 3
+HTV = 2
+FS = 2
+HS = (2, 2)
+TW = NS + K + 1
+TQ = NS + K + 8
+TS = NS + C + 8
+SW = 1024 + 2 * C + 8
+PIECES = (((0, 224), (224, C)), ((0, 224), (224, C)), ((0, 224), (224, C)))
+TURNS, NOISE, MOVES, HEAT = 300, 200.0, 6000, 150.0
+CASES = ((0.83, 200.0, 3500.0), (0.9, 250.0, 3000.0), (1.1, 150.0, 4500.0))
 ORDER = []
 
 X4, U8, F32, BF, I32, U16 = "float8_e4m3fn_x4", "uint8", "float32", "bfloat16", "int32", "uint16"
@@ -22,17 +29,17 @@ for _d, _l in [
           ("ql0", K + 128), ("ql1", K + 128)]),
     (U8, [("sx0", C), ("sx1", C), ("sx2", C), ("su", 128), ("sur", 128), ("sv", 128), ("se", 512), ("sw", 512), ("sf0", 128), ("sf1", 128),
           ("sl0", K + 128), ("sl1", K + 128)]),
-    (I32, [("ci", 64), ("wi", 48)]),
-    (U16, [("co", 64), ("of", 160)]),
-    (BF, [("x0", 4 * C), ("x1", 4 * C), ("x2", 4 * C), ("ut", 512), ("vt", 512), ("zt", 512), ("ez", 516), ("ft", 512), ("keepb", C), ("kptab", C),
-          ("irow", NS), ("kw", VW * M), ("sg", M * NS), ("fl", (M - SCH) * NS), ("fc", (M - SCH) * NS), ("s2", SCH * NS), ("j2", SCH * NS), ("j3", 5 * NS),
-          ("eb", NS), ("ec", NS), ("kp", NS), ("cum", 24 + NS), ("tf", 3 * NS), ("lp", 6 * 208), ("lb", NS), ("lc", NS), ("na", NS), ("nc", C),
-          ("cpv", NS), ("ncs", 16 + NS), ("r0", NS), ("r1", NS), ("r2", NS + 8), ("r3", NS), ("r4", NS), ("r5", TW), ("hb", C), ("hc", C)]),
-    (F32, [("cf", 192), ("j16", C), ("oh", C), ("tri", NS), ("keep", C), ("uraw", 2 * C), ("utab", 2 * C), ("iot", C), ("c2t", NS), ("al", NS),
-           ("ar", NS), ("a0", NS), ("zm", K), ("z0", K), ("idn", 128), ("vv", NS), ("pp", C), ("pq", NS), ("mk", 4 * NS), ("wsc", 4 * NS), ("ssb", C + 8),
-           ("w", 768), ("thp", 16), ("acc", 64), ("uu", NS), ("um", NS), ("lr", M * 208), ("lm", NS), ("rm", NS), ("ex", NS), ("sm", NS),
-           ("sc", NS), ("ngp", NS), ("eq", NS), ("dd", 112), ("npc", K), ("cx", 112), ("zk", K), ("zs", K), ("tt", 4 * TS), ("tq", 4 * TW),
-           ("gq", 4 * K), ("ht", 4 * K), ("hg", 2 * C), ("et", TW), ("er", K), ("olr", C), ("ysb", C)]),
+    (I32, [("ci", 64), ("wi", 64)]),
+    (U16, [("co", 64), ("of", 176)]),
+    (BF, [("x0", 4 * C), ("x1", 4 * C), ("x2", 4 * C), ("ut", 512), ("vt", 512), ("ez", 516), ("zt", 512), ("ft", 512), ("keepb", C), ("kptab", 416),
+          ("irow", NS), ("kw", VW * M + 2), ("fv", VW * M + 2), ("sg", M * NS), ("fl", M * NS), ("fc", M * K), ("pk", NS), ("three", NS), ("yy", NS),
+          ("s2", SCH * NS), ("j2", SCH * NS), ("j3", 6 * NS), ("eq", NS), ("ec", NS), ("noh", NS), ("kp", NS), ("cum", 16 + NS), ("tf", 6 * NS),
+          ("lp", 6 * 208), ("lb", NS), ("lc", NS), ("an", NS), ("cpv", NS), ("nc", 464), ("r0", NS), ("r4", NS), ("r5", NS + 16), ("hb", C + 2), ("hc", C)]),
+    (F32, [("cf", 192), ("j16", C), ("oh", C), ("keep", NS), ("utab", C), ("rb", NS), ("iot", 2 * C), ("al", NS), ("odd", NS), ("vs", C),
+           ("ar", NS), ("a0", NS), ("zm", K), ("z0", K), ("idn", 128), ("pp", NS), ("mk", 4 * NS), ("wsc", 4 * NS), ("ssb", SW),
+           ("w", 768), ("thp", 16), ("acc", 64), ("iv", 6 * K), ("uu", NS), ("um", NS), ("lr", M * 208), ("lm", NS), ("rm", NS), ("ex", NS), ("sm", NS),
+           ("sc", NS), ("ngp", NS), ("aw", K // 2), ("zk", K), ("zs", K), ("mj", C + 2), ("tt", 4 * TS), ("tq", 4 * TQ),
+           ("ht", 4 * K), ("hg", 4 * C), ("et", TW), ("er", K), ("olr", C), ("ysb", C)]),
 ]:
     for _n, _w in _l:
         SCRATCH[_n] = ("sbuf", [128, _w], _d)
@@ -67,9 +74,9 @@ def rank_program(g, core, T, topo):
 
     def cost(o, a, rate):
         if len(a) > 5:
-            return 50 + 1.6 * size(a)
+            return 60 + 1.6 * size(a)
         if len(o) > 5:
-            return 50 + 4.0 * size(o)
+            return 60 + 3.8 * size(o)
         return max(64, size(a) * rate)
 
     def half(*xs):
@@ -104,9 +111,6 @@ def rank_program(g, core, T, topo):
     def scan(o, a, b, init, f0, f1):
         op("v", lambda: g.vector.tensor_tensor_scan(o[0], a[0], b[0], ap(init), f0, f1), [o], [a, b, init], cost(o, a, half(o, a, b)))
 
-    def red(o, a):
-        op("v", lambda: g.vector.tensor_reduce(o[0], a[0], AxisListType.X, A.add), [o], [a], cost(o, a, 1))
-
     def ms(o, c):
         op("v", lambda: g.vector.memset(o[0], c), [o], [], cost(o, o, half(o)))
 
@@ -115,30 +119,30 @@ def rank_program(g, core, T, topo):
         if bias is not None:
             kw["bias"] = ap(bias)
         if scale is not None:
-            kw["scale"] = scale
+            kw["scale"] = ap(scale)
         if acc is not None:
             kw["accum_out"] = acc[0]
-        op("s", lambda: g.scalar.activation(o[0], a[0], f, **kw), [o] + ([acc] if acc else []), [a, bias], cost(o, a, 1) + (20 if acc else 0))
+        op("s", lambda: g.scalar.activation(o[0], a[0], f, **kw), [o] + ([acc] if acc else []), [a, bias, scale], cost(o, a, 1) + (24 if acc else 0))
 
     def lin(o, a, scale, bias):
         act(o, a, AF.Identity, bias=bias, scale=scale)
 
     def quant(q, s, a):
-        op("v", lambda: g.vector.quantize_mx(q[0], s[0], a[0]), [q, s], [a], 12 + 0.25 * size(a))
+        op("v", lambda: g.vector.quantize_mx(q[0], s[0], a[0]), [q, s], [a], 14 + 0.27 * size(a))
 
     def mm(o, lq, ls, rq, rs):
         op("t", lambda: g.tensor.matmul_mx(o[0], lq[0], ls[0], rq[0], rs[0], True, True), [o], [lq, ls, rq, rs], size(rq) + 16)
 
     def iota(o, pat, base, cm=0):
         if SCRATCH[o[1]][2] == I32:
-            op("g", lambda: g.iota(o[0], pat, base, cm), [o], [], 130 + 2 * size(o))
+            op("g", lambda: g.iota(o[0], pat, base, cm), [o], [], 156 + 2 * size(o))
         else:
-            op("g", lambda: g.iota(o[0], pat, base, cm, allow_small_or_imprecise_dtypes=True), [o], [], 130 + 2 * size(o))
+            op("g", lambda: g.iota(o[0], pat, base, cm, allow_small_or_imprecise_dtypes=True), [o], [], 156 + 2 * size(o))
 
     def fill(o, c):
         iota(o, [[0, size(o)]], c)
 
-    def dma(q, sem, out, in_, wr, rd, lat=2000.0):
+    def dma(q, sem, out, in_, wr, rd, lat=1900.0):
         op(q, lambda: Q[q].dma_start(out, in_), wr, rd, 60, dma=(sem, 16), lat=lat)
 
     def W(j, n=M):
@@ -155,241 +159,241 @@ def rank_program(g, core, T, topo):
 
     u8 = dt.uint8
     dma("y", "du", T.ut[:], T.u[:], [V("ut", 0, 512)], [])
-    dma("s", "dx1", T.x0[:, 2 * C:], T.x[:, 2 * C:], [V("x0", 2 * C, 4 * C)], [], 2500)
-    dma("y", "dx0", T.x0[:, :2 * C], T.x[:, :2 * C], [V("x0", 0, 2 * C)], [], 2500)
+    for h, (lo, hi) in enumerate(PIECES[0]):
+        dma("sy"[h], "dx%d" % h, T.x0[:, 4 * lo:4 * hi], T.x[:, 4 * lo:4 * hi], [V("x0", 4 * lo, 4 * hi)], [], 2300 + 300 * h)
     dma("y", "dw", T.qw[:].bitcast(u8), T.wc[:], [V("qw", 0, 512)], [V("x0", 0, 4 * C)])
     dma("y", "dw", T.sw[:], T.ws[:], [V("sw", 0, 512)], [V("x0", 0, 4 * C)])
     dma("y", "dv", T.vt[:], T.v[:], [V("vt", 0, 512)], [V("x0", 0, 4 * C)])
 
-    PM, CW, PK0, JW, J192 = col("cf", 0), V("cf", 4, 16), V("cf", 16, 28), V("cf", 28, 52), V("cf", 52, 76)
-    KH, AT, BASE, KT, KD, JT, CN = V("cf", 76, 82), V("cf", 82, 88), V("cf", 88, 100), V("cf", 100, 106), V("cf", 106, 112), V("cf", 112, 136), V("cf", 136, 148)
-    CK = V("cf", 156, 168)
+    PM, PAR, CW, CW4, KW = col("cf", 0), col("cf", 1), V("cf", 108, 120), V("cf", 108, 156), V("cf", 108, 114)
+    KH, KN, KC, DB, BASE = V("cf", 40, 46), V("cf", 46, 52), V("cf", 52, 58), V("cf", 64, 70), V("cf", 70, 82)
+    UC, UC1 = V("cf", 82, 94), V("cf", 94, 106)
     O_U, O_LR, O_M, O_LP = V("co", 0, 8), V("co", 8, 20), V("co", 20, 32), V("co", 32, 44)
     iota(col("ci", 0), [[1, 1]], 0, 1)
     iota(V("ci", 8, 16), [[16, 8]], 0)
     iota(V("j16", 0, C), [[0, 2 * M], [1, 16]], 0)
     iota(V("idn", 0, 128), [[-1, 128]], 0, 1)
     iota(IO(0, C), [[1, C]], 0)
-    iota(V("uraw", 0, 2 * C), [[-512, C], [1, 2]], C * 512)
+    lin(IO(C, 2 * C), IO(0, C), 1.0, float(C))
     ms(V("ez", 0, 516), 0.0)
+    ms(V("zt", 0, 512), 0.0)
+    for lo in range(0, SW, 512):
+        lin(V("ssb", lo, min(SW, lo + 512)), V("zt", 0, min(SW - lo, 512)), 0.0, BIG if lo < 1024 else -BIG)
+    ms(V("odd", 0, NS, 2), BIG)
+    ms(V("odd", 1, NS, 2), 0.0)
     ts(col("ci", 1), col("ci", 0), 15, A.bitwise_and)
+    ts(col("ci", 2), col("ci", 0), 1, A.bitwise_and)
     cp(O_U, V("ci", 8, 16))
-    cp(PM, col("ci", 1))
+    cp(V("cf", 0, 2), V("ci", 1, 3))
     ts(V("oh", 0, NS), V("j16", 0, NS), PM, A.is_equal)
     ts(V("oh", NS, C), V("j16", NS, C), PM, A.is_equal)
-    act(V("keep", 0, C), V("j16", 0, C), AF.Sign)
+    act(V("keep", 0, NS), V("j16", 0, NS), AF.Sign)
     act(V("keepb", 0, C), V("j16", 0, C), AF.Sign)
     ts(V("ez", 3, 515, 4), V("idn", 0, 128), 0.0, A.is_equal)
-    act(col("mk", 0), col("oh", 0), AF.Copy, scale=-BIG)
-    act(col("mk", 4 * NS - 1), col("oh", 15), AF.Copy, scale=-BIG)
+    act(col("mk", 2 * NS - 1), col("oh", 15), AF.Copy, scale=-BIG)
+    fill(col("mk", 4 * NS - 1), 0)
     quant(V("qu", 0, 128), V("su", 0, 128), V("ut", 0, 512))
-    op("v", lambda: g.vector.tensor_copy(T.qur[:].bitcast(dt.uint32), T.qu[:].bitcast(dt.uint32).indirect(O_U[0])), [V("qur", 0, 128)], [V("qu", 0, 128), O_U], 250)
+    op("v", lambda: g.vector.tensor_copy(T.qur[:].bitcast(dt.uint32), T.qu[:].bitcast(dt.uint32).indirect(O_U[0])), [V("qur", 0, 128)], [V("qu", 0, 128), O_U], 260)
     act(V("sur", 0, 128), IX(V("su", 0, 128), O_U), AF.Copy)
     for b in range(4):
         quant(V("qe", 128 * b, 128 * b + 128), V("se", 128 * b, 128 * b + 128), V("ez", 3 - b, 515 - b))
-    act(V("utab", 0, 2 * C), V("uraw", 0, 2 * C), AF.Copy, scale=KS)
+    fill(V("tt", NS, 4 * TS, TS), 0)
+    fill(V("tq", NS, 4 * TQ, TQ), 0)
+    lin(V("utab", 0, C), IO(0, C), -2048 * KS, 392 * 2048 * KS)
     lin(CW, IO(0, NS, 16), 1.0, PM)
-    lin(PK0, CW, 2.0, 1.0)
-    act(V("cf", 28, 40), CW, AF.Copy, scale=2.0)
-    lin(V("cf", 40, 52), CW, 2.0, 1.0)
-    lin(J192, JW, 1.0, float(NS))
-    lin(JT, JW, 2.0, -float(K))
-    lin(KH, V("cf", 4, 10), 1.0, 0.5)
-    lin(KT, V("cf", 4, 10), 2.0, -float(K))
-    lin(CN, CW, -1.0 / 256, -1.0 / 256)
-    lin(CK, CW, 1.0, -NS - 1.0)
-    act(V("c2t", 0, NS), IO(1, C, 2), AF.Copy, scale=KS)
+    lin(V("cf", 120, 132), IO(0, NS, 16), 1.0, PM)
+    lin(V("cf", 132, 144), CW, 2.0, 1.0)
+    lin(V("cf", 144, 156), CW, 4.0, 0.0)
+    lin(KH, KW, 1.0 / 256, 0.5 / 256)
+    lin(KN, KW, -1.0 / 256, 0.0)
+    lin(KC, KW, 2.0, -float(K))
+    fill(V("three", 0, NS), 3)
+    lin(UC, CW, -1.0 / 256, 1.0)
+    lin(UC1, CW, -1.0 / 256, 255.0 / 256)
     ts(O_LR, IO(0, M), 224.0, A.mult, PM, A.add)
     cp(O_M, IO(0, M))
     ts(V("co", 32, 38), IO(0, 6), 224.0, A.mult, PM, A.add)
-    iota(V("cf", 148, 154), [[-208, 6]], 208 * 5 + NS)
-    ts(V("co", 38, 44), V("cf", 148, 154), PM, A.add)
+    iota(V("cf", 4, 10), [[-208, 6]], 208 * 5 + NS)
+    ts(V("co", 38, 44), V("cf", 4, 10), PM, A.add)
     iota(V("a0", 0, NS), [[1, M], [0, 16]], 52)
     tt(V("a0", 0, NS), V("a0", 0, NS), V("oh", 0, NS), A.mult)
     lin(V("al", 0, NS), V("a0", 0, NS), -1.0, 64.0)
     lin(V("ar", 0, NS), V("a0", 0, NS), -1.0, 65.0)
-    lin(V("lr", 0, M * 208, 208), IO(0, M), 0.0, INIT)
-    lin(V("lr", 207, M * 208, 208), IO(0, M), 0.0, INIT - 1.0)
-    lin(col("ssb", C), IO(0, 1), 0.0, BIG)
-    lin(col("ssb", C + 1), IO(0, 1), 0.0, -BIG)
-    fill(col("dd", 0), 0)
-    lin(V("pp", NS, C), IO(0, NS), 0.0, -BIG)
-    lin(col("cx", 0), IO(0, 1), 0.0, 0.5)
-    ts(V("tri", 0, NS), V("j16", 0, NS), PM, A.is_lt)
-    fill(V("kptab", 0, K), 1)
-    fill(V("kptab", K, C), 0)
-    fill(col("cum", 16 + NS), -1)
-    fill(col("cum", 17 + NS), 0)
-    fill(col("r2", NS), 0)
-    iota(V("z0", 0, K), [[2, K // 2], [2, 2]], 2 * NS)
+    fill(V("lr", 208, M * 208, 208), 0)
+    fill(V("lr", 207, (M - 1) * 208, 208), 0)
+    lin(V("noh", 0, NS), V("oh", 0, NS), -1.0, 1.0)
+    lin(V("kptab", 0, K), IO(0, K), 0.0, 1.0 / 256)
+    fill(V("kptab", K, 416), 0)
+    fill(V("cum", 0, 15), 0)
+    lin(col("cum", 15 + NS), IO(0, 1), 0.0, -K / 256.0)
+    fill(V("r5", NS, NS + 16), 0)
+    fill(col("hb", 0), 0)
+    if VW:
+        fill(V("kw", 0, VW * M), 1)
+        fill(V("kw", 0, VW * M, VW), 0)
+    iota(V("z0", 0, K, 2), [[-2, K // 2]], -2 * (NS + 1))
+    iota(V("z0", 1, K, 2), [[2, K // 2]], 2 * (NS + 2))
     tt(V("zm", 0, K), V("z0", 0, K), V("oh", 0, K), A.mult)
-    cp(V("ci", 16, 22), V("cf", 4, 10))
-    ts(V("ci", 24, 30), V("ci", 16, 22), 126, A.bitwise_and)
-    cp(KD, V("ci", 24, 30))
-    fill(V("cf", 82, 85), 0)
-    fill(V("cf", 85, 88), NS)
-    iota(V("cf", 88, 88 + SCH), [[16, SCH]], 0)
-    fill(V("cf", 88 + SCH, 100), 0)
-    fill(V("acc", 16, 32), 0)
-    fill(col("cum", 15), 0)
-    fill(V("kw", 0, VW * M), 1)
-    fill(V("kw", 0, VW * M, VW), 0)
+    lin(W(45, 6), KW, 1.0, 2.0 * NS + 3)
+    lin(W(46, 6), KW, 2.0, 2.0 * NS + 4)
+    act(W(47, 6), W(45, 6), AF.Identity, scale=PAR)
+    tt(DB, W(46, 6), W(47, 6), A.subtract)
+    iota(V("cf", 70, 70 + SCH), [[16, SCH]], -K)
+    fill(V("cf", 70 + SCH, 82), -K)
+    fill(col("acc", 16), 0)
     fill(V("ft", 4 * K, 512), 0)
-    fill(V("zt", 0, 512), 0)
-    for b in range(4):
-        fill(V("tq", TW * b + NS, TW * b + TW), 0)
     lin(V("irow", 0, NS), IO(0, NS), -1.0 / 256, 255.0 / 256)
     fill(V("lp", 0, 6 * 208, 208), 1)
     fill(V("lp", 16, 6 * 208, 224), 1)
-    fill(col("ncs", 15), 1)
-    fill(col("ncs", 15 + NS), 1)
-    iota(V("et", NS, TW), [[1, K]], 0)
-    iota(V("r5", NS, TW), [[1, K]], 1)
+    iota(V("et", NS, TW), [[1, K + 1]], -1)
+    lin(V("sm", 0, K), IO(0, K), -1.0 / 256, -1.0 / 256)
+    tt(V("mj", 0, K), V("sm", 0, K), V("oh", 0, K), A.mult)
+    lin(V("mj", K, C), V("oh", K, C), -1.0, 0.0)
+    fill(V("mj", C, C + 2), 0)
     for t in range(R):
         quant(V("ql%d" % t, K, K + 128), V("sl%d" % t, K, K + 128), V("zt", 0, 512))
     quant(V("qv", 0, 128), V("sv", 0, 128), V("vt", 0, 512))
 
     oh = V("oh", 0, NS)
-    O_K, O_PK, O_QV, O_QT, O_RK, O_L = [V("of", 12 * j, 12 * j + M) for j in range(6)]
-    O_F, O_CE, O_CO, O_CS, O_H, O_KC = V("of", 72, 78), V("of", 80, 92), V("of", 92, 104), V("of", 80, 104), V("of", 104, 128), V("of", 128, 140)
-    O_NP = V("of", 140, 152)
+    O_K, O_QV, O_QT, O_SC, O_RK, O_L = [V("of", 12 * j, 12 * j + M) for j in (0, 2, 3, 4, 5, 6)]
+    O_F, O_CO, O_CE, O_PK, O_Z, O_H = V("of", 84, 90), V("of", 92, 104), V("of", 104, 116), V("of", 116, 128), V("of", 128, 140), V("of", 140, 164)
 
-    def TB(b, lo=0, hi=C, step=1):
-        return V("tt", TS * b + NS + lo, TS * b + NS + hi, step)
+    def TB(b, lo=0, hi=C):
+        return V("tt", TS * b + NS + 1 + lo, TS * b + NS + 1 + hi)
+
+    def TWIN(b):
+        return V("tt", TS * b + NS, TS * b + NS + 1 + C)
+
+    def VV(lo, hi):
+        return V("vs", 2 * lo + 2, 2 * hi + 1, 2)
 
     for t in range(R):
         QX, SX = V("qx%d" % t, 0, C), V("sx%d" % t, 0, C)
-        quant(QX, SX, V("x%d" % t, 0, 4 * C))
-        for b in (0, 1):
-            mm(PS(b, 0, C), V("qur", 0, 128), V("sur", 0, 128), QX, SX)
+        for h, (lo, hi) in enumerate(PIECES[t]):
+            quant(V(QX[1], lo, hi), V(SX[1], lo, hi), V("x%d" % t, 4 * lo, 4 * hi))
+            for b in (h, 2 + h):
+                mm(PS(b, 0, hi - NS * h), V("qur", 0, 128), V("sur", 0, 128), V(QX[1], NS * h, hi), V(SX[1], NS * h, hi))
         for b in range(4):
             mm(PS(4 + b, 0, C), V("qe", 128 * b, 128 * b + 128), V("se", 128 * b, 128 * b + 128), QX, SX)
 
-        OP_, E_, O_, EN_ = ends("wsc", 0), ends("wsc", NS), ends("wsc", 2 * NS), ends("wsc", 3 * NS)
-        THV, THP, BB, AW, PK = W(0), W(1), W(2), W(3), W(4)
-        act(V("ssb", 0, C), PS(1, 0, C), AF.Copy)
-        tt(V("mk", 2 * NS, 3 * NS), PS(0, 1, C, 2), oh, A.mult)
-        tt(V("mk", 3 * NS, 4 * NS - 1), PS(0, 2, C, 2), V("oh", 0, NS - 1), A.mult)
-        scan(V("wsc", 2 * NS, 4 * NS), V("keep", 0, C), V("mk", 2 * NS, 4 * NS), 0.0, A.mult, A.add)
-        tt(V("vv", 0, NS - 1), V("ssb", 1, C - 2, 2), PS(0, 2, C, 2), A.min)
-        tt(THV, O_, EN_, A.min)
+        E_, EN_, O_, ON_ = ends("wsc", 0), ends("wsc", NS), ends("wsc", 2 * NS), ends("wsc", 3 * NS)
+        MX, THP, THN = W(1, 24), W(1), V("w", 28, 40)
+        for h in range(2):
+            c0, n = K * h, K - h
+            act(V("ssb", 4 + 4 * c0, 4 * (c0 + K) + 1, 4), PS(2 + h, 1, NS, 2), AF.Copy)
+            act(V("ssb", 2 + 4 * c0, 4 * (c0 + K), 4), PS(2 + h, 0, NS, 2), AF.Copy)
+            for j, (d, k) in enumerate(((0, K), (2, n), (1, K), (3, n))):
+                tt(V("mk", NS * j + c0, NS * j + c0 + k), PS(h, d, d + 2 * k - 1, 2), V("oh", 0, k), A.mult)
+                scan(V("wsc", NS * j + c0, NS * j + c0 + K), V("keep", 0, K), V("mk", NS * j + c0, NS * j + c0 + K), 0.0, A.mult, A.add)
+            scan(V("vs", 2 * c0 + 1, 2 * (c0 + n) + 1), V("odd", 0, 2 * n), PS(h, 1, 2 * n + 1), 0.0, A.add, A.min)
+            tt(V("pp", c0, c0 + K), V("ssb", 4 + 4 * c0, 4 * (c0 + K) + 1, 4), PS(h, 0, NS, 2), A.max)
+            tt(V("w", 6 * h, 6 * h + 6), ends("wsc", 2 * NS + c0, 6), ends("wsc", NS + c0, 6), A.min)
         for b in range(4):
             act(TB(b), PS(4 + b, 0, C), AF.Copy)
         for m in range(M):
-            act(V("sg", NS * m, NS * m + NS - 1 - VW), V("vv", VW, NS - 1), AF.Sign, bias=col("w", m), scale=-1.0, acc=col("acc", 32 + m))
-            ts(V("fl", VW * m, VW * m + VW), V("vv", 0, VW), col("w", m), A.is_lt)
-        scan(V("fc", 0, VW * M), V("kw", 0, VW * M), V("fl", 0, VW * M), 0.0, A.mult, A.add)
-        tt(V("pp", 0, NS), V("ssb", 1, C, 2), PS(0, 0, C, 2), A.max)
-        tt(V("mk", NS, 2 * NS), PS(0, 0, C, 2), oh, A.mult)
-        tt(V("mk", 1, NS), PS(0, 1, C - 2, 2), V("oh", 1, NS), A.mult)
-        scan(V("wsc", 0, 2 * NS), V("keep", 0, C), V("mk", 0, 2 * NS), 0.0, A.mult, A.add)
-        tt(W(5), O_, EN_, A.is_ge)
-        tt(THP, E_, O_, A.max)
-        tt(AW, E_, O_, A.is_ge)
-        ts(BB, W(5), float(C), A.add, 0.5, A.mult)
-        tt(PK, PK0, AW, A.subtract)
-        cp(O_PK, PK)
-        tt(W(6), OP_, O_, A.is_ge)
-        tt(W(8), EN_, E_, A.is_gt)
-        tt(W(7), W(6), AW, A.is_gt)
-        tt(W(28), W(8), AW, A.mult)
-        NPW = W(12)
-        tt(W(13), OP_, E_, A.is_ge)
-        tt(W(14), W(13), AW, A.mult)
-        tt(W(45), AW, W(5), A.max)
-        tt(W(46), W(45), W(14), A.subtract)
-        ts(NPW, W(46), -1.0, A.mult, 1.0, A.add)
-        ts(W(18), NPW, float(NS), A.mult)
-        tt(W(47), W(18), CW, A.add)
-        cp(O_NP, W(47))
-        act(V("pq", 0, NS), IX(V("pp", 0, C), O_NP), AF.Copy)
-        ts(W(13), NPW, -BIG, A.mult)
-        tt(W(14), W(13), THP, A.add)
-        CS0 = W(9, 24)
-        tt(V("w", 16 * 9, 16 * 9 + 12), CW, W(7), A.subtract)
-        tt(V("w", 16 * 9 + 12, 16 * 9 + 24), CW, W(28), A.add)
-        tt(V("dd", 1, K + 1), V("ssb", 0, K), PS(0, 1, K + 1), A.is_ge)
-        tt(V("npc", 0, K), V("dd", 1, K + 1), V("dd", 0, K), A.is_le)
-        scan(V("cx", 1, K + 1), V("npc", 0, K), V("npc", 0, K), 0.5, A.add, A.max)
-        tt(V("zk", 0, K), V("npc", 0, K), V("zm", 0, K), A.mult)
+            act(V("sg", NS * m, NS * m + NS - 1 - VW), VV(VW, NS - 1), AF.Sign, bias=col("w", m), scale=-1.0, acc=col("acc", 32 + m))
+            if VW:
+                ts(V("fl", VW * m, VW * m + VW), VV(0, VW), col("w", m), A.is_lt)
+        if VW:
+            scan(V("fv", 0, VW * M), V("kw", 0, VW * M), V("fl", 0, VW * M), 0.0, A.mult, A.add)
+            tt(W(33), V("fv", VW - 1, VW * M, VW), V("acc", 32, 32 + M), A.add)
+        tt(MX, ends("wsc", 0, 24), ends("wsc", 2 * NS, 24), A.max)
+        FL = 16 * 34
+        BW, PK1, IL, IR = W(5), V("w", FL + 72, FL + 84), W(7), W(8)
+        tt(V("w", FL + 24, FL + 36), E_, O_, A.is_lt)
+        tt(W(9), EN_, ON_, A.is_ge)
+        tt(BW, O_, EN_, A.is_ge)
+        ts(W(10), W(9), 2.0, A.add)
+        tt(W(11), W(10), BW, A.mult)
+        tt(V("w", FL + 36, FL + 48), W(11), V("w", FL + 24, FL + 36), A.max)
+        tt(V("w", FL, FL + 12), EN_, THP, A.is_gt)
+        tt(V("w", FL + 12, FL + 24), THN, O_, A.is_gt)
+        tt(V("w", FL + 48, FL + 96), V("w", FL, FL + 48), CW4, A.add)
+        cp(V("of", 92, 140), V("w", FL + 48, FL + 96))
+        act(V("rb", 0, NS), IX(IO(0, 2 * C), O_Z), AF.Identity, scale=KS, bias=4 * KS)
+        lin(IL, PK1, 2 * KS, INIT)
+        lin(IR, PK1, 2 * KS, INIT - 1.0)
+        lin(col("lr", 0), col("w", FL + 72), 2 * KS, INIT)
+        lin(col("lr", M * 208 - 1), col("w", FL + 72 + M - 1), 2 * KS, INIT - 1.0)
+        tt(V("aw", 0, K // 2), PS(0, 0, K, 2), V("ssb", 4, 2 * K + 1, 4), A.is_ge)
+        for e in range(2):
+            tt(V("zk", e, K, 2), V("aw", 0, K // 2), V("zm", e, K, 2), A.mult)
         scan(V("zs", 0, K), V("keep", 0, K), V("zk", 0, K), 0.0, A.mult, A.add)
-        tt(W(29, 6), ends("zs", 0, 6), KD, A.add)
+        D2 = W(17, 6)
+        tt(D2, ends("zs", 0, 6), DB, A.add)
         for m in range(M):
             act(V("sg", NS * m, NS * m + NS), V("pp", 0, NS), AF.Sign, bias=col("w", 16 + m), scale=-1.0)
         for b in range(4):
-            act(V("tt", TS * b, TS * b + NS), IX(TB(b), O_PK), AF.Copy, scale=0.5)
-        tt(W(39), BB, V("fc", VW - 1, VW * M, VW), A.add)
-        tt(W(11), V("acc", 32, 32 + M), W(39), A.add)
-        ts(O_K, W(11), 2.0, A.mult)
-        tt(V("uu", 0, NS), IX(V("utab", 0, 2 * C), O_K), V("c2t", 0, NS), A.add)
+            act(V("tt", TS * b, TS * b + NS), IX(TWIN(b), O_PK), AF.Copy)
+            act(V("tq", TQ * b + NS + 1, TQ * b + TW), TB(b, 0, K), AF.Copy, scale=2.0)
+        ts(O_K, W(33) if VW else V("acc", 32, 32 + M), float(NS), A.add)
+        tt(V("uu", 0, NS), IX(V("utab", 0, C), O_K), V("rb", 0, NS), A.add)
         lin(V("um", 0, NS), V("uu", 0, NS), 1.0, -1.0)
         for m in range(M):
             n = 16 * m + 15
-            scan(V("lr", 208 * m + 1, 208 * m + 1 + n), V("sg", NS * m, NS * m + n), V("uu", 0, n), INIT, A.min, A.max)
-            scan(RV("lr", 208 * m + 16 + 16 * m, 208 * m + 207), RV("sg", NS * m + 16 * m + 1, NS * m + NS), RV("um", 16 * m, NS - 1), INIT - 1.0, A.min, A.max)
+            scan(V("lr", 208 * m + 1, 208 * m + 1 + n), V("sg", NS * m, NS * m + n), V("uu", 0, n), col("w", 16 * 7 + m), A.min, A.max)
+            scan(RV("lr", 208 * m + 16 + 16 * m, 208 * m + 207), RV("sg", NS * m + 16 * m + 1, NS * m + NS), RV("um", 16 * m, NS - 1), col("w", 16 * 8 + m), A.min, A.max)
         tt(V("lm", 0, NS), IX(V("lr", 0, M * 208), O_LR), V("al", 0, NS), A.add)
         tt(V("rm", 0, NS), IX(V("lr", 16, M * 208), O_LR), V("ar", 0, NS), A.add)
         scan(V("ex", 0, NS), V("lm", 0, NS), V("rm", 0, NS), 100.0, A.min, A.min)
-        QI = V("wi", 16, 16 + M)
-        ts(V("wi", 0, M), ends("ex", 0), 1.0 / KS, A.mult)
-        ts(QI, V("wi", 0, M), 511, A.bitwise_and)
-        cp(O_QV, QI)
-        SS = V("ssb", 0, C + 2)
+        WI, A1, A2, A3 = V("wi", 0, M), V("wi", 16, 16 + M), V("wi", 32, 32 + M), V("wi", 32 + M, 32 + 2 * M)
+        ts(WI, ends("ex", 0), 1.0 / KS, A.mult)
+        ts(A1, WI, 2047, A.bitwise_and)
+        cp(O_QV, A1)
+        ts(A2, WI, 1023, A.bitwise_and, 1, A.logical_shift_right)
+        ts(A3, WI, 2047, A.bitwise_and, 2, A.logical_shift_right)
+        cp(V("of", 36, 60), V("wi", 32, 32 + 2 * M))
+        SS = V("ssb", 0, SW)
         tt(V("sm", 0, NS), IX(SS, O_QV), oh, A.mult)
-        tt(V("ngp", 0, NS), IX(SS, O_QV), V("pq", 0, NS), A.subtract)
+        tt(V("ngp", 0, NS), IX(SS, O_QV), V("pp", 0, NS), A.subtract)
         scan(V("sc", 0, NS), V("keep", 0, NS), V("sm", 0, NS), 0.0, A.mult, A.add)
         TH = V("thp", 0, M)
-        tt(TH, ends("sc", 0), W(14), A.subtract)
-        tt(W(16), QI, PK, A.subtract)
-        ts(W(15), QI, float(C), A.is_lt)
-        tt(W(30), W(16), W(15), A.mult)
-        tt(W(17), W(30), PK, A.add)
-        cp(O_QT, W(17))
-        NPA, XA, NN = col("acc", 48), col("acc", 49), col("acc", 50)
-        act(V("j3", 0, NS), V("ngp", 0, NS), AF.Sign, bias=-BIG / 4, acc=NPA)
-        act(V("j3", NS, NS + K), V("cx", 0, K), AF.Sign, bias=NPA, scale=-2.0, acc=XA)
-        act(NN, NPA, AF.Relu, scale=0.5)
+        tt(TH, ends("sc", 0), THP, A.subtract)
         for m in range(SCH):
             s2 = NS * m
             act(V("s2", s2, s2 + NS), V("ngp", 0, NS), AF.Sign, bias=col("thp", m), scale=-1.0)
             act(V("j2", s2 + 16 * m, s2 + NS), V("s2", s2 + 16 * m, s2 + NS), AF.Relu, acc=col("acc", m))
             if m:
                 act(V("j2", s2, s2 + 16 * m), V("s2", s2, s2 + 16 * m), AF.Relu, scale=-1.0, acc=col("acc", 16 + m))
+        tt(V("eq", 0, NS), IX(TH, O_M), V("ngp", 0, NS), A.is_equal)
+        scan(RV("ec", 0, NS), RV("noh", 0, NS), RV("eq", 0, NS), 0.0, A.mult, A.add)
+        act(W(19), TH, AF.Relu, scale=200.0 / BIG)
+        tt(W(20), W(19), BASE, A.add)
+        tt(W(21), W(20), V("ec", 0, NS, 16), A.add)
+        RK = V("fc", K - 1, M * K, K)
         for m in range(SCH, M):
             f0 = NS * (m - SCH)
             ts(V("fl", f0, f0 + 16 * m), V("ngp", 0, 16 * m), col("thp", m), A.is_le)
             ts(V("fl", f0 + 16 * m, f0 + NS), V("ngp", 16 * m, NS), col("thp", m), A.is_lt)
-            f = V("fl", f0, f0 + NS)
-            scan(V("fc", f0, f0 + NS), f, f, 0.0, A.add, A.max)
-        tt(V("eq", 0, NS), IX(TH, O_M), V("ngp", 0, NS), A.is_equal)
-        tt(V("eb", 0, NS), V("eq", 0, NS), V("tri", 0, NS), A.mult)
-        scan(V("ec", 0, NS), V("keepb", 0, NS), V("eb", 0, NS), 0.0, A.mult, A.add)
-        tt(W(31), W(18), BASE, A.add)
-        tt(W(32), W(31), ends("ec", 0), A.add)
-        tt(V("w", 16 * 33 + SCH, 16 * 33 + M), V("w", 16 * 32 + SCH, 16 * 32 + M), V("fc", NS - 1, (M - SCH) * NS, NS), A.add)
+            scan(V("fc", K * m, K * m + K), V("fl", f0, f0 + K), V("fl", f0 + K, f0 + NS), col("w", 16 * 21 + m), A.add, A.add)
+        tt(W(23, SCH), W(21, SCH), V("acc", 16, 16 + SCH), A.subtract)
+        tt(V("fc", K - 1, SCH * K, K), W(23, SCH), V("acc", 0, SCH), A.add)
+        ts(O_RK, RK, K - 1.0, A.add)
+        cp(V("kp", 0, NS), IX(V("kptab", 0, 416), O_RK))
+        scan(RV("cum", 15, 15 + NS), RV("kp", 0, NS), RV("kp", 0, NS), -K / 256.0, A.add, A.min)
         for b in range(4):
-            act(V("tq", TW * b, TW * b + NS), IX(TB(b), O_QT), AF.Copy, scale=0.5)
-        tt(W(19, SCH), W(32, SCH), V("acc", 16, 16 + SCH), A.subtract)
-        tt(W(33, SCH), W(19, SCH), V("acc", 0, SCH), A.add)
-        cp(O_RK, W(33))
-        KP, CUM = V("kp", 0, NS), V("cum", 16, 16 + NS)
-        cp(KP, IX(V("kptab", 0, C), O_RK))
-        scan(CUM, KP, KP, NN, A.add, A.max)
-        ts(W(34, 6), KT, XA, A.is_lt)
-        tt(W(35, 6), W(34, 6), W(29, 6), A.mult)
-        for m in range(3, 6):
-            act(V("j3", NS * (m - 1), NS * m), CUM, AF.Sign, bias=col("cf", 76 + m), scale=-1.0, acc=col("acc", 52 + m))
-        for m in range(3):
+            for h in range(2):
+                tt(V("tq", TQ * b + K * h, TQ * b + K * h + K), IX(TWIN(b), V("of", 36 + 6 * h, 42 + 6 * h)), V("tt", TS * b + K * h, TS * b + K * h + K), A.add)
+        act(V("pk", 0, NS), V("ngp", 0, NS), AF.Sign, bias=-BIG / 2)
+        scan(RV("yy", 0, NS), RV("pk", 0, NS), RV("three", 0, NS), 2.0 * K - 4.0 * (NS - 1), A.add, A.add)
+        act(V("j3", 0, K // 2), V("yy", 0, K // 2), AF.Sign, bias=-5.0, acc=col("acc", 48))
+        act(V("j3", K // 2, K), V("yy", 1, K // 2 + 1), AF.Sign, bias=-3.0, acc=col("acc", 49))
+        ts(W(24, 6), KC, col("acc", 48), A.subtract, col("acc", 49), A.is_lt)
+        tt(W(25, 6), W(24, 6), D2, A.mult)
+        lin(W(26, 6), W(25, 6), 1.0, -float(NS))
+        for m in range(IVV, 6):
+            act(V("j3", NS * m, NS * m + NS), V("cum", 15, 15 + NS), AF.Sign, bias=col("cf", 40 + m), acc=col("iv", K * m + K - 1))
+        for m in range(IVV):
             n = 16 * m + 112
-            ts(V("tf", NS * m, NS * m + n), V("cum", 16, 16 + n), col("cf", 4 + m), A.is_le, 2.0, A.mult)
-            red(col("acc", 52 + m), V("tf", NS * m, NS * m + n))
-        tt(W(20, 6), W(35, 6), AT, A.subtract)
-        tt(W(36, 6), W(20, 6), V("acc", 52, 58), A.max)
-        ts(V("of", 72, 75), W(36, 3), 0.5, A.mult)
-        ts(V("of", 75, 78), V("w", 16 * 36 + 3, 16 * 36 + 6), float(NS), A.add, 0.5, A.mult)
+            ts(V("tf", NS * m, NS * m + n), V("cum", 15, 15 + n), col("cf", 46 + m), A.is_ge, 2.0, A.mult)
+            scan(V("iv", K * m + K - n // 2, K * m + K), V("tf", NS * m, NS * m + n // 2), V("tf", NS * m + n // 2, NS * m + n), -float(NS), A.add, A.add)
+        tt(W(27, 6), W(26, 6), V("iv", K - 1, 6 * K, K), A.max)
+        ts(O_F, W(27, 6), NS - 2.0, A.add, 0.5, A.mult)
         for b in range(4):
-            act(V("gq", K * b, K * b + K), IX(V("tq", TW * b, TW * b + TW), O_F), AF.Copy)
-            tt(V("ft", b, 4 * K, 4), IX(V("tt", TS * b, TS * b + TW), O_F), V("gq", K * b, K * b + K), A.add)
+            if b < FS:
+                act(V("ft", b, 4 * K, 4), IX(V("tq", TQ * b, TQ * b + TW), O_F), AF.Copy, scale=0.5)
+            else:
+                ts(V("ft", b, 4 * K, 4), IX(V("tq", TQ * b, TQ * b + TW), O_F), 0.5, A.mult)
         qf, sf, ql, sl = ["%s%d" % (n, t) for n in ("qf", "sf", "ql", "sl")]
         quant(V(qf, 0, 128), V(sf, 0, 128), V("ft", 0, 512))
         dst = T.cores[rank ^ (1 << t)]
@@ -398,78 +402,65 @@ def rank_program(g, core, T, topo):
         ne = len(topo.engines(core, dst))
         arr = T.sem["ar%d" % t]
         op("g", lambda qf=qf, ql=ql, arr=arr, pid=pid, rid=rid, mask=mask: g.remote_dma(
-            T[ql][:, 0:K].bitcast(u8), T[qf][:, 0:K].bitcast(u8), arr, T.sem.sent, pid, rid, mask), [], [V(qf, 0, K)], 500, dma=("", 0), lat=4000)
+            T[ql][:, 0:K].bitcast(u8), T[qf][:, 0:K].bitcast(u8), arr, T.sem.sent, pid, rid, mask), [], [V(qf, 0, K)], 500, dma=("", 0), lat=3000)
         op("g", lambda sf=sf, sl=sl, arr=arr, pid=pid, rid=rid, mask=mask: g.remote_dma(
-            T[sl][:, 0:K], T[sf][:, 0:K], arr, T.sem.sent, pid, rid, mask), [], [V(sf, 0, K)], 500, dma=("", 0), lat=4000)
-        op("arrive", None, [V(ql, 0, K), V(sl, 0, K)], [V(qf, 0, K)], 0, dma=("ar%d" % t, 2 * ne), lat=6500)
+            T[sl][:, 0:K], T[sf][:, 0:K], arr, T.sem.sent, pid, rid, mask), [], [V(sf, 0, K)], 500, dma=("", 0), lat=3000)
+        op("arrive", None, [V(ql, 0, K), V(sl, 0, K)], [V(qf, 0, K)], 0, dma=("ar%d" % t, 2 * ne), lat=3500)
 
         for m in range(M):
             n = 16 * m + 15
             b0 = 208 * m if m < 6 else 208 * (11 - m) + 16 * (12 - m)
             scan(V("lp", b0 + 1, b0 + 1 + n), V("sg", NS * m, NS * m + n), V("irow", 0, n), 1.0, A.min, A.max)
-        tt(V("lb", 0, NS), IX(V("lp", 0, 6 * 208), O_LP), oh, A.mult)
+        for h in range(2):
+            tt(V("lb", K * h, K * h + K), IX(V("lp", 0, 6 * 208), V("co", 32 + 6 * h, 38 + 6 * h)), V("oh", 0, K), A.mult)
         scan(V("lc", 0, NS), V("keepb", 0, NS), V("lb", 0, NS), 0.0, A.mult, A.add)
-        tt(W(21), QI, PK, A.is_ge)
-        tt(W(22), W(21), CN, A.mult)
-        lin(W(23), W(22), 1.0, 1.0)
-        ts(W(40), W(33), float(K), A.is_lt)
-        tt(W(41), W(40), W(15), A.mult)
-        lin(W(42), W(41), 63.0 / 256 - 1.0, 1.0)
-        tt(W(43), W(42), W(23), A.min)
-        tt(W(37), W(43), ends("lc", 0), A.min)
-        ts(O_L, W(37), -256.0, A.mult, 255.0, A.add)
-        tt(W(44), W(40), CK, A.mult)
-        ts(O_KC, W(44), NS + 1.0, A.add)
-        lin(V("nc", 0, C), IO(0, C), 0.0, 1.0)
+        tt(W(28), PK1, A2, A.subtract)
+        tt(W(29), W(28), UC, A.max)
+        tt(W(30), W(29), ends("lc", 0), A.min)
+        tt(W(31), RK, UC1, A.max)
+        tt(W(32), W(31), W(30), A.min)
+        ts(O_L, W(32), -256.0, A.mult, 271.0, A.add)
+        CUM = V("cum", 0, 16 + NS)
+        fill(V("nc", 0, 464), 0)
         act(V("cpv", 0, NS), V("cum", 15, 15 + NS), AF.Copy)
-        tt(V("na", 0, NS), IX(V("cum", 16, 18 + NS), O_L), V("cpv", 0, NS), A.is_ge)
-        cp(IX(V("nc", 0, C), O_QT), V("na", 0, NS))
-        tt(V("ncs", 16, 15 + NS), V("nc", 1, C - 2, 2), V("nc", 2, C, 2), A.min)
-        act(V("r0", 0, NS), IX(V("cum", 16, 18 + NS), O_KC), AF.Copy)
-        scan(V("r1", 0, NS), V("ncs", 15, 15 + NS), V("r0", 0, NS), 0.0, A.mult, A.max)
-        scan(RV("r2", 0, NS), RV("ncs", 16, 16 + NS), RV("r1", 0, NS), 0.0, A.mult, A.max)
-        tt(V("r3", 0, NS), IX(V("r2", 0, NS + 1), O_L), V("r1", 0, NS), A.max)
-        scan(V("r4", 0, NS), V("ncs", 15, 15 + NS), V("r3", 0, NS), 0.0, A.mult, A.max)
-        scan(RV("r5", 0, NS), RV("ncs", 16, 16 + NS), RV("r4", 0, NS), 0.0, A.mult, A.max)
-        ts(W(24, 24), JT, XA, A.is_lt)
-        tt(W(26, 24), W(24, 24), J192, A.mult)
-        tt(W(38, 24), W(26, 24), CS0, A.max)
-        cp(O_CS, W(38, 24))
-        tt(V("hb", 0, C, 2), IX(V("r5", 0, TW), O_CE), V("oh", 0, C, 2), A.mult)
-        tt(V("hb", 1, C, 2), IX(V("r5", 0, TW), O_CO), V("oh", 1, C, 2), A.mult)
+        tt(V("an", 0, NS), IX(CUM, O_L), V("cpv", 0, NS), A.not_equal)
+        cp(IX(V("nc", 0, 464), O_SC), V("an", 0, NS))
+        tt(V("r0", 0, NS), IX(CUM, O_L), V("an", 0, NS), A.mult)
+        scan(V("r4", 0, NS), V("nc", 0, NS), V("r0", 0, NS), 0.0, A.add, A.min)
+        scan(RV("r5", 0, NS), RV("nc", 1, NS + 1), RV("r4", 0, NS), 0.0, A.add, A.min)
+        tt(V("hb", 1, C, 2), IX(V("r5", 0, NS + 16), O_CO), V("mj", 1, C, 2), A.max)
+        tt(V("hb", 2, C + 2, 2), IX(V("r5", 0, NS + 16), O_CE), V("mj", 2, C + 2, 2), A.max)
         scan(V("hc", 0, C), V("keepb", 0, C), V("hb", 0, C), 0.0, A.mult, A.add)
-        ts(O_H, ends("hc", 0, 2 * M), -1.0, A.add)
+        ts(O_H, ends("hc", 0, 2 * M), -256.0, A.mult, -1.0, A.add)
         if t == R - 1:
-            act(V("et", 0, NS), IX(IO(0, C), O_PK), AF.Copy)
+            act(V("et", 0, NS), IX(IO(0, 2 * C), O_PK), AF.Identity, bias=-1.0)
             act(V("er", 0, K), IX(V("et", 0, TW), O_F), AF.Copy)
 
         XN = "x%d" % (t + 1)
         for b in range(4):
             mm(PS(b, 0, 128), V("qw", 128 * b, 128 * b + 128), V("sw", 128 * b, 128 * b + 128), V(ql, 0, 128), V(sl, 0, 128))
-            if b < 2:
+            if b < HTV:
                 ts(V("ht", K * b, K * b + K), PS(b, 0, K), 0.0, A.max, 0.03125, A.mult)
             else:
                 act(V("ht", K * b, K * b + K), PS(b, 0, K), AF.Relu, scale=0.03125)
-        n = NS if t == R - 1 else C
-        for lo in range(0, C, n):
-            o_h = V("of", 104 + lo // 16, 104 + (lo + n) // 16)
-            for b in (2, 3):
-                act(V("hg", C * (b - 2) + lo, C * (b - 2) + lo + n), IX(V("ht", K * b, K * b + K), o_h), AF.Copy)
-            for b in (0, 1):
-                tt(V(XN, 4 * lo + b, 4 * (lo + n), 4), IX(V("ht", K * b, K * b + K), o_h), TB(b, lo, lo + n), A.add)
-            for b in (2, 3):
-                tt(V(XN, 4 * lo + b, 4 * (lo + n), 4), V("hg", C * (b - 2) + lo, C * (b - 2) + lo + n), PS(4 + b, lo, lo + n), A.add)
+        for h, (lo, hi) in enumerate(PIECES[t + 1]):
+            o_h = V("of", 140 + lo // 16, 140 + hi // 16)
+            for b in range(4):
+                if b < 4 - HS[h]:
+                    tt(V(XN, 4 * lo + b, 4 * hi, 4), IX(V("ht", K * b, K * b + K), o_h), TB(b, lo, hi), A.add)
+                else:
+                    act(V("hg", C * b + lo, C * b + hi), IX(V("ht", K * b, K * b + K), o_h), AF.Copy)
+                    tt(V(XN, 4 * lo + b, 4 * hi, 4), V("hg", C * b + lo, C * b + hi), PS(4 + b, lo, hi), A.add)
 
     act(V("olr", 0, C), IX(V("er", 0, K), O_H), AF.Copy)
     for k in range(8):
         dma("y", "out", T.ol[k:k + 1, :], T.olr[16 * k:16 * k + 1, :], [], [V("olr", 0, C)])
     QX, SX = V("qx%d" % R, 0, C), V("sx%d" % R, 0, C)
-    for h in range(2):
-        lo, hi = NS * h, NS * h + NS
+    for h, (lo, hi) in enumerate(PIECES[R]):
         quant(V(QX[1], lo, hi), V(SX[1], lo, hi), V("x%d" % R, 4 * lo, 4 * hi))
-        mm(PS(h, 0, NS), V("qv", 0, 128), V("sv", 0, 128), V(QX[1], lo, hi), V(SX[1], lo, hi))
+        mm(PS(h, 0, hi - lo), V("qv", 0, 128), V("sv", 0, 128), V(QX[1], lo, hi), V(SX[1], lo, hi))
         dma("y", "out", T.oc[:, 4 * lo:4 * hi], V(QX[1], lo, hi)[0].bitcast(u8), [], [V(QX[1], lo, hi)])
-        act(V("ysb", lo, hi), PS(h, 0, NS), AF.Copy)
+        act(V("ysb", lo, hi), PS(h, 0, hi - lo), AF.Copy)
         dma("s", "out", T.y[:, lo:hi], T.ysb[:, lo:hi], [], [V("ysb", lo, hi)])
     for k in range(4):
         dma("y", "out", T.osc[4 * k:4 * k + 4, :], T[SX[1]][32 * k:32 * k + 4, :], [], [SX])
@@ -512,15 +503,32 @@ def rank_program(g, core, T, topo):
 
     def span_of(order):
         s = 0.0
-        for wake, far in CASES:
+        for f, wake, far in CASES:
             free, end = {}, [0.0] * n
             for i in order:
-                q, lat = ops[i][0], (far if ops[i][0] == "arrive" else ops[i][6])
-                t0 = max([free.get(q, 0.0)] + [end[j] + wake for j in deps[i]])
-                free[q] = t0 + ops[i][5]
-                end[i] = free[q] + lat
+                q, t0 = ops[i][0], -wake
+                for j in deps[i]:
+                    if end[j] > t0:
+                        t0 = end[j]
+                free[q] = max(free.get(q, 0.0), t0 + wake) + f * ops[i][5]
+                end[i] = free[q] + (far if q == "arrive" else ops[i][6])
             s += max(end)
         return s
+
+    def chain(order, case):
+        f, wake, far = case
+        free, end, prev = {}, [0.0] * n, [None] * n
+        for i in order:
+            q = ops[i][0]
+            t0, j, near = max([free.get(q, (0.0, -1, True))] + [(end[j] + wake, j, False) for j in deps[i]])
+            free[q] = (t0 + f * ops[i][5], i, True)
+            end[i], prev[i] = free[q][0] + (far if q == "arrive" else ops[i][6]), (j, near)
+        i, pairs = max(range(n), key=lambda i: end[i]), []
+        while prev[i][0] >= 0:
+            if prev[i][1]:
+                pairs.append((prev[i][0], i))
+            i = prev[i][0]
+        return pairs
 
     if not ORDER:
         seed = [12345]
@@ -529,17 +537,46 @@ def rank_program(g, core, T, topo):
             seed[0] = (seed[0] * 1103515245 + 12345) % 2147483648
             return seed[0] / 2147483648.0
 
-        prio = [float(i) for i in range(n)]
+        prio, rank_in = [float(i) for i in range(n)], [0] * n
         for k in range(TURNS):
-            wake, slack = 80 + 150 * uni(), 200 * uni() ** 2
-            if ORDER and k % 4:
-                back = [x + 2 * NOISE * (1 + k % 3) * (uni() + uni() + uni() - 1.5) for x in ORDER[2]]
+            wake, slack = 150 + 200 * uni(), 200 * uni() ** 2
+            if ORDER and (k > 40 or k % 4):
+                wake, slack = ORDER[3:] if k % 8 else (wake, slack)
+                a, w = n * uni(), 10 + 80 * uni()
+                back = [x + (NOISE * (1 + k % 5) * (uni() - 0.5) if abs(p - a) < w else 0.0) for x, p in zip(ORDER[2], rank_in)]
             else:
                 back = schedule(users, deps, prio, True, wake, slack)[1]
             order, prio = schedule(deps, users, back, False, wake, slack)
             span = span_of(order)
-            if not ORDER or span < ORDER[0]:
-                ORDER[:] = [span, order, back]
+            if not ORDER or span <= ORDER[0]:
+                ORDER[:] = [span, order, back, wake, slack]
+                for p, i in enumerate(order):
+                    rank_in[i] = p
+        span, order = ORDER[:2]
+        best = (span, order)
+        for k in range(MOVES):
+            pairs = chain(order, CASES[k % len(CASES)])
+            j, i = pairs[int(uni() * len(pairs))]
+            at = {x: p for p, x in enumerate(order)}
+            new = list(order)
+            if uni() < 0.5:
+                lo = max([at[x] for x in deps[i]] + [-1]) + 1
+                if lo > at[j]:
+                    continue
+                new.remove(i)
+                new.insert(at[j] - int((at[j] - lo) * uni() ** 4), i)
+            else:
+                hi = min([at[x] for x in users[j]] + [n])
+                if hi <= at[i]:
+                    continue
+                new.insert(at[i] + 1 + int((hi - at[i] - 1) * uni() ** 2), j)
+                del new[at[j]]
+            s = span_of(new)
+            if s <= span + HEAT * (1 - k / MOVES) * uni() ** 2:
+                span, order = s, new
+                if s < best[0]:
+                    best = (s, new)
+        ORDER[:2] = best
     order = ORDER[1]
     place = {i: k for k, i in enumerate(order)}
     waits = {}

@@ -5,21 +5,22 @@ C, K, R = 384, 96, 2
 NS = C // 2
 M = NS // 16
 BIG = 1.0e29
-KS = 2.0 ** -20
-INIT = (500 * 2048 + 1024) * KS
+KS = 2.0 ** -19
+INIT = (500 * 1024 + NS) * KS
+A0 = 6
 SCH = 6
-VW = 0
-IVV = 3
+IVV = 4
 HTV = 2
 FS = 2
-HS = (2, 2)
+HS = (2, 3)
 TW = NS + K + 1
 TQ = NS + K + 8
 TS = NS + C + 8
-SW = 1024 + 2 * C + 8
-PIECES = (((0, 224), (224, C)), ((0, 224), (224, C)), ((0, 224), (224, C)))
-TURNS, NOISE, MOVES, HEAT = 300, 200.0, 6000, 150.0
-CASES = ((0.83, 200.0, 3500.0), (0.9, 250.0, 3000.0), (1.1, 150.0, 4500.0))
+SW = 2 * C + 8
+QW = NS + C + 16
+PIECES = (((0, 224), (224, C)), ((0, 224), (224, C)), ((0, 256), (256, C)))
+TURNS, NOISE, MOVES, HEAT = 300, 200.0, 30000, 300.0
+CASES = ((0.83, 200.0, 1800.0, 0.0), (0.9, 250.0, 2000.0, -1.0), (1.0, 130.0, 2000.0, 0.5), (1.15, 200.0, 2300.0, 1.0))
 ORDER = []
 
 X4, U8, F32, BF, I32, U16 = "float8_e4m3fn_x4", "uint8", "float32", "bfloat16", "int32", "uint16"
@@ -32,13 +33,13 @@ for _d, _l in [
     (I32, [("ci", 64), ("wi", 64)]),
     (U16, [("co", 64), ("of", 176)]),
     (BF, [("x0", 4 * C), ("x1", 4 * C), ("x2", 4 * C), ("ut", 512), ("vt", 512), ("ez", 516), ("zt", 512), ("ft", 512), ("keepb", C), ("kptab", 416),
-          ("irow", NS), ("kw", VW * M + 2), ("fv", VW * M + 2), ("sg", M * NS), ("fl", M * NS), ("fc", M * K), ("pk", NS), ("three", NS), ("yy", NS),
+          ("irow", NS), ("sg", M * NS), ("sa", M * K), ("fl", M * NS), ("fc", M * K), ("pk", NS), ("three", NS), ("yy", NS),
           ("s2", SCH * NS), ("j2", SCH * NS), ("j3", 6 * NS), ("eq", NS), ("ec", NS), ("noh", NS), ("kp", NS), ("cum", 16 + NS), ("tf", 6 * NS),
-          ("lp", 6 * 208), ("lb", NS), ("lc", NS), ("an", NS), ("cpv", NS), ("nc", 464), ("r0", NS), ("r4", NS), ("r5", NS + 16), ("hb", C + 2), ("hc", C)]),
-    (F32, [("cf", 192), ("j16", C), ("oh", C), ("keep", NS), ("utab", C), ("rb", NS), ("iot", 2 * C), ("al", NS), ("odd", NS), ("vs", C),
-           ("ar", NS), ("a0", NS), ("zm", K), ("z0", K), ("idn", 128), ("pp", NS), ("mk", 4 * NS), ("wsc", 4 * NS), ("ssb", SW),
-           ("w", 768), ("thp", 16), ("acc", 64), ("iv", 6 * K), ("uu", NS), ("um", NS), ("lr", M * 208), ("lm", NS), ("rm", NS), ("ex", NS), ("sm", NS),
-           ("sc", NS), ("ngp", NS), ("aw", K // 2), ("zk", K), ("zs", K), ("mj", C + 2), ("tt", 4 * TS), ("tq", 4 * TQ),
+          ("lp", 6 * 208), ("lb", NS), ("lc", NS), ("an", NS), ("cpv", NS), ("nc", QW + 16), ("r0", NS), ("r4", NS), ("r5", NS + 16), ("hb", C + 2), ("hc", C)]),
+    (F32, [("cf", 192), ("j16", NS), ("oh", C), ("keep", NS), ("keep2", C), ("utab", C), ("c2t", NS), ("vq", QW), ("iot", C + 16), ("al", NS), ("ar", NS),
+           ("a0", NS), ("odd", NS), ("vs", C), ("zm", K), ("z0", K), ("z1", K), ("pp", NS), ("mk", 4 * NS), ("wsc", 4 * NS), ("ssb", SW),
+           ("w", 768), ("acc", 64), ("iv", 6 * K), ("uu", NS), ("um", NS), ("lr", M * 208), ("lm", NS), ("rm", NS), ("ex", NS), ("sm", C),
+           ("sc", C), ("ngp", NS), ("aw", K // 2), ("zk", K), ("zs", K), ("mj", C + 2), ("tt", 4 * TS), ("tp", 4 * NS), ("tq", 4 * TQ),
            ("ht", 4 * K), ("hg", 4 * C), ("et", TW), ("er", K), ("olr", C), ("ysb", C)]),
 ]:
     for _n, _w in _l:
@@ -55,7 +56,7 @@ def rank_program(g, core, T, topo):
     if rank is None:
         return
     Q = {"v": g.vector, "s": g.scalar, "t": g.tensor, "g": g, "y": g.sync}
-    ops = []
+    ops, first, slow = [], [], []
 
     def V(n, lo, hi, step=1):
         return (T[n][:, lo:hi:step], n, lo, hi, step)
@@ -74,9 +75,9 @@ def rank_program(g, core, T, topo):
 
     def cost(o, a, rate):
         if len(a) > 5:
-            return 60 + 1.6 * size(a)
+            return (60 + 1.6 * size(a), 0.5 * size(a))
         if len(o) > 5:
-            return 60 + 3.8 * size(o)
+            return (60 + 3.8 * size(o), 2.2 * size(o))
         return max(64, size(a) * rate)
 
     def half(*xs):
@@ -91,7 +92,8 @@ def rank_program(g, core, T, topo):
                     rs.append(a[5][1:5])
         ws = [a[1:5] for a in wr]
         rs += [a[5][1:5] for a in wr if len(a) > 5]
-        ops.append((q, fn, ws, rs, dma, ns, lat))
+        slow.append(ns[1] if isinstance(ns, tuple) else 0.0)
+        ops.append((q, fn, ws, rs, dma, ns[0] if isinstance(ns, tuple) else ns, lat))
 
     def ap(a):
         return a[0] if isinstance(a, tuple) else a
@@ -122,7 +124,7 @@ def rank_program(g, core, T, topo):
             kw["scale"] = ap(scale)
         if acc is not None:
             kw["accum_out"] = acc[0]
-        op("s", lambda: g.scalar.activation(o[0], a[0], f, **kw), [o] + ([acc] if acc else []), [a, bias, scale], cost(o, a, 1) + (24 if acc else 0))
+        op("s", lambda: g.scalar.activation(o[0], a[0], f, **kw), [o] + ([acc] if acc else []), [a, bias, scale], cost(o, a, 1) + 24 if acc else cost(o, a, 1))
 
     def lin(o, a, scale, bias):
         act(o, a, AF.Identity, bias=bias, scale=scale)
@@ -161,57 +163,63 @@ def rank_program(g, core, T, topo):
     dma("y", "du", T.ut[:], T.u[:], [V("ut", 0, 512)], [])
     for h, (lo, hi) in enumerate(PIECES[0]):
         dma("sy"[h], "dx%d" % h, T.x0[:, 4 * lo:4 * hi], T.x[:, 4 * lo:4 * hi], [V("x0", 4 * lo, 4 * hi)], [], 2300 + 300 * h)
+    first.append((0, 2))
     dma("y", "dw", T.qw[:].bitcast(u8), T.wc[:], [V("qw", 0, 512)], [V("x0", 0, 4 * C)])
     dma("y", "dw", T.sw[:], T.ws[:], [V("sw", 0, 512)], [V("x0", 0, 4 * C)])
     dma("y", "dv", T.vt[:], T.v[:], [V("vt", 0, 512)], [V("x0", 0, 4 * C)])
 
-    PM, PAR, CW, CW4, KW = col("cf", 0), col("cf", 1), V("cf", 108, 120), V("cf", 108, 156), V("cf", 108, 114)
-    KH, KN, KC, DB, BASE = V("cf", 40, 46), V("cf", 46, 52), V("cf", 52, 58), V("cf", 64, 70), V("cf", 70, 82)
+    PM, PAR, CW, CW5, KW = col("cf", 0), col("cf", 1), V("cf", 108, 120), V("cf", 108, 168), V("cf", 108, 114)
+    KH, KC, DB, BASE = V("cf", 40, 46), V("cf", 52, 58), V("cf", 64, 70), V("cf", 70, 82)
     UC, UC1 = V("cf", 82, 94), V("cf", 94, 106)
-    O_U, O_LR, O_M, O_LP = V("co", 0, 8), V("co", 8, 20), V("co", 20, 32), V("co", 32, 44)
-    iota(col("ci", 0), [[1, 1]], 0, 1)
+    O_U, O_LR, O_M = V("co", 0, 8), V("co", 8, 20), V("co", 20, 32)
+    iota(col("ci", 3), [[1, 1]], 0, 1)
     iota(V("ci", 8, 16), [[16, 8]], 0)
-    iota(V("j16", 0, C), [[0, 2 * M], [1, 16]], 0)
-    iota(V("idn", 0, 128), [[-1, 128]], 0, 1)
-    iota(IO(0, C), [[1, C]], 0)
-    lin(IO(C, 2 * C), IO(0, C), 1.0, float(C))
+    iota(V("j16", 0, NS), [[0, M], [1, 16]], 0)
+    iota(IO(0, C + 16), [[1, C + 16]], 0)
+    lin(V("vq", NS, QW), IO(0, QW - NS), 0.0, -BIG)
+    lin(V("c2t", 0, NS), IO(0, NS), KS, 0.0)
     ms(V("ez", 0, 516), 0.0)
     ms(V("zt", 0, 512), 0.0)
     for lo in range(0, SW, 512):
-        lin(V("ssb", lo, min(SW, lo + 512)), V("zt", 0, min(SW - lo, 512)), 0.0, BIG if lo < 1024 else -BIG)
+        lin(V("ssb", lo, min(SW, lo + 512)), V("zt", 0, min(SW - lo, 512)), 0.0, BIG)
     ms(V("odd", 0, NS, 2), BIG)
     ms(V("odd", 1, NS, 2), 0.0)
-    ts(col("ci", 1), col("ci", 0), 15, A.bitwise_and)
-    ts(col("ci", 2), col("ci", 0), 1, A.bitwise_and)
+    ts(col("ci", 1), col("ci", 3), 15, A.bitwise_and)
+    ts(col("ci", 2), col("ci", 3), 1, A.bitwise_and)
     cp(O_U, V("ci", 8, 16))
-    cp(V("cf", 0, 2), V("ci", 1, 3))
+    cp(V("cf", 0, 3), V("ci", 1, 4))
     ts(V("oh", 0, NS), V("j16", 0, NS), PM, A.is_equal)
-    ts(V("oh", NS, C), V("j16", NS, C), PM, A.is_equal)
+    act(V("oh", NS, C), V("oh", 0, NS), AF.Copy)
     act(V("keep", 0, NS), V("j16", 0, NS), AF.Sign)
-    act(V("keepb", 0, C), V("j16", 0, C), AF.Sign)
-    ts(V("ez", 3, 515, 4), V("idn", 0, 128), 0.0, A.is_equal)
+    for n, k in (("keepb", 16), ("keep2", 32)):
+        fill(V(n, 0, C), 1)
+        fill(V(n, 0, C, k), 0)
+    ts(V("ez", 3, 515, 4), IO(0, 128), col("cf", 2), A.is_equal)
     act(col("mk", 2 * NS - 1), col("oh", 15), AF.Copy, scale=-BIG)
-    fill(col("mk", 4 * NS - 1), 0)
+    ms(col("mk", 4 * NS - 1), 0.0)
     quant(V("qu", 0, 128), V("su", 0, 128), V("ut", 0, 512))
     op("v", lambda: g.vector.tensor_copy(T.qur[:].bitcast(dt.uint32), T.qu[:].bitcast(dt.uint32).indirect(O_U[0])), [V("qur", 0, 128)], [V("qu", 0, 128), O_U], 260)
     act(V("sur", 0, 128), IX(V("su", 0, 128), O_U), AF.Copy)
     for b in range(4):
         quant(V("qe", 128 * b, 128 * b + 128), V("se", 128 * b, 128 * b + 128), V("ez", 3 - b, 515 - b))
     fill(V("tt", NS, 4 * TS, TS), 0)
+    fill(V("tt", NS + C + 1, 4 * TS, TS), 0)
     fill(V("tq", NS, 4 * TQ, TQ), 0)
-    lin(V("utab", 0, C), IO(0, C), -2048 * KS, 392 * 2048 * KS)
+    lin(V("utab", 0, C), IO(0, C), -1024 * KS, 392 * 1024 * KS)
     lin(CW, IO(0, NS, 16), 1.0, PM)
     lin(V("cf", 120, 132), IO(0, NS, 16), 1.0, PM)
     lin(V("cf", 132, 144), CW, 2.0, 1.0)
-    lin(V("cf", 144, 156), CW, 4.0, 0.0)
-    lin(KH, KW, 1.0 / 256, 0.5 / 256)
-    lin(KN, KW, -1.0 / 256, 0.0)
+    lin(V("cf", 144, 156), CW, 2.0, 2.0)
+    lin(V("cf", 156, 168), CW, 4.0, 4.0)
+    lin(V("cf", 40, 40 + IVV), V("cf", 108, 108 + IVV), -1.0 / 256, 0.0)
+    lin(V("cf", 40 + IVV, 46), V("cf", 108 + IVV, 114), -1.0 / 256, -0.5 / 256)
     lin(KC, KW, 2.0, -float(K))
     fill(V("three", 0, NS), 3)
     lin(UC, CW, -1.0 / 256, 1.0)
     lin(UC1, CW, -1.0 / 256, 255.0 / 256)
     ts(O_LR, IO(0, M), 224.0, A.mult, PM, A.add)
-    cp(O_M, IO(0, M))
+    cp(O_M, IO(31, C, 32))
+    fill(V("sm", 1, C, 2), 0)
     ts(V("co", 32, 38), IO(0, 6), 224.0, A.mult, PM, A.add)
     iota(V("cf", 4, 10), [[-208, 6]], 208 * 5 + NS)
     ts(V("co", 38, 44), V("cf", 4, 10), PM, A.add)
@@ -228,11 +236,8 @@ def rank_program(g, core, T, topo):
     lin(col("cum", 15 + NS), IO(0, 1), 0.0, -K / 256.0)
     fill(V("r5", NS, NS + 16), 0)
     fill(col("hb", 0), 0)
-    if VW:
-        fill(V("kw", 0, VW * M), 1)
-        fill(V("kw", 0, VW * M, VW), 0)
-    iota(V("z0", 0, K, 2), [[-2, K // 2]], -2 * (NS + 1))
-    iota(V("z0", 1, K, 2), [[2, K // 2]], 2 * (NS + 2))
+    lin(V("z0", 0, K, 2), IO(0, K // 2), -2.0, -2.0 * (NS + 1))
+    lin(V("z0", 1, K, 2), IO(0, K // 2), 2.0, 2.0 * (NS + 2))
     tt(V("zm", 0, K), V("z0", 0, K), V("oh", 0, K), A.mult)
     lin(W(45, 6), KW, 1.0, 2.0 * NS + 3)
     lin(W(46, 6), KW, 2.0, 2.0 * NS + 4)
@@ -246,8 +251,8 @@ def rank_program(g, core, T, topo):
     fill(V("lp", 0, 6 * 208, 208), 1)
     fill(V("lp", 16, 6 * 208, 224), 1)
     iota(V("et", NS, TW), [[1, K + 1]], -1)
-    lin(V("sm", 0, K), IO(0, K), -1.0 / 256, -1.0 / 256)
-    tt(V("mj", 0, K), V("sm", 0, K), V("oh", 0, K), A.mult)
+    lin(V("z1", 0, K), IO(0, K), -1.0 / 256, -1.0 / 256)
+    tt(V("mj", 0, K), V("z1", 0, K), V("oh", 0, K), A.mult)
     lin(V("mj", K, C), V("oh", K, C), -1.0, 0.0)
     fill(V("mj", C, C + 2), 0)
     for t in range(R):
@@ -255,17 +260,14 @@ def rank_program(g, core, T, topo):
     quant(V("qv", 0, 128), V("sv", 0, 128), V("vt", 0, 512))
 
     oh = V("oh", 0, NS)
-    O_K, O_QV, O_QT, O_SC, O_RK, O_L = [V("of", 12 * j, 12 * j + M) for j in (0, 2, 3, 4, 5, 6)]
-    O_F, O_CO, O_CE, O_PK, O_Z, O_H = V("of", 84, 90), V("of", 92, 104), V("of", 104, 116), V("of", 116, 128), V("of", 128, 140), V("of", 140, 164)
+    O_QV, O_RK, O_L, O_F, O_H = V("of", 24, 36), V("of", 60, 72), V("of", 72, 84), V("of", 84, 90), V("of", 152, 176)
+    O_CO, O_CE, O_PK, O_VC, O_Z = [V("of", 92 + M * j, 104 + M * j) for j in range(5)]
 
     def TB(b, lo=0, hi=C):
         return V("tt", TS * b + NS + 1 + lo, TS * b + NS + 1 + hi)
 
     def TWIN(b):
-        return V("tt", TS * b + NS, TS * b + NS + 1 + C)
-
-    def VV(lo, hi):
-        return V("vs", 2 * lo + 2, 2 * hi + 1, 2)
+        return V("tt", TS * b + NS, TS * b + NS + 2 + C)
 
     for t in range(R):
         QX, SX = V("qx%d" % t, 0, C), V("sx%d" % t, 0, C)
@@ -277,7 +279,7 @@ def rank_program(g, core, T, topo):
             mm(PS(4 + b, 0, C), V("qe", 128 * b, 128 * b + 128), V("se", 128 * b, 128 * b + 128), QX, SX)
 
         E_, EN_, O_, ON_ = ends("wsc", 0), ends("wsc", NS), ends("wsc", 2 * NS), ends("wsc", 3 * NS)
-        MX, THP, THN = W(1, 24), W(1), V("w", 28, 40)
+        THP, THN = W(1), W(2)
         for h in range(2):
             c0, n = K * h, K - h
             act(V("ssb", 4 + 4 * c0, 4 * (c0 + K) + 1, 4), PS(2 + h, 1, NS, 2), AF.Copy)
@@ -291,30 +293,27 @@ def rank_program(g, core, T, topo):
         for b in range(4):
             act(TB(b), PS(4 + b, 0, C), AF.Copy)
         for m in range(M):
-            act(V("sg", NS * m, NS * m + NS - 1 - VW), VV(VW, NS - 1), AF.Sign, bias=col("w", m), scale=-1.0, acc=col("acc", 32 + m))
-            if VW:
-                ts(V("fl", VW * m, VW * m + VW), VV(0, VW), col("w", m), A.is_lt)
-        if VW:
-            scan(V("fv", 0, VW * M), V("kw", 0, VW * M), V("fl", 0, VW * M), 0.0, A.mult, A.add)
-            tt(W(33), V("fv", VW - 1, VW * M, VW), V("acc", 32, 32 + M), A.add)
-        tt(MX, ends("wsc", 0, 24), ends("wsc", 2 * NS, 24), A.max)
+            act(V("sg", NS * m, NS * m + NS - 1), V("vs", 2, C - 1, 2), AF.Sign, bias=col("w", m), scale=-1.0, acc=col("acc", 32 + m))
+        tt(THP, E_, O_, A.max)
+        tt(THN, EN_, ON_, A.max)
         FL = 16 * 34
-        BW, PK1, IL, IR = W(5), V("w", FL + 72, FL + 84), W(7), W(8)
-        tt(V("w", FL + 24, FL + 36), E_, O_, A.is_lt)
+        NAW, BW, PK1, IL, IR = V("w", FL + 24, FL + 36), V("w", FL + 36, FL + 48), W(6), W(7), W(8)
+        tt(NAW, E_, O_, A.is_lt)
         tt(W(9), EN_, ON_, A.is_ge)
         tt(BW, O_, EN_, A.is_ge)
-        ts(W(10), W(9), 2.0, A.add)
+        lin(W(10), W(9), 1.0, 2.0)
         tt(W(11), W(10), BW, A.mult)
-        tt(V("w", FL + 36, FL + 48), W(11), V("w", FL + 24, FL + 36), A.max)
+        tt(V("w", FL + 48, FL + 60), W(11), NAW, A.max)
+        tt(PK1, NAW, V("cf", 132, 144), A.add)
         tt(V("w", FL, FL + 12), EN_, THP, A.is_gt)
         tt(V("w", FL + 12, FL + 24), THN, O_, A.is_gt)
-        tt(V("w", FL + 48, FL + 96), V("w", FL, FL + 48), CW4, A.add)
-        cp(V("of", 92, 140), V("w", FL + 48, FL + 96))
-        act(V("rb", 0, NS), IX(IO(0, 2 * C), O_Z), AF.Identity, scale=KS, bias=4 * KS)
-        lin(IL, PK1, 2 * KS, INIT)
-        lin(IR, PK1, 2 * KS, INIT - 1.0)
-        lin(col("lr", 0), col("w", FL + 72), 2 * KS, INIT)
-        lin(col("lr", M * 208 - 1), col("w", FL + 72 + M - 1), 2 * KS, INIT - 1.0)
+        tt(V("w", FL + 64, FL + 124), V("w", FL, FL + 60), CW5, A.add)
+        cp(V("of", 92, 152), V("w", FL + 64, FL + 124))
+        act(V("vq", 0, NS), IX(V("ssb", 0, SW), O_Z), AF.Copy)
+        ts(IL, PK1, KS, A.mult, INIT, A.add)
+        lin(IR, PK1, KS, INIT - 1.0)
+        lin(col("lr", 0), col("w", 16 * 6), KS, INIT)
+        lin(col("lr", M * 208 - 1), col("w", 16 * 6 + M - 1), KS, INIT - 1.0)
         tt(V("aw", 0, K // 2), PS(0, 0, K, 2), V("ssb", 4, 2 * K + 1, 4), A.is_ge)
         for e in range(2):
             tt(V("zk", e, K, 2), V("aw", 0, K // 2), V("zm", e, K, 2), A.mult)
@@ -324,71 +323,78 @@ def rank_program(g, core, T, topo):
         for m in range(M):
             act(V("sg", NS * m, NS * m + NS), V("pp", 0, NS), AF.Sign, bias=col("w", 16 + m), scale=-1.0)
         for b in range(4):
-            act(V("tt", TS * b, TS * b + NS), IX(TWIN(b), O_PK), AF.Copy)
+            act(V("tp", NS * b, NS * b + NS), IX(TWIN(b), O_PK), AF.Copy)
+            act(V("tt", TS * b, TS * b + NS), IX(TWIN(b), O_VC), AF.Copy)
             act(V("tq", TQ * b + NS + 1, TQ * b + TW), TB(b, 0, K), AF.Copy, scale=2.0)
-        ts(O_K, W(33) if VW else V("acc", 32, 32 + M), float(NS), A.add)
-        tt(V("uu", 0, NS), IX(V("utab", 0, C), O_K), V("rb", 0, NS), A.add)
-        lin(V("um", 0, NS), V("uu", 0, NS), 1.0, -1.0)
+        for h in range(2):
+            ts(V("of", 6 * h, 6 * h + 6), V("acc", 32 + 6 * h, 38 + 6 * h), float(NS), A.add)
+            tt(V("uu", K * h, K * h + K), IX(V("utab", 0, C), V("of", 6 * h, 6 * h + 6)), V("c2t", K * h, K * h + K), A.add)
+            lin(V("um", K * h, K * h + K), V("uu", K * h, K * h + K), 1.0, -1.0)
         for m in range(M):
-            n = 16 * m + 15
-            scan(V("lr", 208 * m + 1, 208 * m + 1 + n), V("sg", NS * m, NS * m + n), V("uu", 0, n), col("w", 16 * 7 + m), A.min, A.max)
+            n, b0 = 16 * m + 15, 208 * m + 1
+            if m < A0:
+                scan(V("lr", b0, b0 + n), V("sg", NS * m, NS * m + n), V("uu", 0, n), col("w", 16 * 7 + m), A.min, A.max)
+            else:
+                k = min(n, K)
+                ts(V("sa", K * m, K * m + k), V("pp", 0, k), col("w", 16 + m), A.is_lt)
+                scan(V("lr", b0, b0 + k), V("sa", K * m, K * m + k), V("uu", 0, k), col("w", 16 * 7 + m), A.min, A.max)
+                if n > k:
+                    scan(V("lr", b0 + k, b0 + n), V("sg", NS * m + k, NS * m + n), V("uu", k, n), col("lr", b0 + k - 1), A.min, A.max)
             scan(RV("lr", 208 * m + 16 + 16 * m, 208 * m + 207), RV("sg", NS * m + 16 * m + 1, NS * m + NS), RV("um", 16 * m, NS - 1), col("w", 16 * 8 + m), A.min, A.max)
         tt(V("lm", 0, NS), IX(V("lr", 0, M * 208), O_LR), V("al", 0, NS), A.add)
         tt(V("rm", 0, NS), IX(V("lr", 16, M * 208), O_LR), V("ar", 0, NS), A.add)
         scan(V("ex", 0, NS), V("lm", 0, NS), V("rm", 0, NS), 100.0, A.min, A.min)
-        WI, A1, A2, A3 = V("wi", 0, M), V("wi", 16, 16 + M), V("wi", 32, 32 + M), V("wi", 32 + M, 32 + 2 * M)
+        WI, A1 = V("wi", 0, M), V("wi", 16, 16 + M)
         ts(WI, ends("ex", 0), 1.0 / KS, A.mult)
-        ts(A1, WI, 2047, A.bitwise_and)
+        ts(A1, WI, 1023, A.bitwise_and)
         cp(O_QV, A1)
-        ts(A2, WI, 1023, A.bitwise_and, 1, A.logical_shift_right)
-        ts(A3, WI, 2047, A.bitwise_and, 2, A.logical_shift_right)
-        cp(V("of", 36, 60), V("wi", 32, 32 + 2 * M))
-        SS = V("ssb", 0, SW)
-        tt(V("sm", 0, NS), IX(SS, O_QV), oh, A.mult)
+        SS = V("vq", 0, QW)
+        lin(V("sm", 31, C, 32), THP, -1.0, 0.0)
+        tt(V("sm", 0, C, 2), IX(SS, O_QV), oh, A.mult)
         tt(V("ngp", 0, NS), IX(SS, O_QV), V("pp", 0, NS), A.subtract)
-        scan(V("sc", 0, NS), V("keep", 0, NS), V("sm", 0, NS), 0.0, A.mult, A.add)
-        TH = V("thp", 0, M)
-        tt(TH, ends("sc", 0), THP, A.subtract)
+        scan(V("sc", 0, C), V("keep2", 0, C), V("sm", 0, C), 0.0, A.mult, A.add)
         for m in range(SCH):
             s2 = NS * m
-            act(V("s2", s2, s2 + NS), V("ngp", 0, NS), AF.Sign, bias=col("thp", m), scale=-1.0)
+            act(V("s2", s2, s2 + NS), V("ngp", 0, NS), AF.Sign, bias=col("sc", 32 * m + 31), scale=-1.0)
             act(V("j2", s2 + 16 * m, s2 + NS), V("s2", s2 + 16 * m, s2 + NS), AF.Relu, acc=col("acc", m))
             if m:
                 act(V("j2", s2, s2 + 16 * m), V("s2", s2, s2 + 16 * m), AF.Relu, scale=-1.0, acc=col("acc", 16 + m))
-        tt(V("eq", 0, NS), IX(TH, O_M), V("ngp", 0, NS), A.is_equal)
+        tt(V("eq", 0, NS), IX(V("sc", 0, C), O_M), V("ngp", 0, NS), A.is_equal)
         scan(RV("ec", 0, NS), RV("noh", 0, NS), RV("eq", 0, NS), 0.0, A.mult, A.add)
-        act(W(19), TH, AF.Relu, scale=200.0 / BIG)
+        act(W(19), V("sc", 31, C, 32), AF.Relu, scale=200.0 / BIG)
         tt(W(20), W(19), BASE, A.add)
         tt(W(21), W(20), V("ec", 0, NS, 16), A.add)
         RK = V("fc", K - 1, M * K, K)
         for m in range(SCH, M):
             f0 = NS * (m - SCH)
-            ts(V("fl", f0, f0 + 16 * m), V("ngp", 0, 16 * m), col("thp", m), A.is_le)
-            ts(V("fl", f0 + 16 * m, f0 + NS), V("ngp", 16 * m, NS), col("thp", m), A.is_lt)
+            ts(V("fl", f0, f0 + 16 * m), V("ngp", 0, 16 * m), col("sc", 32 * m + 31), A.is_le)
+            ts(V("fl", f0 + 16 * m, f0 + NS), V("ngp", 16 * m, NS), col("sc", 32 * m + 31), A.is_lt)
             scan(V("fc", K * m, K * m + K), V("fl", f0, f0 + K), V("fl", f0 + K, f0 + NS), col("w", 16 * 21 + m), A.add, A.add)
         tt(W(23, SCH), W(21, SCH), V("acc", 16, 16 + SCH), A.subtract)
         tt(V("fc", K - 1, SCH * K, K), W(23, SCH), V("acc", 0, SCH), A.add)
         ts(O_RK, RK, K - 1.0, A.add)
-        cp(V("kp", 0, NS), IX(V("kptab", 0, 416), O_RK))
+        act(V("kp", 0, NS), IX(V("kptab", 0, 416), O_RK), AF.Copy)
         scan(RV("cum", 15, 15 + NS), RV("kp", 0, NS), RV("kp", 0, NS), -K / 256.0, A.add, A.min)
         for b in range(4):
             for h in range(2):
-                tt(V("tq", TQ * b + K * h, TQ * b + K * h + K), IX(TWIN(b), V("of", 36 + 6 * h, 42 + 6 * h)), V("tt", TS * b + K * h, TS * b + K * h + K), A.add)
+                tt(V("tq", TQ * b + K * h, TQ * b + K * h + K), IX(V("tt", TS * b, TS * b + NS + 1 + C), V("of", 24 + 6 * h, 30 + 6 * h)),
+                   V("tp", NS * b + K * h, NS * b + K * h + K), A.add)
         act(V("pk", 0, NS), V("ngp", 0, NS), AF.Sign, bias=-BIG / 2)
         scan(RV("yy", 0, NS), RV("pk", 0, NS), RV("three", 0, NS), 2.0 * K - 4.0 * (NS - 1), A.add, A.add)
         act(V("j3", 0, K // 2), V("yy", 0, K // 2), AF.Sign, bias=-5.0, acc=col("acc", 48))
         act(V("j3", K // 2, K), V("yy", 1, K // 2 + 1), AF.Sign, bias=-3.0, acc=col("acc", 49))
         ts(W(24, 6), KC, col("acc", 48), A.subtract, col("acc", 49), A.is_lt)
         tt(W(25, 6), W(24, 6), D2, A.mult)
-        lin(W(26, 6), W(25, 6), 1.0, -float(NS))
+        lin(W(26, 6), W(25, 6), 1.0, NS - 2.0)
+        tt(W(27, 6), W(24, 6), KH, A.add)
         for m in range(IVV, 6):
-            act(V("j3", NS * m, NS * m + NS), V("cum", 15, 15 + NS), AF.Sign, bias=col("cf", 40 + m), acc=col("iv", K * m + K - 1))
+            act(V("j3", NS * m, NS * m + NS), V("cum", 15, 15 + NS), AF.Sign, bias=col("w", 16 * 27 + m), scale=-1.0, acc=col("acc", 52 + m))
+            ts(col("of", 84 + m), col("acc", 52 + m), col("w", 16 * 26 + m), A.subtract, -0.5, A.mult)
         for m in range(IVV):
             n = 16 * m + 112
-            ts(V("tf", NS * m, NS * m + n), V("cum", 15, 15 + n), col("cf", 46 + m), A.is_ge, 2.0, A.mult)
-            scan(V("iv", K * m + K - n // 2, K * m + K), V("tf", NS * m, NS * m + n // 2), V("tf", NS * m + n // 2, NS * m + n), -float(NS), A.add, A.add)
-        tt(W(27, 6), W(26, 6), V("iv", K - 1, 6 * K, K), A.max)
-        ts(O_F, W(27, 6), NS - 2.0, A.add, 0.5, A.mult)
+            ts(V("tf", NS * m, NS * m + n), V("cum", 15, 15 + n), col("w", 16 * 27 + m), A.is_ge, 2.0, A.mult)
+            scan(V("iv", K * m + K - n // 2, K * m + K), V("tf", NS * m, NS * m + n // 2), V("tf", NS * m + n // 2, NS * m + n), col("w", 16 * 26 + m), A.add, A.add)
+        ts(V("of", 84, 84 + IVV), V("iv", K - 1, IVV * K, K), -float(NS), A.add, 0.5, A.mult)
         for b in range(4):
             if b < FS:
                 act(V("ft", b, 4 * K, 4), IX(V("tq", TQ * b, TQ * b + TW), O_F), AF.Copy, scale=0.5)
@@ -405,6 +411,7 @@ def rank_program(g, core, T, topo):
             T[ql][:, 0:K].bitcast(u8), T[qf][:, 0:K].bitcast(u8), arr, T.sem.sent, pid, rid, mask), [], [V(qf, 0, K)], 500, dma=("", 0), lat=3000)
         op("g", lambda sf=sf, sl=sl, arr=arr, pid=pid, rid=rid, mask=mask: g.remote_dma(
             T[sl][:, 0:K], T[sf][:, 0:K], arr, T.sem.sent, pid, rid, mask), [], [V(sf, 0, K)], 500, dma=("", 0), lat=3000)
+        first.append((len(ops) - 2, len(ops) - 1))
         op("arrive", None, [V(ql, 0, K), V(sl, 0, K)], [V(qf, 0, K)], 0, dma=("ar%d" % t, 2 * ne), lat=3500)
 
         for m in range(M):
@@ -414,26 +421,26 @@ def rank_program(g, core, T, topo):
         for h in range(2):
             tt(V("lb", K * h, K * h + K), IX(V("lp", 0, 6 * 208), V("co", 32 + 6 * h, 38 + 6 * h)), V("oh", 0, K), A.mult)
         scan(V("lc", 0, NS), V("keepb", 0, NS), V("lb", 0, NS), 0.0, A.mult, A.add)
-        tt(W(28), PK1, A2, A.subtract)
+        tt(W(28), CW, A1, A.subtract)
         tt(W(29), W(28), UC, A.max)
         tt(W(30), W(29), ends("lc", 0), A.min)
         tt(W(31), RK, UC1, A.max)
         tt(W(32), W(31), W(30), A.min)
         ts(O_L, W(32), -256.0, A.mult, 271.0, A.add)
         CUM = V("cum", 0, 16 + NS)
-        fill(V("nc", 0, 464), 0)
+        fill(V("nc", 0, QW + 16), 0)
         act(V("cpv", 0, NS), V("cum", 15, 15 + NS), AF.Copy)
         tt(V("an", 0, NS), IX(CUM, O_L), V("cpv", 0, NS), A.not_equal)
-        cp(IX(V("nc", 0, 464), O_SC), V("an", 0, NS))
+        cp(IX(V("nc", 16, QW + 16), O_QV), V("an", 0, NS))
         tt(V("r0", 0, NS), IX(CUM, O_L), V("an", 0, NS), A.mult)
-        scan(V("r4", 0, NS), V("nc", 0, NS), V("r0", 0, NS), 0.0, A.add, A.min)
-        scan(RV("r5", 0, NS), RV("nc", 1, NS + 1), RV("r4", 0, NS), 0.0, A.add, A.min)
+        scan(V("r4", 0, NS), V("nc", 15, NS + 15), V("r0", 0, NS), 0.0, A.add, A.min)
+        scan(RV("r5", 0, NS), RV("nc", 16, NS + 16), RV("r4", 0, NS), 0.0, A.add, A.min)
         tt(V("hb", 1, C, 2), IX(V("r5", 0, NS + 16), O_CO), V("mj", 1, C, 2), A.max)
         tt(V("hb", 2, C + 2, 2), IX(V("r5", 0, NS + 16), O_CE), V("mj", 2, C + 2, 2), A.max)
         scan(V("hc", 0, C), V("keepb", 0, C), V("hb", 0, C), 0.0, A.mult, A.add)
         ts(O_H, ends("hc", 0, 2 * M), -256.0, A.mult, -1.0, A.add)
         if t == R - 1:
-            act(V("et", 0, NS), IX(IO(0, 2 * C), O_PK), AF.Identity, bias=-1.0)
+            act(V("et", 0, NS), IX(IO(0, C + 8), O_PK), AF.Identity, bias=-1.0)
             act(V("er", 0, K), IX(V("et", 0, TW), O_F), AF.Copy)
 
         XN = "x%d" % (t + 1)
@@ -444,7 +451,7 @@ def rank_program(g, core, T, topo):
             else:
                 act(V("ht", K * b, K * b + K), PS(b, 0, K), AF.Relu, scale=0.03125)
         for h, (lo, hi) in enumerate(PIECES[t + 1]):
-            o_h = V("of", 140 + lo // 16, 140 + hi // 16)
+            o_h = V("of", 152 + lo // 16, 152 + hi // 16)
             for b in range(4):
                 if b < 4 - HS[h]:
                     tt(V(XN, 4 * lo + b, 4 * hi, 4), IX(V("ht", K * b, K * b + K), o_h), TB(b, lo, hi), A.add)
@@ -479,6 +486,13 @@ def rank_program(g, core, T, topo):
         for a, wr in [(a, True) for a in ws] + [(a, False) for a in rs]:
             touch.setdefault(a[0], []).append((i, a, wr))
     n = len(ops)
+    above = []
+    for i in range(n):
+        far = set()
+        for j in deps[i]:
+            far |= above[j]
+        above.append(set() if ops[i][0] == "arrive" else far | deps[i])
+        deps[i] = sorted(deps[i] - far)
     users = [[] for i in range(n)]
     for i in range(n):
         for j in deps[i]:
@@ -489,8 +503,8 @@ def rank_program(g, core, T, topo):
         ready = [i for i in range(n) if not left[i]]
         can, free, order, end = [(ops[i][6] if back else 0.0) for i in range(n)], {}, [], [0.0] * n
         while ready:
-            first, q = min((max(can[i], free.get(ops[i][0], 0.0)), ops[i][0]) for i in ready)
-            i = -max((prio[i], -i) for i in ready if ops[i][0] == q and can[i] <= first + slack)[1]
+            soon, q = min((max(can[i], free.get(ops[i][0], 0.0)), ops[i][0]) for i in ready)
+            i = -max((prio[i], -i) for i in ready if ops[i][0] == q and can[i] <= soon + slack)[1]
             end[i] = free[q] = max(can[i], free.get(q, 0.0)) + ops[i][5]
             ready.remove(i)
             order.append(i)
@@ -501,28 +515,32 @@ def rank_program(g, core, T, topo):
                     ready.append(u)
         return order, end
 
+    queue = ["vstgya".index(o[0][0]) for o in ops]
+    timing = [([f * (o[5] + jump * x) for o, x in zip(ops, slow)], [wake + (far if o[0] == "arrive" else o[6]) for o in ops]) for f, wake, far, jump in CASES]
+
     def span_of(order):
         s = 0.0
-        for f, wake, far in CASES:
-            free, end = {}, [0.0] * n
+        for busy, lag in timing:
+            free, end = [0.0] * 6, [0.0] * n
             for i in order:
-                q, t0 = ops[i][0], -wake
+                q = queue[i]
+                t0 = free[q]
                 for j in deps[i]:
                     if end[j] > t0:
                         t0 = end[j]
-                free[q] = max(free.get(q, 0.0), t0 + wake) + f * ops[i][5]
-                end[i] = free[q] + (far if q == "arrive" else ops[i][6])
+                t0 += busy[i]
+                free[q] = t0
+                end[i] = t0 + lag[i]
             s += max(end)
         return s
 
     def chain(order, case):
-        f, wake, far = case
-        free, end, prev = {}, [0.0] * n, [None] * n
+        busy, lag = case
+        free, end, prev = [(0.0, -1, True)] * 6, [0.0] * n, [None] * n
         for i in order:
-            q = ops[i][0]
-            t0, j, near = max([free.get(q, (0.0, -1, True))] + [(end[j] + wake, j, False) for j in deps[i]])
-            free[q] = (t0 + f * ops[i][5], i, True)
-            end[i], prev[i] = free[q][0] + (far if q == "arrive" else ops[i][6]), (j, near)
+            t0, j, near = max([free[queue[i]]] + [(end[j], j, False) for j in deps[i]])
+            free[queue[i]] = (t0 + busy[i], i, True)
+            end[i], prev[i] = t0 + busy[i] + lag[i], (j, near)
         i, pairs = max(range(n), key=lambda i: end[i]), []
         while prev[i][0] >= 0:
             if prev[i][1]:
@@ -555,7 +573,7 @@ def rank_program(g, core, T, topo):
         span, order = ORDER[:2]
         best = (span, order)
         for k in range(MOVES):
-            pairs = chain(order, CASES[k % len(CASES)])
+            pairs = chain(order, timing[k % len(CASES)])
             j, i = pairs[int(uni() * len(pairs))]
             at = {x: p for p, x in enumerate(order)}
             new = list(order)
@@ -577,7 +595,10 @@ def rank_program(g, core, T, topo):
                 if s < best[0]:
                     best = (s, new)
         ORDER[:2] = best
-    order = ORDER[1]
+    order = list(ORDER[1])
+    for i, j in first:
+        a, b = order.index(i), order.index(j)
+        order[min(a, b)], order[max(a, b)] = i, j
     place = {i: k for k, i in enumerate(order)}
     waits = {}
     for i in order:

import math
from concourse.mybir import dt, AluOpType as A, ActivationFunctionType as AF

C, K, R = 384, 96, 2
NS = C // 2
M = NS // 16
BIG = 1.0e29
KS = 2.0 ** -19
INIT = (500 * 1024 + NS) * KS
A0 = 6
SCH = 6
IVV = 4
HTV = 2
FS = 2
HS = (2, 3)
TW = NS + K + 1
TQ = NS + K + 8
TS = NS + C + 8
SW = 2 * C + 8
QW = NS + C + 16
PIECES = (((0, 224), (224, C)), ((0, 224), (224, C)), ((0, 256), (256, C)))
TURNS, NOISE, MOVES, HEAT = 300, 200.0, 30000, 300.0
CASES = ((0.83, 200.0, 1800.0, 0.0), (0.9, 250.0, 2000.0, -1.0), (1.0, 130.0, 2000.0, 0.5), (1.15, 200.0, 2300.0, 1.0))
ORDER = []

X4, U8, F32, BF, I32, U16 = "float8_e4m3fn_x4", "uint8", "float32", "bfloat16", "int32", "uint16"
SCRATCH = {}
for _d, _l in [
    (X4, [("qx0", C), ("qx1", C), ("qx2", C), ("qu", 128), ("qur", 128), ("qv", 128), ("qe", 512), ("qw", 512), ("qf0", 128), ("qf1", 128),
          ("ql0", K + 128), ("ql1", K + 128)]),
    (U8, [("sx0", C), ("sx1", C), ("sx2", C), ("su", 128), ("sur", 128), ("sv", 128), ("se", 512), ("sw", 512), ("sf0", 128), ("sf1", 128),
          ("sl0", K + 128), ("sl1", K + 128)]),
    (I32, [("ci", 64), ("wi", 64)]),
    (U16, [("co", 64), ("of", 176)]),
    (BF, [("x0", 4 * C), ("x1", 4 * C), ("x2", 4 * C), ("ut", 512), ("vt", 512), ("ez", 516), ("zt", 512), ("ft", 512), ("keepb", C), ("kptab", 416),
          ("irow", NS), ("sg", M * NS), ("sa", M * K), ("fl", M * NS), ("fc", M * K), ("pk", NS), ("three", NS), ("yy", NS),
          ("s2", SCH * NS), ("j2", SCH * NS), ("j3", 6 * NS), ("eq", NS), ("ec", NS), ("noh", NS), ("kp", NS), ("cum", 16 + NS), ("tf", 6 * NS),
          ("lp", 6 * 208), ("lb", NS), ("lc", NS), ("an", NS), ("cpv", NS), ("nc", QW + 16), ("r0", NS), ("r4", NS), ("r5", NS + 16), ("hb", C + 2), ("hc", C)]),
    (F32, [("cf", 192), ("j16", NS), ("oh", C), ("keep", NS), ("keep2", C), ("utab", C), ("c2t", NS), ("vq", QW), ("iot", C + 16), ("al", NS), ("ar", NS),
           ("a0", NS), ("odd", NS), ("vs", C), ("zm", K), ("z0", K), ("z1", K), ("pp", NS), ("mk", 4 * NS), ("wsc", 4 * NS), ("ssb", SW),
           ("w", 768), ("acc", 64), ("iv", 6 * K), ("uu", NS), ("um", NS), ("lr", M * 208), ("lm", NS), ("rm", NS), ("ex", NS), ("sm", C),
           ("sc", C), ("ngp", NS), ("aw", K // 2), ("zk", K), ("zs", K), ("mj", C + 2), ("tt", 4 * TS), ("tp", 4 * NS), ("tq", 4 * TQ),
           ("ht", 4 * K), ("hg", 4 * C), ("et", TW), ("er", K), ("olr", C), ("ysb", C)]),
]:
    for _n, _w in _l:
        SCRATCH[_n] = ("sbuf", [128, _w], _d)
for _b in range(8):
    SCRATCH["ps%d" % _b] = ("psum", [128, 512], F32)

SEMAPHORES = ["cv", "cs", "ct", "cg", "du", "dx0", "dx1", "dw", "dv", "out", "ar0", "ar1", "sent"]
COUNTER = {"v": "cv", "s": "cs", "t": "ct", "g": "cg"}


def rank_program(g, core, T, topo):
    rank = T.rank_of(core)
    if rank is None:
        return
    Q = {"v": g.vector, "s": g.scalar, "t": g.tensor, "g": g, "y": g.sync}
    ops, first, slow = [], [], []

    def V(n, lo, hi, step=1):
        return (T[n][:, lo:hi:step], n, lo, hi, step)

    def RV(n, lo, hi):
        return (T[n][:, hi - 1:(lo - 1 if lo else None):-1], n, lo, hi, 1)

    def col(n, j):
        return V(n, j, j + 1)

    def IX(win, off):
        return (win[0].indirect(off[0]), win[1], win[2], win[3], 1, off)

    def size(a):
        return 16 * size(a[5]) if len(a) > 5 else len(range(a[2], a[3], a[4]))

    def cost(o, a, rate):
        if len(a) > 5:
            return (60 + 1.6 * size(a), 0.5 * size(a))
        if len(o) > 5:
            return (60 + 3.8 * size(o), 2.2 * size(o))
        return max(64, size(a) * rate)

    def half(*xs):
        return 0.5 if all(SCRATCH[x[1]][2] in (BF, U16) for x in xs) else 1.0

    def op(q, fn, wr, rd, ns, dma=None, lat=0.0):
        rs = []
        for a in rd:
            if isinstance(a, tuple):
                rs.append(a[1:5])
                if len(a) > 5:
                    rs.append(a[5][1:5])
        ws = [a[1:5] for a in wr]
        rs += [a[5][1:5] for a in wr if len(a) > 5]
        slow.append(ns[1] if isinstance(ns, tuple) else 0.0)
        ops.append((q, fn, ws, rs, dma, ns[0] if isinstance(ns, tuple) else ns, lat))

    def ap(a):
        return a[0] if isinstance(a, tuple) else a

    def tt(o, a, b, f):
        op("v", lambda: g.vector.tensor_tensor(o[0], a[0], b[0], f), [o], [a, b], cost(o, a, 1 if "ps" in (a[1][:2], b[1][:2]) else 2))

    def ts(o, a, s1, f0, s2=None, f1=None):
        if s2 is None:
            op("v", lambda: g.vector.tensor_scalar(o[0], a[0], ap(s1), None, f0), [o], [a, s1], cost(o, a, half(o, a)))
        else:
            op("v", lambda: g.vector.tensor_scalar(o[0], a[0], ap(s1), ap(s2), f0, f1), [o], [a, s1, s2], cost(o, a, half(o, a)))

    def cp(o, a):
        op("v", lambda: g.vector.tensor_copy(o[0], a[0]), [o], [a], cost(o, a, half(o, a)))

    def scan(o, a, b, init, f0, f1):
        op("v", lambda: g.vector.tensor_tensor_scan(o[0], a[0], b[0], ap(init), f0, f1), [o], [a, b, init], cost(o, a, half(o, a, b)))

    def ms(o, c):
        op("v", lambda: g.vector.memset(o[0], c), [o], [], cost(o, o, half(o)))

    def act(o, a, f, bias=None, scale=None, acc=None):
        kw = {}
        if bias is not None:
            kw["bias"] = ap(bias)
        if scale is not None:
            kw["scale"] = ap(scale)
        if acc is not None:
            kw["accum_out"] = acc[0]
        op("s", lambda: g.scalar.activation(o[0], a[0], f, **kw), [o] + ([acc] if acc else []), [a, bias, scale], cost(o, a, 1) + 24 if acc else cost(o, a, 1))

    def lin(o, a, scale, bias):
        act(o, a, AF.Identity, bias=bias, scale=scale)

    def quant(q, s, a):
        op("v", lambda: g.vector.quantize_mx(q[0], s[0], a[0]), [q, s], [a], 14 + 0.27 * size(a))

    def mm(o, lq, ls, rq, rs):
        op("t", lambda: g.tensor.matmul_mx(o[0], lq[0], ls[0], rq[0], rs[0], True, True), [o], [lq, ls, rq, rs], size(rq) + 16)

    def iota(o, pat, base, cm=0):
        if SCRATCH[o[1]][2] == I32:
            op("g", lambda: g.iota(o[0], pat, base, cm), [o], [], 156 + 2 * size(o))
        else:
            op("g", lambda: g.iota(o[0], pat, base, cm, allow_small_or_imprecise_dtypes=True), [o], [], 156 + 2 * size(o))

    def fill(o, c):
        iota(o, [[0, size(o)]], c)

    def dma(q, sem, out, in_, wr, rd, lat=1900.0):
        op(q, lambda: Q[q].dma_start(out, in_), wr, rd, 60, dma=(sem, 16), lat=lat)

    def W(j, n=M):
        return V("w", 16 * j, 16 * j + n)

    def ends(n, lo, k=M):
        return V(n, lo + 15, lo + 16 * k, 16)

    def PS(b, lo, hi, step=1):
        return V("ps%d" % b, lo, hi, step)

    def IO(lo, hi, step=1):
        return V("iot", lo, hi, step)

    u8 = dt.uint8
    dma("y", "du", T.ut[:], T.u[:], [V("ut", 0, 512)], [])
    for h, (lo, hi) in enumerate(PIECES[0]):
        dma("sy"[h], "dx%d" % h, T.x0[:, 4 * lo:4 * hi], T.x[:, 4 * lo:4 * hi], [V("x0", 4 * lo, 4 * hi)], [], 2300 + 300 * h)
    first.append((0, 2))
    dma("y", "dw", T.qw[:].bitcast(u8), T.wc[:], [V("qw", 0, 512)], [V("x0", 0, 4 * C)])
    dma("y", "dw", T.sw[:], T.ws[:], [V("sw", 0, 512)], [V("x0", 0, 4 * C)])
    dma("y", "dv", T.vt[:], T.v[:], [V("vt", 0, 512)], [V("x0", 0, 4 * C)])

    PM, PAR, CW, CW5, KW = col("cf", 0), col("cf", 1), V("cf", 108, 120), V("cf", 108, 168), V("cf", 108, 114)
    KH, KC, DB, BASE = V("cf", 40, 46), V("cf", 52, 58), V("cf", 64, 70), V("cf", 70, 82)
    UC, UC1 = V("cf", 82, 94), V("cf", 94, 106)
    O_U, O_LR, O_M = V("co", 0, 8), V("co", 8, 20), V("co", 20, 32)
    iota(col("ci", 3), [[1, 1]], 0, 1)
    iota(V("ci", 8, 16), [[16, 8]], 0)
    iota(V("j16", 0, NS), [[0, M], [1, 16]], 0)
    iota(IO(0, C + 16), [[1, C + 16]], 0)
    lin(V("vq", NS, QW), IO(0, QW - NS), 0.0, -BIG)
    lin(V("c2t", 0, NS), IO(0, NS), KS, 0.0)
    ms(V("ez", 0, 516), 0.0)
    ms(V("zt", 0, 512), 0.0)
    for lo in range(0, SW, 512):
        lin(V("ssb", lo, min(SW, lo + 512)), V("zt", 0, min(SW - lo, 512)), 0.0, BIG)
    ms(V("odd", 0, NS, 2), BIG)
    ms(V("odd", 1, NS, 2), 0.0)
    ts(col("ci", 1), col("ci", 3), 15, A.bitwise_and)
    ts(col("ci", 2), col("ci", 3), 1, A.bitwise_and)
    cp(O_U, V("ci", 8, 16))
    cp(V("cf", 0, 3), V("ci", 1, 4))
    ts(V("oh", 0, NS), V("j16", 0, NS), PM, A.is_equal)
    act(V("oh", NS, C), V("oh", 0, NS), AF.Copy)
    act(V("keep", 0, NS), V("j16", 0, NS), AF.Sign)
    for n, k in (("keepb", 16), ("keep2", 32)):
        fill(V(n, 0, C), 1)
        fill(V(n, 0, C, k), 0)
    ts(V("ez", 3, 515, 4), IO(0, 128), col("cf", 2), A.is_equal)
    act(col("mk", 2 * NS - 1), col("oh", 15), AF.Copy, scale=-BIG)
    ms(col("mk", 4 * NS - 1), 0.0)
    quant(V("qu", 0, 128), V("su", 0, 128), V("ut", 0, 512))
    op("v", lambda: g.vector.tensor_copy(T.qur[:].bitcast(dt.uint32), T.qu[:].bitcast(dt.uint32).indirect(O_U[0])), [V("qur", 0, 128)], [V("qu", 0, 128), O_U], 260)
    act(V("sur", 0, 128), IX(V("su", 0, 128), O_U), AF.Copy)
    for b in range(4):
        quant(V("qe", 128 * b, 128 * b + 128), V("se", 128 * b, 128 * b + 128), V("ez", 3 - b, 515 - b))
    fill(V("tt", NS, 4 * TS, TS), 0)
    fill(V("tt", NS + C + 1, 4 * TS, TS), 0)
    fill(V("tq", NS, 4 * TQ, TQ), 0)
    lin(V("utab", 0, C), IO(0, C), -1024 * KS, 392 * 1024 * KS)
    lin(CW, IO(0, NS, 16), 1.0, PM)
    lin(V("cf", 120, 132), IO(0, NS, 16), 1.0, PM)
    lin(V("cf", 132, 144), CW, 2.0, 1.0)
    lin(V("cf", 144, 156), CW, 2.0, 2.0)
    lin(V("cf", 156, 168), CW, 4.0, 4.0)
    lin(V("cf", 40, 40 + IVV), V("cf", 108, 108 + IVV), -1.0 / 256, 0.0)
    lin(V("cf", 40 + IVV, 46), V("cf", 108 + IVV, 114), -1.0 / 256, -0.5 / 256)
    lin(KC, KW, 2.0, -float(K))
    fill(V("three", 0, NS), 3)
    lin(UC, CW, -1.0 / 256, 1.0)
    lin(UC1, CW, -1.0 / 256, 255.0 / 256)
    ts(O_LR, IO(0, M), 224.0, A.mult, PM, A.add)
    cp(O_M, IO(31, C, 32))
    fill(V("sm", 1, C, 2), 0)
    ts(V("co", 32, 38), IO(0, 6), 224.0, A.mult, PM, A.add)
    iota(V("cf", 4, 10), [[-208, 6]], 208 * 5 + NS)
    ts(V("co", 38, 44), V("cf", 4, 10), PM, A.add)
    iota(V("a0", 0, NS), [[1, M], [0, 16]], 52)
    tt(V("a0", 0, NS), V("a0", 0, NS), V("oh", 0, NS), A.mult)
    lin(V("al", 0, NS), V("a0", 0, NS), -1.0, 64.0)
    lin(V("ar", 0, NS), V("a0", 0, NS), -1.0, 65.0)
    fill(V("lr", 208, M * 208, 208), 0)
    fill(V("lr", 207, (M - 1) * 208, 208), 0)
    lin(V("noh", 0, NS), V("oh", 0, NS), -1.0, 1.0)
    lin(V("kptab", 0, K), IO(0, K), 0.0, 1.0 / 256)
    fill(V("kptab", K, 416), 0)
    fill(V("cum", 0, 15), 0)
    lin(col("cum", 15 + NS), IO(0, 1), 0.0, -K / 256.0)
    fill(V("r5", NS, NS + 16), 0)
    fill(col("hb", 0), 0)
    lin(V("z0", 0, K, 2), IO(0, K // 2), -2.0, -2.0 * (NS + 1))
    lin(V("z0", 1, K, 2), IO(0, K // 2), 2.0, 2.0 * (NS + 2))
    tt(V("zm", 0, K), V("z0", 0, K), V("oh", 0, K), A.mult)
    lin(W(45, 6), KW, 1.0, 2.0 * NS + 3)
    lin(W(46, 6), KW, 2.0, 2.0 * NS + 4)
    act(W(47, 6), W(45, 6), AF.Identity, scale=PAR)
    tt(DB, W(46, 6), W(47, 6), A.subtract)
    iota(V("cf", 70, 70 + SCH), [[16, SCH]], -K)
    fill(V("cf", 70 + SCH, 82), -K)
    fill(col("acc", 16), 0)
    fill(V("ft", 4 * K, 512), 0)
    lin(V("irow", 0, NS), IO(0, NS), -1.0 / 256, 255.0 / 256)
    fill(V("lp", 0, 6 * 208, 208), 1)
    fill(V("lp", 16, 6 * 208, 224), 1)
    iota(V("et", NS, TW), [[1, K + 1]], -1)
    lin(V("z1", 0, K), IO(0, K), -1.0 / 256, -1.0 / 256)
    tt(V("mj", 0, K), V("z1", 0, K), V("oh", 0, K), A.mult)
    lin(V("mj", K, C), V("oh", K, C), -1.0, 0.0)
    fill(V("mj", C, C + 2), 0)
    for t in range(R):
        quant(V("ql%d" % t, K, K + 128), V("sl%d" % t, K, K + 128), V("zt", 0, 512))
    quant(V("qv", 0, 128), V("sv", 0, 128), V("vt", 0, 512))

    oh = V("oh", 0, NS)
    O_QV, O_RK, O_L, O_F, O_H = V("of", 24, 36), V("of", 60, 72), V("of", 72, 84), V("of", 84, 90), V("of", 152, 176)
    O_CO, O_CE, O_PK, O_VC, O_Z = [V("of", 92 + M * j, 104 + M * j) for j in range(5)]

    def TB(b, lo=0, hi=C):
        return V("tt", TS * b + NS + 1 + lo, TS * b + NS + 1 + hi)

    def TWIN(b):
        return V("tt", TS * b + NS, TS * b + NS + 2 + C)

    for t in range(R):
        QX, SX = V("qx%d" % t, 0, C), V("sx%d" % t, 0, C)
        for h, (lo, hi) in enumerate(PIECES[t]):
            quant(V(QX[1], lo, hi), V(SX[1], lo, hi), V("x%d" % t, 4 * lo, 4 * hi))
            for b in (h, 2 + h):
                mm(PS(b, 0, hi - NS * h), V("qur", 0, 128), V("sur", 0, 128), V(QX[1], NS * h, hi), V(SX[1], NS * h, hi))
        for b in range(4):
            mm(PS(4 + b, 0, C), V("qe", 128 * b, 128 * b + 128), V("se", 128 * b, 128 * b + 128), QX, SX)

        E_, EN_, O_, ON_ = ends("wsc", 0), ends("wsc", NS), ends("wsc", 2 * NS), ends("wsc", 3 * NS)
        THP, THN = W(1), W(2)
        for h in range(2):
            c0, n = K * h, K - h
            act(V("ssb", 4 + 4 * c0, 4 * (c0 + K) + 1, 4), PS(2 + h, 1, NS, 2), AF.Copy)
            act(V("ssb", 2 + 4 * c0, 4 * (c0 + K), 4), PS(2 + h, 0, NS, 2), AF.Copy)
            for j, (d, k) in enumerate(((0, K), (2, n), (1, K), (3, n))):
                tt(V("mk", NS * j + c0, NS * j + c0 + k), PS(h, d, d + 2 * k - 1, 2), V("oh", 0, k), A.mult)
                scan(V("wsc", NS * j + c0, NS * j + c0 + K), V("keep", 0, K), V("mk", NS * j + c0, NS * j + c0 + K), 0.0, A.mult, A.add)
            scan(V("vs", 2 * c0 + 1, 2 * (c0 + n) + 1), V("odd", 0, 2 * n), PS(h, 1, 2 * n + 1), 0.0, A.add, A.min)
            tt(V("pp", c0, c0 + K), V("ssb", 4 + 4 * c0, 4 * (c0 + K) + 1, 4), PS(h, 0, NS, 2), A.max)
            tt(V("w", 6 * h, 6 * h + 6), ends("wsc", 2 * NS + c0, 6), ends("wsc", NS + c0, 6), A.min)
        for b in range(4):
            act(TB(b), PS(4 + b, 0, C), AF.Copy)
        for m in range(M):
            act(V("sg", NS * m, NS * m + NS - 1), V("vs", 2, C - 1, 2), AF.Sign, bias=col("w", m), scale=-1.0, acc=col("acc", 32 + m))
        tt(THP, E_, O_, A.max)
        tt(THN, EN_, ON_, A.max)
        FL = 16 * 34
        NAW, BW, PK1, IL, IR = V("w", FL + 24, FL + 36), V("w", FL + 36, FL + 48), W(6), W(7), W(8)
        tt(NAW, E_, O_, A.is_lt)
        tt(W(9), EN_, ON_, A.is_ge)
        tt(BW, O_, EN_, A.is_ge)
        lin(W(10), W(9), 1.0, 2.0)
        tt(W(11), W(10), BW, A.mult)
        tt(V("w", FL + 48, FL + 60), W(11), NAW, A.max)
        tt(PK1, NAW, V("cf", 132, 144), A.add)
        tt(V("w", FL, FL + 12), EN_, THP, A.is_gt)
        tt(V("w", FL + 12, FL + 24), THN, O_, A.is_gt)
        tt(V("w", FL + 64, FL + 124), V("w", FL, FL + 60), CW5, A.add)
        cp(V("of", 92, 152), V("w", FL + 64, FL + 124))
        act(V("vq", 0, NS), IX(V("ssb", 0, SW), O_Z), AF.Copy)
        ts(IL, PK1, KS, A.mult, INIT, A.add)
        lin(IR, PK1, KS, INIT - 1.0)
        lin(col("lr", 0), col("w", 16 * 6), KS, INIT)
        lin(col("lr", M * 208 - 1), col("w", 16 * 6 + M - 1), KS, INIT - 1.0)
        tt(V("aw", 0, K // 2), PS(0, 0, K, 2), V("ssb", 4, 2 * K + 1, 4), A.is_ge)
        for e in range(2):
            tt(V("zk", e, K, 2), V("aw", 0, K // 2), V("zm", e, K, 2), A.mult)
        scan(V("zs", 0, K), V("keep", 0, K), V("zk", 0, K), 0.0, A.mult, A.add)
        D2 = W(17, 6)
        tt(D2, ends("zs", 0, 6), DB, A.add)
        for m in range(M):
            act(V("sg", NS * m, NS * m + NS), V("pp", 0, NS), AF.Sign, bias=col("w", 16 + m), scale=-1.0)
        for b in range(4):
            act(V("tp", NS * b, NS * b + NS), IX(TWIN(b), O_PK), AF.Copy)
            act(V("tt", TS * b, TS * b + NS), IX(TWIN(b), O_VC), AF.Copy)
            act(V("tq", TQ * b + NS + 1, TQ * b + TW), TB(b, 0, K), AF.Copy, scale=2.0)
        for h in range(2):
            ts(V("of", 6 * h, 6 * h + 6), V("acc", 32 + 6 * h, 38 + 6 * h), float(NS), A.add)
            tt(V("uu", K * h, K * h + K), IX(V("utab", 0, C), V("of", 6 * h, 6 * h + 6)), V("c2t", K * h, K * h + K), A.add)
            lin(V("um", K * h, K * h + K), V("uu", K * h, K * h + K), 1.0, -1.0)
        for m in range(M):
            n, b0 = 16 * m + 15, 208 * m + 1
            if m < A0:
                scan(V("lr", b0, b0 + n), V("sg", NS * m, NS * m + n), V("uu", 0, n), col("w", 16 * 7 + m), A.min, A.max)
            else:
                k = min(n, K)
                ts(V("sa", K * m, K * m + k), V("pp", 0, k), col("w", 16 + m), A.is_lt)
                scan(V("lr", b0, b0 + k), V("sa", K * m, K * m + k), V("uu", 0, k), col("w", 16 * 7 + m), A.min, A.max)
                if n > k:
                    scan(V("lr", b0 + k, b0 + n), V("sg", NS * m + k, NS * m + n), V("uu", k, n), col("lr", b0 + k - 1), A.min, A.max)
            scan(RV("lr", 208 * m + 16 + 16 * m, 208 * m + 207), RV("sg", NS * m + 16 * m + 1, NS * m + NS), RV("um", 16 * m, NS - 1), col("w", 16 * 8 + m), A.min, A.max)
        tt(V("lm", 0, NS), IX(V("lr", 0, M * 208), O_LR), V("al", 0, NS), A.add)
        tt(V("rm", 0, NS), IX(V("lr", 16, M * 208), O_LR), V("ar", 0, NS), A.add)
        scan(V("ex", 0, NS), V("lm", 0, NS), V("rm", 0, NS), 100.0, A.min, A.min)
        WI, A1 = V("wi", 0, M), V("wi", 16, 16 + M)
        ts(WI, ends("ex", 0), 1.0 / KS, A.mult)
        ts(A1, WI, 1023, A.bitwise_and)
        cp(O_QV, A1)
        SS = V("vq", 0, QW)
        lin(V("sm", 31, C, 32), THP, -1.0, 0.0)
        tt(V("sm", 0, C, 2), IX(SS, O_QV), oh, A.mult)
        tt(V("ngp", 0, NS), IX(SS, O_QV), V("pp", 0, NS), A.subtract)
        scan(V("sc", 0, C), V("keep2", 0, C), V("sm", 0, C), 0.0, A.mult, A.add)
        for m in range(SCH):
            s2 = NS * m
            act(V("s2", s2, s2 + NS), V("ngp", 0, NS), AF.Sign, bias=col("sc", 32 * m + 31), scale=-1.0)
            act(V("j2", s2 + 16 * m, s2 + NS), V("s2", s2 + 16 * m, s2 + NS), AF.Relu, acc=col("acc", m))
            if m:
                act(V("j2", s2, s2 + 16 * m), V("s2", s2, s2 + 16 * m), AF.Relu, scale=-1.0, acc=col("acc", 16 + m))
        tt(V("eq", 0, NS), IX(V("sc", 0, C), O_M), V("ngp", 0, NS), A.is_equal)
        scan(RV("ec", 0, NS), RV("noh", 0, NS), RV("eq", 0, NS), 0.0, A.mult, A.add)
        act(W(19), V("sc", 31, C, 32), AF.Relu, scale=200.0 / BIG)
        tt(W(20), W(19), BASE, A.add)
        tt(W(21), W(20), V("ec", 0, NS, 16), A.add)
        RK = V("fc", K - 1, M * K, K)
        for m in range(SCH, M):
            f0 = NS * (m - SCH)
            ts(V("fl", f0, f0 + 16 * m), V("ngp", 0, 16 * m), col("sc", 32 * m + 31), A.is_le)
            ts(V("fl", f0 + 16 * m, f0 + NS), V("ngp", 16 * m, NS), col("sc", 32 * m + 31), A.is_lt)
            scan(V("fc", K * m, K * m + K), V("fl", f0, f0 + K), V("fl", f0 + K, f0 + NS), col("w", 16 * 21 + m), A.add, A.add)
        tt(W(23, SCH), W(21, SCH), V("acc", 16, 16 + SCH), A.subtract)
        tt(V("fc", K - 1, SCH * K, K), W(23, SCH), V("acc", 0, SCH), A.add)
        ts(O_RK, RK, K - 1.0, A.add)
        act(V("kp", 0, NS), IX(V("kptab", 0, 416), O_RK), AF.Copy)
        scan(RV("cum", 15, 15 + NS), RV("kp", 0, NS), RV("kp", 0, NS), -K / 256.0, A.add, A.min)
        for b in range(4):
            for h in range(2):
                tt(V("tq", TQ * b + K * h, TQ * b + K * h + K), IX(V("tt", TS * b, TS * b + NS + 1 + C), V("of", 24 + 6 * h, 30 + 6 * h)),
                   V("tp", NS * b + K * h, NS * b + K * h + K), A.add)
        act(V("pk", 0, NS), V("ngp", 0, NS), AF.Sign, bias=-BIG / 2)
        scan(RV("yy", 0, NS), RV("pk", 0, NS), RV("three", 0, NS), 2.0 * K - 4.0 * (NS - 1), A.add, A.add)
        act(V("j3", 0, K // 2), V("yy", 0, K // 2), AF.Sign, bias=-5.0, acc=col("acc", 48))
        act(V("j3", K // 2, K), V("yy", 1, K // 2 + 1), AF.Sign, bias=-3.0, acc=col("acc", 49))
        ts(W(24, 6), KC, col("acc", 48), A.subtract, col("acc", 49), A.is_lt)
        tt(W(25, 6), W(24, 6), D2, A.mult)
        lin(W(26, 6), W(25, 6), 1.0, NS - 2.0)
        tt(W(27, 6), W(24, 6), KH, A.add)
        for m in range(IVV, 6):
            act(V("j3", NS * m, NS * m + NS), V("cum", 15, 15 + NS), AF.Sign, bias=col("w", 16 * 27 + m), scale=-1.0, acc=col("acc", 52 + m))
            ts(col("of", 84 + m), col("acc", 52 + m), col("w", 16 * 26 + m), A.subtract, -0.5, A.mult)
        for m in range(IVV):
            n = 16 * m + 112
            ts(V("tf", NS * m, NS * m + n), V("cum", 15, 15 + n), col("w", 16 * 27 + m), A.is_ge, 2.0, A.mult)
            scan(V("iv", K * m + K - n // 2, K * m + K), V("tf", NS * m, NS * m + n // 2), V("tf", NS * m + n // 2, NS * m + n), col("w", 16 * 26 + m), A.add, A.add)
        ts(V("of", 84, 84 + IVV), V("iv", K - 1, IVV * K, K), -float(NS), A.add, 0.5, A.mult)
        for b in range(4):
            if b < FS:
                act(V("ft", b, 4 * K, 4), IX(V("tq", TQ * b, TQ * b + TW), O_F), AF.Copy, scale=0.5)
            else:
                ts(V("ft", b, 4 * K, 4), IX(V("tq", TQ * b, TQ * b + TW), O_F), 0.5, A.mult)
        qf, sf, ql, sl = ["%s%d" % (n, t) for n in ("qf", "sf", "ql", "sl")]
        quant(V(qf, 0, 128), V(sf, 0, 128), V("ft", 0, 512))
        dst = T.cores[rank ^ (1 << t)]
        rid, pid = topo.addr(dst)[:2]
        mask = topo.mask(core, dst)
        ne = len(topo.engines(core, dst))
        arr = T.sem["ar%d" % t]
        op("g", lambda qf=qf, ql=ql, arr=arr, pid=pid, rid=rid, mask=mask: g.remote_dma(
            T[ql][:, 0:K].bitcast(u8), T[qf][:, 0:K].bitcast(u8), arr, T.sem.sent, pid, rid, mask), [], [V(qf, 0, K)], 500, dma=("", 0), lat=3000)
        op("g", lambda sf=sf, sl=sl, arr=arr, pid=pid, rid=rid, mask=mask: g.remote_dma(
            T[sl][:, 0:K], T[sf][:, 0:K], arr, T.sem.sent, pid, rid, mask), [], [V(sf, 0, K)], 500, dma=("", 0), lat=3000)
        first.append((len(ops) - 2, len(ops) - 1))
        op("arrive", None, [V(ql, 0, K), V(sl, 0, K)], [V(qf, 0, K)], 0, dma=("ar%d" % t, 2 * ne), lat=3500)

        for m in range(M):
            n = 16 * m + 15
            b0 = 208 * m if m < 6 else 208 * (11 - m) + 16 * (12 - m)
            scan(V("lp", b0 + 1, b0 + 1 + n), V("sg", NS * m, NS * m + n), V("irow", 0, n), 1.0, A.min, A.max)
        for h in range(2):
            tt(V("lb", K * h, K * h + K), IX(V("lp", 0, 6 * 208), V("co", 32 + 6 * h, 38 + 6 * h)), V("oh", 0, K), A.mult)
        scan(V("lc", 0, NS), V("keepb", 0, NS), V("lb", 0, NS), 0.0, A.mult, A.add)
        tt(W(28), CW, A1, A.subtract)
        tt(W(29), W(28), UC, A.max)
        tt(W(30), W(29), ends("lc", 0), A.min)
        tt(W(31), RK, UC1, A.max)
        tt(W(32), W(31), W(30), A.min)
        ts(O_L, W(32), -256.0, A.mult, 271.0, A.add)
        CUM = V("cum", 0, 16 + NS)
        fill(V("nc", 0, QW + 16), 0)
        act(V("cpv", 0, NS), V("cum", 15, 15 + NS), AF.Copy)
        tt(V("an", 0, NS), IX(CUM, O_L), V("cpv", 0, NS), A.not_equal)
        cp(IX(V("nc", 16, QW + 16), O_QV), V("an", 0, NS))
        tt(V("r0", 0, NS), IX(CUM, O_L), V("an", 0, NS), A.mult)
        scan(V("r4", 0, NS), V("nc", 15, NS + 15), V("r0", 0, NS), 0.0, A.add, A.min)
        scan(RV("r5", 0, NS), RV("nc", 16, NS + 16), RV("r4", 0, NS), 0.0, A.add, A.min)
        tt(V("hb", 1, C, 2), IX(V("r5", 0, NS + 16), O_CO), V("mj", 1, C, 2), A.max)
        tt(V("hb", 2, C + 2, 2), IX(V("r5", 0, NS + 16), O_CE), V("mj", 2, C + 2, 2), A.max)
        scan(V("hc", 0, C), V("keepb", 0, C), V("hb", 0, C), 0.0, A.mult, A.add)
        ts(O_H, ends("hc", 0, 2 * M), -256.0, A.mult, -1.0, A.add)
        if t == R - 1:
            act(V("et", 0, NS), IX(IO(0, C + 8), O_PK), AF.Identity, bias=-1.0)
            act(V("er", 0, K), IX(V("et", 0, TW), O_F), AF.Copy)

        XN = "x%d" % (t + 1)
        for b in range(4):
            mm(PS(b, 0, 128), V("qw", 128 * b, 128 * b + 128), V("sw", 128 * b, 128 * b + 128), V(ql, 0, 128), V(sl, 0, 128))
            if b < HTV:
                ts(V("ht", K * b, K * b + K), PS(b, 0, K), 0.0, A.max, 0.03125, A.mult)
            else:
                act(V("ht", K * b, K * b + K), PS(b, 0, K), AF.Relu, scale=0.03125)
        for h, (lo, hi) in enumerate(PIECES[t + 1]):
            o_h = V("of", 152 + lo // 16, 152 + hi // 16)
            for b in range(4):
                if b < 4 - HS[h]:
                    tt(V(XN, 4 * lo + b, 4 * hi, 4), IX(V("ht", K * b, K * b + K), o_h), TB(b, lo, hi), A.add)
                else:
                    act(V("hg", C * b + lo, C * b + hi), IX(V("ht", K * b, K * b + K), o_h), AF.Copy)
                    tt(V(XN, 4 * lo + b, 4 * hi, 4), V("hg", C * b + lo, C * b + hi), PS(4 + b, lo, hi), A.add)

    act(V("olr", 0, C), IX(V("er", 0, K), O_H), AF.Copy)
    for k in range(8):
        dma("y", "out", T.ol[k:k + 1, :], T.olr[16 * k:16 * k + 1, :], [], [V("olr", 0, C)])
    QX, SX = V("qx%d" % R, 0, C), V("sx%d" % R, 0, C)
    for h, (lo, hi) in enumerate(PIECES[R]):
        quant(V(QX[1], lo, hi), V(SX[1], lo, hi), V("x%d" % R, 4 * lo, 4 * hi))
        mm(PS(h, 0, hi - lo), V("qv", 0, 128), V("sv", 0, 128), V(QX[1], lo, hi), V(SX[1], lo, hi))
        dma("y", "out", T.oc[:, 4 * lo:4 * hi], V(QX[1], lo, hi)[0].bitcast(u8), [], [V(QX[1], lo, hi)])
        act(V("ysb", lo, hi), PS(h, 0, hi - lo), AF.Copy)
        dma("s", "out", T.y[:, lo:hi], T.ysb[:, lo:hi], [], [V("ysb", lo, hi)])
    for k in range(4):
        dma("y", "out", T.osc[4 * k:4 * k + 4, :], T[SX[1]][32 * k:32 * k + 4, :], [], [SX])

    def meet(a, b):
        return a[1] < b[2] and b[1] < a[2] and (a[1] - b[1]) % math.gcd(a[3], b[3]) == 0

    deps, touch = [], {}
    for i, (q, fn, ws, rs, d, ns, lat) in enumerate(ops):
        ds = set()
        for a, wr in [(a, True) for a in ws] + [(a, False) for a in rs]:
            for j, b, wr2 in touch.get(a[0], []):
                if (a[0][:2] == "ps" and (ops[j][0] != q or wr or wr2)) or ((wr or wr2) and meet(a, b)):
                    ds.add(j)
        deps.append(ds)
        for a, wr in [(a, True) for a in ws] + [(a, False) for a in rs]:
            touch.setdefault(a[0], []).append((i, a, wr))
    n = len(ops)
    above = []
    for i in range(n):
        far = set()
        for j in deps[i]:
            far |= above[j]
        above.append(set() if ops[i][0] == "arrive" else far | deps[i])
        deps[i] = sorted(deps[i] - far)
    users = [[] for i in range(n)]
    for i in range(n):
        for j in deps[i]:
            users[j].append(i)

    def schedule(before, after, prio, back, wake, slack):
        left = [len(ds) for ds in before]
        ready = [i for i in range(n) if not left[i]]
        can, free, order, end = [(ops[i][6] if back else 0.0) for i in range(n)], {}, [], [0.0] * n
        while ready:
            soon, q = min((max(can[i], free.get(ops[i][0], 0.0)), ops[i][0]) for i in ready)
            i = -max((prio[i], -i) for i in ready if ops[i][0] == q and can[i] <= soon + slack)[1]
            end[i] = free[q] = max(can[i], free.get(q, 0.0)) + ops[i][5]
            ready.remove(i)
            order.append(i)
            for u in after[i]:
                can[u] = max(can[u], end[i] + ops[u if back else i][6] + wake)
                left[u] -= 1
                if not left[u]:
                    ready.append(u)
        return order, end

    queue = ["vstgya".index(o[0][0]) for o in ops]
    timing = [([f * (o[5] + jump * x) for o, x in zip(ops, slow)], [wake + (far if o[0] == "arrive" else o[6]) for o in ops]) for f, wake, far, jump in CASES]

    def span_of(order):
        s = 0.0
        for busy, lag in timing:
            free, end = [0.0] * 6, [0.0] * n
            for i in order:
                q = queue[i]
                t0 = free[q]
                for j in deps[i]:
                    if end[j] > t0:
                        t0 = end[j]
                t0 += busy[i]
                free[q] = t0
                end[i] = t0 + lag[i]
            s += max(end)
        return s

    def chain(order, case):
        busy, lag = case
        free, end, prev = [(0.0, -1, True)] * 6, [0.0] * n, [None] * n
        for i in order:
            t0, j, near = max([free[queue[i]]] + [(end[j], j, False) for j in deps[i]])
            free[queue[i]] = (t0 + busy[i], i, True)
            end[i], prev[i] = t0 + busy[i] + lag[i], (j, near)
        i, pairs = max(range(n), key=lambda i: end[i]), []
        while prev[i][0] >= 0:
            if prev[i][1]:
                pairs.append((prev[i][0], i))
            i = prev[i][0]
        return pairs

    if not ORDER:
        seed = [12345]

        def uni():
            seed[0] = (seed[0] * 1103515245 + 12345) % 2147483648
            return seed[0] / 2147483648.0

        prio, rank_in = [float(i) for i in range(n)], [0] * n
        for k in range(TURNS):
            wake, slack = 150 + 200 * uni(), 200 * uni() ** 2
            if ORDER and (k > 40 or k % 4):
                wake, slack = ORDER[3:] if k % 8 else (wake, slack)
                a, w = n * uni(), 10 + 80 * uni()
                back = [x + (NOISE * (1 + k % 5) * (uni() - 0.5) if abs(p - a) < w else 0.0) for x, p in zip(ORDER[2], rank_in)]
            else:
                back = schedule(users, deps, prio, True, wake, slack)[1]
            order, prio = schedule(deps, users, back, False, wake, slack)
            span = span_of(order)
            if not ORDER or span <= ORDER[0]:
                ORDER[:] = [span, order, back, wake, slack]
                for p, i in enumerate(order):
                    rank_in[i] = p
        span, order = ORDER[:2]
        best = (span, order)
        for k in range(MOVES):
            pairs = chain(order, timing[k % len(CASES)])
            j, i = pairs[int(uni() * len(pairs))]
            at = {x: p for p, x in enumerate(order)}
            new = list(order)
            if uni() < 0.5:
                lo = max([at[x] for x in deps[i]] + [-1]) + 1
                if lo > at[j]:
                    continue
                new.remove(i)
                new.insert(at[j] - int((at[j] - lo) * uni() ** 4), i)
            else:
                hi = min([at[x] for x in users[j]] + [n])
                if hi <= at[i]:
                    continue
                new.insert(at[i] + 1 + int((hi - at[i] - 1) * uni() ** 2), j)
                del new[at[j]]
            s = span_of(new)
            if s <= span + HEAT * (1 - k / MOVES) * uni() ** 2:
                span, order = s, new
                if s < best[0]:
                    best = (s, new)
        ORDER[:2] = best
    order = list(ORDER[1])
    for i, j in first:
        a, b = order.index(i), order.index(j)
        order[min(a, b)], order[max(a, b)] = i, j
    place = {i: k for k, i in enumerate(order)}
    waits = {}
    for i in order:
        last = {}
        for j in sorted(deps[i], key=lambda j: place[j]):
            last[ops[j][4][0] if ops[j][4] else ops[j][0]] = j
        waits[i] = [] if ops[i][0] == "arrive" else list(last.values())
    total = {}
    for o in ops:
        if o[4] and o[4][0]:
            total[o[4][0]] = total.get(o[4][0], 0) + o[4][1]
    needed, seen = set(), {}
    for i in order:
        for j in waits[i]:
            if not ops[j][4] and seen.get((ops[i][0], ops[j][0]), -1) < place[j]:
                needed.add(j)
                seen[(ops[i][0], ops[j][0])] = place[j]
    token, count, seen, mark = {}, {}, {}, {}
    for i in order:
        q, fn, ws, rs, d, ns, lat = ops[i]
        if q == "arrive":
            continue
        for j in waits[i]:
            if ops[j][4]:
                s, c = ops[j][4][0], total[ops[j][4][0]]
            elif mark.get((q, ops[j][0]), -1) < place[j]:
                s, c = token[j]
                mark[(q, ops[j][0])] = place[j]
            else:
                continue
            if seen.get((q, s), 0) < c:
                Q[q].wait_ge(T.sem[s], c)
                seen[(q, s)] = c
        ins = fn()
        if d:
            if d[0]:
                ins.then_inc(T.sem[d[0]], d[1])
        elif i in needed:
            s = COUNTER[q]
            count[s] = count.get(s, 0) + 1
            ins.then_inc(T.sem[s], 1)
            token[i] = (s, count[s])
    g.sync.wait_ge(T.sem.out, total["out"])
    g.wait_ge(T.sem.sent, 2 * R * ne)
